import numpy as np
import ml_dtypes


def mxq(x, axis, fmt="e4m3"):
    dtype, down = {"e4m3": (ml_dtypes.float8_e4m3fn, 7), "e5m2": (ml_dtypes.float8_e5m2, 14)}[fmt]
    v = np.moveaxis(np.asarray(x, np.float32).astype(ml_dtypes.bfloat16).astype(np.float64), axis, -1)
    blocks = v.reshape(v.shape[:-1] + (-1, 32))
    amax = np.abs(blocks).max(-1, keepdims=True)
    byte = np.maximum(np.where(amax > 0, np.frexp(amax)[1] - 1 + 127, 0) - down, 1)
    scale = np.exp2(byte - 127.0)
    codes = (blocks / scale).astype(np.float32).astype(dtype).astype(np.float64)
    return np.moveaxis((codes * scale).reshape(v.shape), -1, axis)


WIDE = False


def mx_kscale(k):
    if not WIDE:
        return np.ones(k)
    levels = np.array([24, -24, 12, -12, 0])
    if k % 512:
        return np.exp2(np.random.permutation(np.resize(levels, k // 32))).repeat(32)
    a = np.empty((k // 512, 16))
    for p in range(k // 512):
        a[p, :8] = np.random.permutation(np.resize(levels, 8))
        for g in range(8):
            far = levels[np.abs(levels - a[p, g]) >= 10]
            a[p, g + 8] = far[np.random.randint(len(far))]
    return np.exp2(a.ravel()).repeat(32)


def f64(x):
    return np.asarray(x).astype(np.float64)


def striped8(idx):
    return np.concatenate([v.reshape(-1, 16).T for v in idx]).astype(np.uint16)


def unstriped8(offs):
    return np.stack([offs[16 * g:16 * g + 16].T.reshape(-1) for g in range(8)]).astype(np.int64)


E2M1 = np.array([0.0, 0.5, 1.0, 1.5, 2.0, 3.0, 4.0, 6.0, -0.0, -0.5, -1.0, -1.5, -2.0, -3.0, -4.0, -6.0])


def pack_weight(w, fmt):
    k, n = w.shape
    w = f64(np.asarray(w, np.float32).astype(ml_dtypes.bfloat16)).reshape(k // 32, 32, n)
    amax = np.abs(w).max(1)
    if fmt == "e4m3":
        byte = np.frexp(amax)[1] - 1 + 127 - 7
    else:
        mant, ex = np.frexp(amax / 6.0)
        byte = np.where(mant > 0.5, ex, ex - 1) + 127
    byte = np.clip(np.where(amax > 0, byte, 1), 1, 254)
    scaled = (w * np.exp2(127.0 - byte)[:, None, :]).reshape(k, n).astype(np.float32)
    by_word = np.ascontiguousarray(scaled.reshape(k // 512, 128, 4, n).transpose(0, 1, 3, 2))
    if fmt == "e4m3":
        words = by_word.astype(ml_dtypes.float8_e4m3fn).view(np.uint8)
    else:
        c = by_word.astype(ml_dtypes.float4_e2m1fn).view(np.uint8) & 0xF
        words = (c[..., 0::2] | (c[..., 1::2] << 4)).reshape(k // 512, 128, 2 * n)
    return np.ascontiguousarray(words), np.ascontiguousarray(byte.astype(np.uint8).reshape(k // 512, 16, n))


def unpack_weight(words, scales, fmt):
    g, _, n = scales.shape
    words = np.ascontiguousarray(words).reshape(g, 128, n, -1)
    if fmt == "e4m3":
        vals = words.view(ml_dtypes.float8_e4m3fn).astype(np.float64)
    else:
        nib = np.empty((g, 128, n, 4), np.uint8)
        nib[..., 0::2] = words & 0xF
        nib[..., 1::2] = words >> 4
        vals = E2M1[nib]
    vals = vals * np.repeat(np.exp2(scales.astype(np.float64) - 127.0), 8, axis=1)[..., None]
    return vals.transpose(0, 1, 3, 2).reshape(g * 512, n)


def planes(y):
    n, m = y.shape
    v = y.astype(np.float32).astype(ml_dtypes.bfloat16).astype(np.float64).reshape(n // 32, 32, m)
    top = np.abs(v).max(1)
    byte = np.clip(np.where(top > 0, np.frexp(top)[1] - 1 + 127 - 7, 1), 1, 254)
    codes = (v * np.exp2(127.0 - byte)[:, None, :]).reshape(n, m).astype(np.float32).astype(ml_dtypes.float8_e4m3fn).view(np.uint8)
    words = codes.reshape(n // 512, 128, 4, m).transpose(0, 1, 3, 2)
    return np.ascontiguousarray(words), np.ascontiguousarray(byte.astype(np.uint8).reshape(n // 512, 16, m))


K, R, N, T, J = 1024, 1024, 512, 2048, 1024


def setup_inputs():
    n = np.random.standard_normal
    s = mx_kscale(K)[:, None]
    u = mx_kscale(R)[:, None]
    p_wg = pack_weight(n((K, R)) / np.sqrt(K) / s, "e2m1")
    p_wu = pack_weight(n((K, R)) / np.sqrt(K) / s * u.T, "e4m3")
    p_wd = pack_weight(n((R, N)) / np.sqrt(R) / u, "e4m3")
    return {
        "xT": (n((K, T)) * s).astype(np.float32),
        "wgt": np.repeat(np.random.uniform(0.5, 2.0, (8, J)), 16, axis=0).astype(np.float32),
        "wg_words": p_wg[0],
        "wg_scales": p_wg[1],
        "wu_words": p_wu[0],
        "wu_scales": p_wu[1],
        "wd_words": p_wd[0],
        "wd_scales": p_wd[1],
        "b": (0.3 * n(N)).astype(np.float32),
        "offs": striped8(np.stack([np.random.permutation(T)[:J] for _ in range(8)])),
    }


def reference(xT, wgt, wg_words, wg_scales, wu_words, wu_scales, wd_words, wd_scales, b, offs):
    idx = unstriped8(offs)
    rows = np.arange(K)
    xg = f64(wgt)[rows // 4 % 128] * f64(xT)[rows[:, None], idx[rows % 512 // 64]]
    xT_ = mxq(xg, 0, "e4m3")
    wg_ = unpack_weight(wg_words, wg_scales, "e2m1")
    wu_ = unpack_weight(wu_words, wu_scales, "e4m3")
    ga = wg_.T @ xT_
    ub = wu_.T @ xT_
    h = np.maximum(ga, 0.0) * ub
    h_ = mxq(h, 0, "e4m3")
    wd_ = unpack_weight(wd_words, wd_scales, "e4m3")
    y = wd_.T @ h_
    out_0 = y + f64(b)[:, None]
    return (out_0,) + planes(out_0)

@@ -1,0 +1,301 @@
+from contextlib import ExitStack
+
+import concourse.mybir as mybir
+from concourse.masks import make_identity
+
+K, R, N, T, J = 1024, 1024, 512, 2048, 1024
+FLOPS = 2 * J * (2 * K * R + R * N)
+
+F32 = mybir.dt.float32
+BF16 = mybir.dt.bfloat16
+I32 = mybir.dt.int32
+U8 = mybir.dt.uint8
+U16 = mybir.dt.uint16
+FP8X4 = mybir.dt.float8_e4m3fn_x4
+FP4X4 = mybir.dt.float4_e2m1fn_x4
+MULT = mybir.AluOpType.mult
+ACT = mybir.ActivationFunctionType
+
+P = 128
+PACK = 4
+PASSES = 2
+HALF = 512
+EARLY = 896
+PAIR = 256
+HEAD = 256
+
+
+def tile_list_relu_biasP_kernel(
+    tc, xT, wgt, wg_words, wg_scales, wu_words, wu_scales, wd_words, wd_scales, b, offs, out_0, out_1, out_2
+):
+    nc = tc.nc
+    with ExitStack() as ctx:
+        keep = ctx.enter_context(tc.tile_pool(name="keep", bufs=1))
+        ring = ctx.enter_context(tc.tile_pool(name="ring", bufs=3))
+        gates = ctx.enter_context(tc.tile_pool(name="gates", bufs=6))
+        psum = ctx.enter_context(tc.psum_pool(name="psum", bufs=2))
+        psum_mm = ctx.enter_context(tc.psum_pool(name="psum_mm", bufs=6))
+
+        offsets = keep.tile([P, J // 16], U16, name="offsets")
+        nc.sync.dma_start(offsets[:], offs)
+
+        x_rows = xT.rearrange("(a p t) n -> a t p n", a=PASSES, t=PACK)
+        x_plane = {}
+        for a in range(PASSES):
+            for t in range(PACK):
+                x_plane[a, t] = keep.tile([P, T], F32, name="x_%d_%d" % (a, t))
+        wgt_all = keep.tile([P, J], F32, name="wgt_all")
+        wg_w = [keep.tile([P, 2 * R], U8, name="wg_%d" % a, align_bytes=64) for a in range(PASSES)]
+        wu_w = [keep.tile([P, PASSES, HALF], I32, name="wu_%d" % hf, align_bytes=64) for hf in range(2)]
+        wd_raw = keep.tile([P, PASSES, N], I32, name="wd_raw", align_bytes=64)
+
+        nc.sync.dma_start(x_plane[0, 0][:], x_rows[0, 0])
+        nc.sync.dma_start(wgt_all[:, 0:HEAD], wgt[:, 0:HEAD])
+        nc.sync.dma_start(wgt_all[:, HEAD:J], wgt[:, HEAD:J])
+        for a in range(PASSES):
+            for t in range(PACK):
+                if (a, t) == (1, 3):
+                    nc.sync.dma_start(wg_w[0][:].bitcast(I32), wg_words[0].bitcast(I32))
+                if (a, t) != (0, 0):
+                    nc.sync.dma_start(x_plane[a, t][:], x_rows[a, t])
+        nc.sync.dma_start(wg_w[1][:].bitcast(I32), wg_words[1].bitcast(I32))
+        for hf in range(2):
+            nc.sync.dma_start(
+                wu_w[hf][:],
+                wu_words[:, :, HALF * hf : HALF * (hf + 1), :].rearrange("a p r i -> p a (r i)").bitcast(I32),
+            )
+
+        wg_sc = keep.tile([P, PASSES, R], U8, name="wg_sc", align_bytes=64)
+        wud_sc = keep.tile([P, R], U8, name="wud_sc", align_bytes=64)
+        nc.vector.memset(wg_sc[:].rearrange("p a r -> p (a r)").bitcast(I32), 0)
+        nc.vector.memset(wud_sc[:].bitcast(I32), 0)
+        ident = keep.tile([P, P], F32, name="ident")
+        make_identity(nc, ident[:])
+        for q in range(4):
+            nc.gpsimd.dma_start(
+                wg_sc[32 * q : 32 * q + 4, :, :].bitcast(I32),
+                wg_scales[:, 4 * q : 4 * q + 4, :].rearrange("a q r -> q a r").bitcast(I32),
+            )
+        for q in range(4):
+            nc.gpsimd.dma_start(
+                wud_sc[32 * q : 32 * q + 8, :].bitcast(I32),
+                wu_scales[:, 4 * q : 4 * q + 4, :].bitcast(I32),
+            )
+
+        nc.sync.dma_start(wd_raw[:], wd_words.rearrange("a p n i -> p a (n i)").bitcast(I32))
+        wd_sc_raw = keep.tile([P, N], U8, name="wd_sc_raw", align_bytes=64)
+        nc.vector.memset(wd_sc_raw[:].bitcast(I32), 0)
+        for q in range(4):
+            nc.sync.dma_start(
+                wd_sc_raw[32 * q + 8 : 32 * q + 16, :].bitcast(I32),
+                wd_scales[:, 4 * q : 4 * q + 4, :].bitcast(I32),
+            )
+
+        bias = keep.tile([P, PACK], F32, name="bias")
+        nc.sync.dma_start(bias[:], b.rearrange("(p t) -> p t", t=PACK))
+
+        picked = {(0, 0): keep.tile([P, PACK, J], F32, name="picked_0"), (1, 0): keep.tile([P, PACK, EARLY], F32, name="picked_1")}
+        xq = [keep.tile([P, J], I32, name="xq_%d" % a, align_bytes=64) for a in range(PASSES)]
+        xs = [keep.tile([P, J], U8, name="xs_%d" % a, align_bytes=64) for a in range(PASSES)]
+
+        def picked_cols(a, c0, c1):
+            base = EARLY if (a == 1 and c0 >= EARLY) else 0
+            return picked[a, base][:, :, c0 - base : c1 - base]
+
+        def gather(a, t, c0, c1):
+            nc.vector.tensor_tensor(
+                picked_cols(a, c0, c1)[:, t, :],
+                x_plane[a, t][:].indirect(offsets[:, c0 // 16 : c1 // 16]),
+                wgt_all[:, c0:c1],
+                MULT,
+            )
+
+        x_woven = {}
+
+        def weave_x(a, c0, c1):
+            tag = "handed_on" if (a, c0) == (1, 0) else "xw_%d_%d" % (a, c0)
+            woven = keep.tile([P, c1 - c0, PACK], BF16, name="xw_%d_%d" % (a, c0), tag=tag, align_bytes=64)
+            nc.scalar.activation(
+                woven[:].rearrange("p (c i) t -> p c t i", i=4),
+                picked_cols(a, c0, c1).rearrange("p t (c i) -> p c t i", i=4),
+                ACT.Copy,
+            )
+            x_woven[a, c0] = woven
+
+        def quant_x(a, c0, c1):
+            nc.vector.quantize_mx(
+                out=xq[a][:, c0:c1].bitcast(FP8X4),
+                scales=xs[a][:, c0:c1],
+                in_=x_woven[a, c0][:].rearrange("p j t -> p (j t)"),
+            )
+
+        h_rows = {}
+
+        def unit(jt, hf):
+            cols = slice(P * jt, P * (jt + 1))
+            rcols = slice(HALF * hf, HALF * (hf + 1))
+            ga = psum_mm.tile([P, HALF], F32, name="ga", tag="sum")
+            for a in range(PASSES):
+                nc.tensor.matmul_mx(
+                    out=ga[:],
+                    lhsT=xq[a][:, cols].bitcast(FP8X4),
+                    lhsT_scale=xs[a][:, cols],
+                    rhs=wg_w[a][:, 2 * HALF * hf : 2 * HALF * (hf + 1)].bitcast(FP4X4),
+                    rhs_scale=wg_sc[:, a, rcols],
+                    start=(a == 0),
+                    stop=(a == PASSES - 1),
+                )
+            ub = psum_mm.tile([P, HALF], F32, name="ub", tag="sum")
+            for a in range(PASSES):
+                nc.tensor.matmul_mx(
+                    out=ub[:],
+                    lhsT=xq[a][:, cols].bitcast(FP8X4),
+                    lhsT_scale=xs[a][:, cols],
+                    rhs=wu_w[hf][:, a, :].bitcast(FP8X4),
+                    rhs_scale=wud_sc[4 * a : P, rcols],
+                    start=(a == 0),
+                    stop=(a == PASSES - 1),
+                )
+            gate = gates.tile([P, 2, P, 2], F32, name="gate")
+            nc.scalar.activation(gate[:], ga[:].rearrange("p (m u e) -> p u m e", u=2, e=2), ACT.Relu)
+            h = keep.tile([P, 2, P, 2], BF16, name="h_%d_%d" % (jt, hf), align_bytes=64)
+            nc.vector.tensor_tensor(h[:], ub[:].rearrange("p (m u e) -> p u m e", u=2, e=2), gate[:], MULT)
+            h_rows[jt, hf] = h
+
+        hq = [keep.tile([P, J], I32, name="hq_%d" % a, align_bytes=64) for a in range(PASSES)]
+        hs = [keep.tile([P, J], U8, name="hs_%d" % a, align_bytes=64) for a in range(PASSES)]
+
+        def turn(jt0, tiles, a):
+            width = P * tiles
+            turned = psum.tile([P, 2, width], F32, name="turned", tag="misc")
+            for k in range(tiles):
+                words = h_rows[jt0 + k, a][:].rearrange("p u m e -> p (u m e)").bitcast(F32)
+                for u in range(2):
+                    nc.tensor.transpose(turned[:, u, P * k : P * (k + 1)], words[:, P * u : P * (u + 1)], ident[:])
+            woven = ring.tile([P, width, PACK], BF16, name="hw", align_bytes=64)
+            flat = woven[:].rearrange("p j t -> p (j t)")
+            nc.scalar.copy(flat.bitcast(F32).rearrange("p (j u) -> p j u", u=2), turned[:].rearrange("p u j -> p j u"))
+            cols = slice(P * jt0, P * jt0 + width)
+            nc.vector.quantize_mx(out=hq[a][:, cols].bitcast(FP8X4), scales=hs[a][:, cols], in_=flat)
+
+        wd_w = keep.tile([P, PASSES, PACK, P], I32, name="wd_w", align_bytes=64)
+        wd_sc = keep.tile([P, PACK, P], U8, name="wd_sc", align_bytes=64)
+
+        def deal_wd():
+            nc.vector.tensor_copy(wd_sc[:], wd_sc_raw[:].rearrange("p (m t) -> p t m", t=PACK))
+            nc.vector.tensor_copy(wd_w[:], wd_raw[:].rearrange("p a (m t) -> p a t m", t=PACK))
+
+        out_rows = out_0.rearrange("(p t) j -> p t j", t=PACK)
+        out_words = out_1[0].rearrange("p j i -> p (j i)").bitcast(I32)
+        y_sc = keep.tile([P, J], U8, name="y_sc", align_bytes=64)
+
+        def down_pass(out, t, a, cols):
+            nc.tensor.matmul_mx(
+                out=out,
+                lhsT=wd_w[:, a, t, :].bitcast(FP8X4),
+                lhsT_scale=wd_sc[8 + 4 * a : P, t, :],
+                rhs=hq[a][:, cols].bitcast(FP8X4),
+                rhs_scale=hs[a][:, cols],
+                start=(a == 0),
+                stop=(a == PASSES - 1),
+            )
+
+        def hand_out(y, cols, width):
+            nc.sync.dma_start(out_rows[:, :, cols], y[:])
+            woven = ring.tile([P, width, PACK], BF16, name="yw", align_bytes=64)
+            nc.vector.tensor_copy(
+                woven[:].rearrange("p (c i) t -> p c t i", i=4), y[:].rearrange("p t (c i) -> p c t i", i=4)
+            )
+            yq = ring.tile([P, width], I32, name="yq", align_bytes=64)
+            nc.vector.quantize_mx(
+                out=yq[:].bitcast(FP8X4), scales=y_sc[:, cols], in_=woven[:].rearrange("p j t -> p (j t)")
+            )
+            nc.sync.dma_start(out_words[:, cols], yq[:])
+
+        def down(jt0, tiles):
+            width = P * tiles
+            per_bank = HALF // width
+            cols = slice(P * jt0, P * jt0 + width)
+            y = ring.tile([P, PACK, width], F32, name="y")
+            for t0 in range(0, PACK, per_bank):
+                acc = psum.tile([P, per_bank, width], F32, name="acc", tag="misc")
+                for e in range(per_bank):
+                    for a in range(PASSES):
+                        down_pass(acc[:, e, :], t0 + e, a, cols)
+                for e in range(per_bank):
+                    t = t0 + e
+                    nc.scalar.activation(y[:, t, :], acc[:, e, :], ACT.Identity, bias=bias[:, t : t + 1])
+            hand_out(y, cols, width)
+
+        def down_last(jt):
+            cols = slice(P * jt, P * (jt + 1))
+            y = ring.tile([P, PACK, P], F32, name="y")
+            accs = [psum_mm.tile([P, P], F32, name="acc_%d" % t, tag="sum") for t in range(PACK)]
+            for a in range(PASSES):
+                for t in range(PACK):
+                    down_pass(accs[t][:], t, a, cols)
+            for t in range(PACK):
+                if t % 2 == 0:
+                    nc.vector.tensor_scalar_add(y[:, t, :], accs[t][:], bias[:, t : t + 1])
+                else:
+                    nc.scalar.activation(y[:, t, :], accs[t][:], ACT.Identity, bias=bias[:, t : t + 1])
+            hand_out(y, cols, P)
+
+        gather(0, 0, 0, HEAD)
+        gather(0, 0, HEAD, J)
+        for t in range(1, PACK):
+            gather(0, t, 0, J)
+        chunks0 = [(0, 512), (512, J)]
+        gather(1, 0, 0, EARLY)
+        for c in chunks0:
+            weave_x(0, *c)
+        gather(1, 1, 0, EARLY)
+        for c in chunks0:
+            quant_x(0, *c)
+        gather(1, 2, 0, EARLY)
+        chunks1 = [(0, 128), (128, 256), (256, 512), (512, 768), (768, EARLY)]
+        for c in chunks1:
+            gather(1, 3, *c)
+            weave_x(1, *c)
+        for c in chunks1[0:2]:
+            quant_x(1, *c)
+        picked[1, EARLY] = keep.tile([P, PACK, J - EARLY], F32, name="picked_late", tag="handed_on", align_bytes=64)
+
+        unit(0, 0)
+        unit(1, 0)
+        quant_x(1, *chunks1[2])
+        unit(0, 1)
+        quant_x(1, *chunks1[3])
+        unit(1, 1)
+        quant_x(1, *chunks1[4])
+        deal_wd()
+        for pair in range(1, 3):
+            unit(2 * pair, 0)
+            turn(2 * pair - 2, 2, 0)
+            turn(2 * pair - 2, 2, 1)
+            unit(2 * pair + 1, 0)
+            if pair == 1:
+                for t in range(PACK):
+                    gather(1, t, EARLY, J)
+                weave_x(1, EARLY, J)
+            unit(2 * pair, 1)
+            down(2 * pair - 2, 2)
+            if pair == 1:
+                quant_x(1, EARLY, J)
+            unit(2 * pair + 1, 1)
+        unit(6, 0)
+        turn(4, 2, 0)
+        turn(4, 2, 1)
+        unit(6, 1)
+        unit(7, 0)
+        down(4, 2)
+        turn(6, 1, 0)
+        turn(6, 1, 1)
+        unit(7, 1)
+        turn(7, 1, 0)
+        turn(7, 1, 1)
+        down_last(7)
+        down(6, 1)
+        for q in range(4):
+            eng = nc.sync if q % 2 == 0 else nc.scalar
+            eng.dma_start(out_2[0, 4 * q : 4 * q + 4, :].bitcast(I32), y_sc[32 * q : 32 * q + 4, :].bitcast(I32))

@@ -20,7 +20,6 @@ P = 128
 PACK = 4
 PASSES = 2
 HALF = 512
-EARLY = 896
 PAIR = 256
 HEAD = 256
 
@@ -32,7 +31,7 @@ def tile_list_relu_biasP_kernel(
     with ExitStack() as ctx:
         keep = ctx.enter_context(tc.tile_pool(name="keep", bufs=1))
         ring = ctx.enter_context(tc.tile_pool(name="ring", bufs=3))
-        gates = ctx.enter_context(tc.tile_pool(name="gates", bufs=6))
+        gates = ctx.enter_context(tc.tile_pool(name="gates", bufs=8))
         psum = ctx.enter_context(tc.psum_pool(name="psum", bufs=2))
         psum_mm = ctx.enter_context(tc.psum_pool(name="psum_mm", bufs=6))
 
@@ -49,39 +48,46 @@ def tile_list_relu_biasP_kernel(
         wu_w = [keep.tile([P, PASSES, HALF], I32, name="wu_%d" % hf, align_bytes=64) for hf in range(2)]
         wd_raw = keep.tile([P, PASSES, N], I32, name="wd_raw", align_bytes=64)
 
-        nc.sync.dma_start(x_plane[0, 0][:], x_rows[0, 0])
+        wg_sc = keep.tile([P, PASSES, R], U8, name="wg_sc", align_bytes=64)
+        wu_sc = keep.tile([P, R], U8, name="wu_sc", align_bytes=64)
+        nc.vector.memset(wg_sc[:].rearrange("p a r -> p (a r)").bitcast(I32), 0)
+        nc.vector.memset(wu_sc[:].bitcast(I32), 0)
+        ident = keep.tile([P, P], F32, name="ident")
+        make_identity(nc, ident[:])
+
+        def load_x(a, t):
+            nc.sync.dma_start(x_plane[a, t][:], x_rows[a, t])
+
+        load_x(0, 0)
         nc.sync.dma_start(wgt_all[:, 0:HEAD], wgt[:, 0:HEAD])
         nc.sync.dma_start(wgt_all[:, HEAD:J], wgt[:, HEAD:J])
-        for a in range(PASSES):
-            for t in range(PACK):
-                if (a, t) == (1, 3):
-                    nc.sync.dma_start(wg_w[0][:].bitcast(I32), wg_words[0].bitcast(I32))
-                if (a, t) != (0, 0):
-                    nc.sync.dma_start(x_plane[a, t][:], x_rows[a, t])
-        nc.sync.dma_start(wg_w[1][:].bitcast(I32), wg_words[1].bitcast(I32))
-        for hf in range(2):
+        for t in range(1, PACK):
+            load_x(0, t)
+        load_x(1, 0)
+        load_x(1, 1)
+        for q in range(4):
+            nc.sync.dma_start(
+                wg_sc[32 * q : 32 * q + 4, :, :].bitcast(I32),
+                wg_scales[:, 4 * q : 4 * q + 4, :].rearrange("a q r -> q a r").bitcast(I32),
+            )
+        load_x(1, 2)
+        for q in range(4):
+            nc.sync.dma_start(
+                wu_sc[32 * q + 4 : 32 * q + 12, :].bitcast(I32),
+                wu_scales[:, 4 * q : 4 * q + 4, :].bitcast(I32),
+            )
+
+        def load_wu(hf):
             nc.sync.dma_start(
                 wu_w[hf][:],
                 wu_words[:, :, HALF * hf : HALF * (hf + 1), :].rearrange("a p r i -> p a (r i)").bitcast(I32),
             )
 
-        wg_sc = keep.tile([P, PASSES, R], U8, name="wg_sc", align_bytes=64)
-        wud_sc = keep.tile([P, R], U8, name="wud_sc", align_bytes=64)
-        nc.vector.memset(wg_sc[:].rearrange("p a r -> p (a r)").bitcast(I32), 0)
-        nc.vector.memset(wud_sc[:].bitcast(I32), 0)
-        ident = keep.tile([P, P], F32, name="ident")
-        make_identity(nc, ident[:])
-        for q in range(4):
-            nc.gpsimd.dma_start(
-                wg_sc[32 * q : 32 * q + 4, :, :].bitcast(I32),
-                wg_scales[:, 4 * q : 4 * q + 4, :].rearrange("a q r -> q a r").bitcast(I32),
-            )
-        for q in range(4):
-            nc.gpsimd.dma_start(
-                wud_sc[32 * q : 32 * q + 8, :].bitcast(I32),
-                wu_scales[:, 4 * q : 4 * q + 4, :].bitcast(I32),
-            )
-
+        nc.sync.dma_start(wg_w[1][:].bitcast(I32), wg_words[1].bitcast(I32))
+        nc.sync.dma_start(wg_w[0][:].bitcast(I32), wg_words[0].bitcast(I32))
+        load_x(1, 3)
+        load_wu(0)
+        load_wu(1)
         nc.sync.dma_start(wd_raw[:], wd_words.rearrange("a p n i -> p a (n i)").bitcast(I32))
         wd_sc_raw = keep.tile([P, N], U8, name="wd_sc_raw", align_bytes=64)
         nc.vector.memset(wd_sc_raw[:].bitcast(I32), 0)
@@ -94,72 +100,104 @@ def tile_list_relu_biasP_kernel(
         bias = keep.tile([P, PACK], F32, name="bias")
         nc.sync.dma_start(bias[:], b.rearrange("(p t) -> p t", t=PACK))
 
-        picked = {(0, 0): keep.tile([P, PACK, J], F32, name="picked_0"), (1, 0): keep.tile([P, PACK, EARLY], F32, name="picked_1")}
+        picked0 = keep.tile([P, PACK, J], F32, name="picked0")
+        picked1 = keep.tile([P, 2, J - P], F32, name="picked1")
+        woven0 = [keep.tile([P, PAIR, PACK], BF16, name="woven0_%d" % c, align_bytes=64) for c in range(4)]
+        woven1 = [keep.tile([P, P, PACK], BF16, name="woven1_%d" % jt, align_bytes=64) for jt in range(J // P)]
         xq = [keep.tile([P, J], I32, name="xq_%d" % a, align_bytes=64) for a in range(PASSES)]
         xs = [keep.tile([P, J], U8, name="xs_%d" % a, align_bytes=64) for a in range(PASSES)]
 
-        def picked_cols(a, c0, c1):
-            base = EARLY if (a == 1 and c0 >= EARLY) else 0
-            return picked[a, base][:, :, c0 - base : c1 - base]
-
-        def gather(a, t, c0, c1):
+        def gather(dst, a, t, c0, c1):
             nc.vector.tensor_tensor(
-                picked_cols(a, c0, c1)[:, t, :],
-                x_plane[a, t][:].indirect(offsets[:, c0 // 16 : c1 // 16]),
-                wgt_all[:, c0:c1],
-                MULT,
+                dst, x_plane[a, t][:].indirect(offsets[:, c0 // 16 : c1 // 16]), wgt_all[:, c0:c1], MULT
             )
 
-        x_woven = {}
+        def weave(dst, src):
+            dst = dst.rearrange("p (c i) t -> p c t i", i=4)
+            src = src.rearrange("p t (c i) -> p c t i", i=4)
+            nc.scalar.activation(dst, src, ACT.Copy)
 
-        def weave_x(a, c0, c1):
-            tag = "handed_on" if (a, c0) == (1, 0) else "xw_%d_%d" % (a, c0)
-            woven = keep.tile([P, c1 - c0, PACK], BF16, name="xw_%d_%d" % (a, c0), tag=tag, align_bytes=64)
-            nc.scalar.activation(
-                woven[:].rearrange("p (c i) t -> p c t i", i=4),
-                picked_cols(a, c0, c1).rearrange("p t (c i) -> p c t i", i=4),
-                ACT.Copy,
-            )
-            x_woven[a, c0] = woven
-
-        def quant_x(a, c0, c1):
+        def quant_x(a, src, c0, c1):
             nc.vector.quantize_mx(
-                out=xq[a][:, c0:c1].bitcast(FP8X4),
-                scales=xs[a][:, c0:c1],
-                in_=x_woven[a, c0][:].rearrange("p j t -> p (j t)"),
+                out=xq[a][:, c0:c1].bitcast(FP8X4), scales=xs[a][:, c0:c1], in_=src.rearrange("p j t -> p (j t)")
             )
+
+        rest = {}
+
+        def first_rest_plane(jt):
+            return 0 if jt == J // P - 1 else 2
+
+        def pick_rest(jt, t, tag=None):
+            first = first_rest_plane(jt)
+            if jt not in rest:
+                rest[jt] = keep.tile([P, PACK - first, P], F32, name="rest_%d" % jt, tag=tag, align_bytes=64)
+            gather(rest[jt][:, t - first, :], 1, t, P * jt, P * (jt + 1))
+
+        def finish(jt):
+            weave(woven1[jt][:, :, first_rest_plane(jt) : PACK], rest[jt][:])
+            quant_x(1, woven1[jt][:], P * jt, P * (jt + 1))
 
         h_rows = {}
 
-        def unit(jt, hf):
+        gate_sums = {}
+
+        def gate_pass(jt, hf, a):
             cols = slice(P * jt, P * (jt + 1))
-            rcols = slice(HALF * hf, HALF * (hf + 1))
-            ga = psum_mm.tile([P, HALF], F32, name="ga", tag="sum")
-            for a in range(PASSES):
-                nc.tensor.matmul_mx(
-                    out=ga[:],
-                    lhsT=xq[a][:, cols].bitcast(FP8X4),
-                    lhsT_scale=xs[a][:, cols],
-                    rhs=wg_w[a][:, 2 * HALF * hf : 2 * HALF * (hf + 1)].bitcast(FP4X4),
-                    rhs_scale=wg_sc[:, a, rcols],
-                    start=(a == 0),
-                    stop=(a == PASSES - 1),
-                )
-            ub = psum_mm.tile([P, HALF], F32, name="ub", tag="sum")
-            for a in range(PASSES):
-                nc.tensor.matmul_mx(
-                    out=ub[:],
-                    lhsT=xq[a][:, cols].bitcast(FP8X4),
-                    lhsT_scale=xs[a][:, cols],
-                    rhs=wu_w[hf][:, a, :].bitcast(FP8X4),
-                    rhs_scale=wud_sc[4 * a : P, rcols],
-                    start=(a == 0),
-                    stop=(a == PASSES - 1),
-                )
+            if a == 0 and (jt, hf) in [(2, 0), (3, 0)]:
+                gate_sums[jt, hf] = psum.tile([P, HALF], F32, name="ga", tag="misc")
+            elif a == 0:
+                gate_sums[jt, hf] = psum_mm.tile([P, HALF], F32, name="ga", tag="sum")
+            nc.tensor.matmul_mx(
+                out=gate_sums[jt, hf][:],
+                lhsT=xq[a][:, cols].bitcast(FP8X4),
+                lhsT_scale=xs[a][:, cols],
+                rhs=wg_w[a][:, 2 * HALF * hf : 2 * HALF * (hf + 1)].bitcast(FP4X4),
+                rhs_scale=wg_sc[:, a, HALF * hf : HALF * (hf + 1)],
+                start=(a == 0),
+                stop=(a == PASSES - 1),
+            )
+
+        gate_rows = {}
+
+        def gate_finish(jt, hf):
+            if (jt, hf) not in gate_sums:
+                gate_pass(jt, hf, 0)
+            gate_pass(jt, hf, 1)
             gate = gates.tile([P, 2, P, 2], F32, name="gate")
-            nc.scalar.activation(gate[:], ga[:].rearrange("p (m u e) -> p u m e", u=2, e=2), ACT.Relu)
-            h = keep.tile([P, 2, P, 2], BF16, name="h_%d_%d" % (jt, hf), align_bytes=64)
-            nc.vector.tensor_tensor(h[:], ub[:].rearrange("p (m u e) -> p u m e", u=2, e=2), gate[:], MULT)
+            nc.scalar.activation(gate[:], gate_sums[jt, hf][:].rearrange("p (m u e) -> p u m e", u=2, e=2), ACT.Relu)
+            gate_rows[jt, hf] = gate
+
+        up_sums = {}
+
+        def up_pass(jt, hf, a):
+            cols = slice(P * jt, P * (jt + 1))
+            if a == 0:
+                up_sums[jt, hf] = psum_mm.tile([P, HALF], F32, name="ub", tag="sum")
+            nc.tensor.matmul_mx(
+                out=up_sums[jt, hf][:],
+                lhsT=xq[a][:, cols].bitcast(FP8X4),
+                lhsT_scale=xs[a][:, cols],
+                rhs=wu_w[hf][:, a, :].bitcast(FP8X4),
+                rhs_scale=wu_sc[4 + 4 * a : P, HALF * hf : HALF * (hf + 1)],
+                start=(a == 0),
+                stop=(a == PASSES - 1),
+            )
+
+        def unit(jt, hf):
+            if (jt, hf) not in gate_rows:
+                gate_finish(jt, hf)
+            gate = gate_rows[jt, hf]
+            if (jt, hf) not in up_sums:
+                up_pass(jt, hf, 0)
+            up_pass(jt, hf, 1)
+            ub = up_sums[jt, hf]
+            h = keep.tile([P, 2, P, 2], BF16, name="h_%d_%d" % (jt, hf), tag="h_%d_%d" % (jt, hf), align_bytes=64)
+            sums = ub[:].rearrange("p (m u e) -> p u m e", u=2, e=2)
+            if (jt, hf) == (7, 1):
+                for u in range(2):
+                    nc.vector.tensor_tensor(h[:, u, :, :], sums[:, u, :, :], gate[:, u, :, :], MULT)
+            else:
+                nc.vector.tensor_tensor(h[:], sums, gate[:], MULT)
             h_rows[jt, hf] = h
 
         hq = [keep.tile([P, J], I32, name="hq_%d" % a, align_bytes=64) for a in range(PASSES)]
@@ -182,8 +220,9 @@ def tile_list_relu_biasP_kernel(
         wd_sc = keep.tile([P, PACK, P], U8, name="wd_sc", align_bytes=64)
 
         def deal_wd():
-            nc.vector.tensor_copy(wd_sc[:], wd_sc_raw[:].rearrange("p (m t) -> p t m", t=PACK))
-            nc.vector.tensor_copy(wd_w[:], wd_raw[:].rearrange("p a (m t) -> p a t m", t=PACK))
+            nc.gpsimd.tensor_copy(wd_sc[:], wd_sc_raw[:].rearrange("p (m t) -> p t m", t=PACK))
+            for a in range(PASSES):
+                nc.gpsimd.tensor_copy(wd_w[:, a, :, :], wd_raw[:, a, :].rearrange("p (m t) -> p t m", t=PACK))
 
         out_rows = out_0.rearrange("(p t) j -> p t j", t=PACK)
         out_words = out_1[0].rearrange("p j i -> p (j i)").bitcast(I32)
@@ -212,13 +251,13 @@ def tile_list_relu_biasP_kernel(
             )
             nc.sync.dma_start(out_words[:, cols], yq[:])
 
-        def down(jt0, tiles):
+        def down(jt0, tiles, pool=psum, tag="misc"):
             width = P * tiles
             per_bank = HALF // width
             cols = slice(P * jt0, P * jt0 + width)
             y = ring.tile([P, PACK, width], F32, name="y")
             for t0 in range(0, PACK, per_bank):
-                acc = psum.tile([P, per_bank, width], F32, name="acc", tag="misc")
+                acc = pool.tile([P, per_bank, width], F32, name="acc", tag=tag)
                 for e in range(per_bank):
                     for a in range(PASSES):
                         down_pass(acc[:, e, :], t0 + e, a, cols)
@@ -241,61 +280,74 @@ def tile_list_relu_biasP_kernel(
                     nc.scalar.activation(y[:, t, :], accs[t][:], ACT.Identity, bias=bias[:, t : t + 1])
             hand_out(y, cols, P)
 
-        gather(0, 0, 0, HEAD)
-        gather(0, 0, HEAD, J)
+        gather(picked0[:, 0, 0:HEAD], 0, 0, 0, HEAD)
+        gather(picked0[:, 0, HEAD:J], 0, 0, HEAD, J)
         for t in range(1, PACK):
-            gather(0, t, 0, J)
-        chunks0 = [(0, 512), (512, J)]
-        gather(1, 0, 0, EARLY)
-        for c in chunks0:
-            weave_x(0, *c)
-        gather(1, 1, 0, EARLY)
-        for c in chunks0:
-            quant_x(0, *c)
-        gather(1, 2, 0, EARLY)
-        chunks1 = [(0, 128), (128, 256), (256, 512), (512, 768), (768, EARLY)]
-        for c in chunks1:
-            gather(1, 3, *c)
-            weave_x(1, *c)
-        for c in chunks1[0:2]:
-            quant_x(1, *c)
-        picked[1, EARLY] = keep.tile([P, PACK, J - EARLY], F32, name="picked_late", tag="handed_on", align_bytes=64)
+            gather(picked0[:, t, :], 0, t, 0, J)
+        for c in range(4):
+            weave(woven0[c][:], picked0[:, :, PAIR * c : PAIR * (c + 1)])
+        gather(picked1[:, 0, :], 1, 0, 0, J - P)
+        for c in range(4):
+            quant_x(0, woven0[c][:], PAIR * c, PAIR * (c + 1))
+        for jt0, jt1 in [(0, 4), (4, 7)]:
+            gather(picked1[:, 1, P * jt0 : P * jt1], 1, 1, P * jt0, P * jt1)
+            for jt in range(jt0, jt1):
+                weave(woven1[jt][:, :, 0:2], picked1[:, :, P * jt : P * (jt + 1)])
+        for jt in range(4):
+            pick_rest(jt, 2, "rest_%d" % jt)
+        for jt, hf in [(0, 0), (0, 1), (1, 0), (1, 1), (2, 0), (3, 0), (2, 1), (3, 1)]:
+            gate_pass(jt, hf, 0)
 
+        for jt in range(4):
+            pick_rest(jt, 3)
+        for jt in range(4):
+            finish(jt)
+        for jt, hf in [(0, 0), (0, 1), (1, 0), (1, 1), (2, 0), (3, 0), (2, 1), (3, 1)]:
+            gate_finish(jt, hf)
         unit(0, 0)
         unit(1, 0)
-        quant_x(1, *chunks1[2])
         unit(0, 1)
-        quant_x(1, *chunks1[3])
         unit(1, 1)
-        quant_x(1, *chunks1[4])
+        unit(2, 0)
+        unit(3, 0)
         deal_wd()
-        for pair in range(1, 3):
-            unit(2 * pair, 0)
-            turn(2 * pair - 2, 2, 0)
-            turn(2 * pair - 2, 2, 1)
-            unit(2 * pair + 1, 0)
-            if pair == 1:
-                for t in range(PACK):
-                    gather(1, t, EARLY, J)
-                weave_x(1, EARLY, J)
-            unit(2 * pair, 1)
-            down(2 * pair - 2, 2)
-            if pair == 1:
-                quant_x(1, EARLY, J)
-            unit(2 * pair + 1, 1)
+        turn(0, 2, 0)
+        turn(0, 2, 1)
+        unit(2, 1)
+        for t in (2, 3):
+            pick_rest(4, t, "h_0_0")
+        finish(4)
+        unit(3, 1)
+        for t in (2, 3):
+            pick_rest(5, t, "h_1_0")
+        finish(5)
+        down(0, 2)
+        unit(4, 0)
+        turn(2, 2, 0)
+        turn(2, 2, 1)
+        unit(5, 0)
+        for t in (2, 3):
+            pick_rest(6, t, "h_2_0")
+        finish(6)
+        unit(4, 1)
+        down(2, 2)
+        for t in range(PACK):
+            pick_rest(7, t, "h_3_0")
+        finish(7)
+        unit(5, 1)
         unit(6, 0)
         turn(4, 2, 0)
         turn(4, 2, 1)
         unit(6, 1)
         unit(7, 0)
-        down(4, 2)
+        unit(7, 1)
         turn(6, 1, 0)
         turn(6, 1, 1)
-        unit(7, 1)
+        down(4, 2, psum_mm, "sum")
         turn(7, 1, 0)
         turn(7, 1, 1)
+        down(6, 1, psum_mm, "sum")
         down_last(7)
-        down(6, 1)
         for q in range(4):
             eng = nc.sync if q % 2 == 0 else nc.scalar
             eng.dma_start(out_2[0, 4 * q : 4 * q + 4, :].bitcast(I32), y_sc[32 * q : 32 * q + 4, :].bitcast(I32))

@@ -83,9 +83,9 @@ def tile_list_relu_biasP_kernel(
                 wu_words[:, :, HALF * hf : HALF * (hf + 1), :].rearrange("a p r i -> p a (r i)").bitcast(I32),
             )
 
-        nc.sync.dma_start(wg_w[1][:].bitcast(I32), wg_words[1].bitcast(I32))
         nc.sync.dma_start(wg_w[0][:].bitcast(I32), wg_words[0].bitcast(I32))
         load_x(1, 3)
+        nc.sync.dma_start(wg_w[1][:].bitcast(I32), wg_words[1].bitcast(I32))
         load_wu(0)
         load_wu(1)
         nc.sync.dma_start(wd_raw[:], wd_words.rearrange("a p n i -> p a (n i)").bitcast(I32))
@@ -101,9 +101,9 @@ def tile_list_relu_biasP_kernel(
         nc.sync.dma_start(bias[:], b.rearrange("(p t) -> p t", t=PACK))
 
         picked0 = keep.tile([P, PACK, J], F32, name="picked0")
-        picked1 = keep.tile([P, 2, J - P], F32, name="picked1")
+        picked1 = keep.tile([P, 2, J - 2 * P], F32, name="picked1")
         woven0 = [keep.tile([P, PAIR, PACK], BF16, name="woven0_%d" % c, align_bytes=64) for c in range(4)]
-        woven1 = [keep.tile([P, P, PACK], BF16, name="woven1_%d" % jt, align_bytes=64) for jt in range(J // P)]
+        woven1 = [keep.tile([P, P, PACK], BF16, name="woven1_%d" % jt, tag="woven1_%d" % jt, align_bytes=64) for jt in range(J // P)]
         xq = [keep.tile([P, J], I32, name="xq_%d" % a, align_bytes=64) for a in range(PASSES)]
         xs = [keep.tile([P, J], U8, name="xs_%d" % a, align_bytes=64) for a in range(PASSES)]
 
@@ -125,7 +125,7 @@ def tile_list_relu_biasP_kernel(
         rest = {}
 
         def first_rest_plane(jt):
-            return 0 if jt == J // P - 1 else 2
+            return 0 if jt >= J // P - 2 else 2
 
         def pick_rest(jt, t, tag=None):
             first = first_rest_plane(jt)
@@ -143,7 +143,7 @@ def tile_list_relu_biasP_kernel(
 
         def gate_pass(jt, hf, a):
             cols = slice(P * jt, P * (jt + 1))
-            if a == 0 and (jt, hf) in [(2, 0), (3, 0)]:
+            if a == 0 and (jt, hf) in [(2, 1), (3, 1)]:
                 gate_sums[jt, hf] = psum.tile([P, HALF], F32, name="ga", tag="misc")
             elif a == 0:
                 gate_sums[jt, hf] = psum_mm.tile([P, HALF], F32, name="ga", tag="sum")
@@ -206,7 +206,7 @@ def tile_list_relu_biasP_kernel(
         def turn(jt0, tiles, a):
             width = P * tiles
             turned = psum.tile([P, 2, width], F32, name="turned", tag="misc")
-            for k in range(tiles):
+            for k in reversed(range(tiles)):
                 words = h_rows[jt0 + k, a][:].rearrange("p u m e -> p (u m e)").bitcast(F32)
                 for u in range(2):
                     nc.tensor.transpose(turned[:, u, P * k : P * (k + 1)], words[:, P * u : P * (u + 1)], ident[:])
@@ -286,10 +286,10 @@ def tile_list_relu_biasP_kernel(
             gather(picked0[:, t, :], 0, t, 0, J)
         for c in range(4):
             weave(woven0[c][:], picked0[:, :, PAIR * c : PAIR * (c + 1)])
-        gather(picked1[:, 0, :], 1, 0, 0, J - P)
+        gather(picked1[:, 0, :], 1, 0, 0, J - 2 * P)
         for c in range(4):
             quant_x(0, woven0[c][:], PAIR * c, PAIR * (c + 1))
-        for jt0, jt1 in [(0, 4), (4, 7)]:
+        for jt0, jt1 in [(0, 4), (4, 6)]:
             gather(picked1[:, 1, P * jt0 : P * jt1], 1, 1, P * jt0, P * jt1)
             for jt in range(jt0, jt1):
                 weave(woven1[jt][:, :, 0:2], picked1[:, :, P * jt : P * (jt + 1)])
@@ -304,45 +304,44 @@ def tile_list_relu_biasP_kernel(
             finish(jt)
         for jt, hf in [(0, 0), (0, 1), (1, 0), (1, 1), (2, 0), (3, 0), (2, 1), (3, 1)]:
             gate_finish(jt, hf)
+        for jt in (4, 5):
+            for t in (2, 3):
+                pick_rest(jt, t, "woven1_%d" % (jt - 2))
         unit(0, 0)
         unit(1, 0)
         unit(0, 1)
         unit(1, 1)
+        finish(4)
         unit(2, 0)
+        finish(5)
         unit(3, 0)
         deal_wd()
-        turn(0, 2, 0)
         turn(0, 2, 1)
+        turn(0, 2, 0)
         unit(2, 1)
-        for t in (2, 3):
-            pick_rest(4, t, "h_0_0")
-        finish(4)
         unit(3, 1)
-        for t in (2, 3):
-            pick_rest(5, t, "h_1_0")
-        finish(5)
         down(0, 2)
-        unit(4, 0)
-        turn(2, 2, 0)
-        turn(2, 2, 1)
-        unit(5, 0)
-        for t in (2, 3):
-            pick_rest(6, t, "h_2_0")
-        finish(6)
-        unit(4, 1)
-        down(2, 2)
         for t in range(PACK):
-            pick_rest(7, t, "h_3_0")
-        finish(7)
+            pick_rest(6, t, "h_0_0")
+        unit(4, 0)
+        finish(6)
+        unit(5, 0)
+        turn(2, 2, 1)
+        turn(2, 2, 0)
+        unit(4, 1)
+        for t in range(PACK):
+            pick_rest(7, t, "h_2_0")
         unit(5, 1)
+        finish(7)
+        down(2, 2)
         unit(6, 0)
-        turn(4, 2, 0)
-        turn(4, 2, 1)
         unit(6, 1)
+        turn(4, 2, 1)
+        turn(4, 2, 0)
         unit(7, 0)
         unit(7, 1)
-        turn(6, 1, 0)
         turn(6, 1, 1)
+        turn(6, 1, 0)
         down(4, 2, psum_mm, "sum")
         turn(7, 1, 0)
         turn(7, 1, 1)

@@ -1,7 +1,6 @@
 from contextlib import ExitStack
 
 import concourse.mybir as mybir
-from concourse.masks import make_identity
 
 K, R, N, T, J = 1024, 1024, 512, 2048, 1024
 FLOPS = 2 * J * (2 * K * R + R * N)
@@ -14,6 +13,7 @@ U16 = mybir.dt.uint16
 FP8X4 = mybir.dt.float8_e4m3fn_x4
 FP4X4 = mybir.dt.float4_e2m1fn_x4
 MULT = mybir.AluOpType.mult
+ADD = mybir.AluOpType.add
 ACT = mybir.ActivationFunctionType
 
 P = 128
@@ -31,9 +31,7 @@ def tile_list_relu_biasP_kernel(
     with ExitStack() as ctx:
         keep = ctx.enter_context(tc.tile_pool(name="keep", bufs=1))
         ring = ctx.enter_context(tc.tile_pool(name="ring", bufs=3))
-        gates = ctx.enter_context(tc.tile_pool(name="gates", bufs=8))
-        psum = ctx.enter_context(tc.psum_pool(name="psum", bufs=2))
-        psum_mm = ctx.enter_context(tc.psum_pool(name="psum_mm", bufs=6))
+        psum = ctx.enter_context(tc.psum_pool(name="psum", bufs=8))
 
         offsets = keep.tile([P, J // 16], U16, name="offsets")
         nc.sync.dma_start(offsets[:], offs)
@@ -44,67 +42,98 @@ def tile_list_relu_biasP_kernel(
             for t in range(PACK):
                 x_plane[a, t] = keep.tile([P, T], F32, name="x_%d_%d" % (a, t))
         wgt_all = keep.tile([P, J], F32, name="wgt_all")
-        wg_w = [keep.tile([P, 2 * R], U8, name="wg_%d" % a, align_bytes=64) for a in range(PASSES)]
-        wu_w = [keep.tile([P, PASSES, HALF], I32, name="wu_%d" % hf, align_bytes=64) for hf in range(2)]
-        wd_raw = keep.tile([P, PASSES, N], I32, name="wd_raw", align_bytes=64)
+        wg_raw = [keep.tile([P, R // 2], I32, name="wg_raw_%d" % a) for a in range(PASSES)]
+        wu_raw = [keep.tile([P, PASSES, HALF], I32, name="wu_raw_%d" % hf, tag="wu_raw_%d" % hf) for hf in range(2)]
+        wd_raw = keep.tile([P, PASSES, N], I32, name="wd_raw")
+        sc_raw = keep.tile([P, R], U8, name="sc_raw")
+        sc_dealt = keep.tile([P, R], U8, name="sc_dealt")
+        gsc = keep.tile([P, PASSES * R], U8, name="gsc", align_bytes=64)
+        usc = keep.tile([P, PASSES * R], U8, name="usc", align_bytes=64)
+        dsc = keep.tile([P, PASSES * N], U8, name="dsc", align_bytes=64)
+        sc_home = [(gsc, 0), (usc, 4), (dsc, 8)]
+        nc.vector.memset(sc_raw[64:96, N:R].bitcast(I32), 0)
+        nc.vector.memset(sc_raw[96:P, :].bitcast(I32), 0)
+        nc.vector.memset(gsc[:].bitcast(I32), 0)
+        nc.vector.memset(usc[:].bitcast(I32), 0)
+        nc.vector.memset(dsc[:].bitcast(I32), 0)
+        for k, (scales, width) in enumerate([(wg_scales, R), (wu_scales, R), (wd_scales, N)]):
+            nc.sync.dma_start(
+                sc_raw[32 * k : 32 * (k + 1), 0:width].bitcast(I32), scales.rearrange("a q r -> q a r").bitcast(I32)
+            )
 
-        wg_sc = keep.tile([P, PASSES, R], U8, name="wg_sc", align_bytes=64)
-        wu_sc = keep.tile([P, R], U8, name="wu_sc", align_bytes=64)
-        nc.vector.memset(wg_sc[:].rearrange("p a r -> p (a r)").bitcast(I32), 0)
-        nc.vector.memset(wu_sc[:].bitcast(I32), 0)
-        ident = keep.tile([P, P], F32, name="ident")
-        make_identity(nc, ident[:])
+        def deal_narrow(dst, src):
+            nc.vector.tensor_copy(dst, src.rearrange("p (g m t) -> p g t m", t=PACK, m=P))
+
+        deal_narrow(sc_dealt[:].rearrange("p (g t m) -> p g t m", t=PACK, m=P), sc_raw[:])
+
+        def place_scales(k, width):
+            home, row = sc_home[k]
+            for q in range(4):
+                nc.sync.dma_start(
+                    home[32 * q + row : 32 * q + row + 4, 0 : PASSES * width].bitcast(I32),
+                    sc_dealt[32 * k + 8 * q : 32 * k + 8 * q + 8, 0:width].bitcast(I32),
+                )
 
         def load_x(a, t):
             nc.sync.dma_start(x_plane[a, t][:], x_rows[a, t])
 
-        load_x(0, 0)
-        nc.sync.dma_start(wgt_all[:, 0:HEAD], wgt[:, 0:HEAD])
-        nc.sync.dma_start(wgt_all[:, HEAD:J], wgt[:, HEAD:J])
-        for t in range(1, PACK):
-            load_x(0, t)
-        load_x(1, 0)
-        load_x(1, 1)
-        for q in range(4):
-            nc.sync.dma_start(
-                wg_sc[32 * q : 32 * q + 4, :, :].bitcast(I32),
-                wg_scales[:, 4 * q : 4 * q + 4, :].rearrange("a q r -> q a r").bitcast(I32),
-            )
-        load_x(1, 2)
-        for q in range(4):
-            nc.sync.dma_start(
-                wu_sc[32 * q + 4 : 32 * q + 12, :].bitcast(I32),
-                wu_scales[:, 4 * q : 4 * q + 4, :].bitcast(I32),
-            )
-
         def load_wu(hf):
             nc.sync.dma_start(
-                wu_w[hf][:],
+                wu_raw[hf][:],
                 wu_words[:, :, HALF * hf : HALF * (hf + 1), :].rearrange("a p r i -> p a (r i)").bitcast(I32),
             )
 
-        nc.sync.dma_start(wg_w[0][:].bitcast(I32), wg_words[0].bitcast(I32))
-        load_x(1, 3)
-        nc.sync.dma_start(wg_w[1][:].bitcast(I32), wg_words[1].bitcast(I32))
+        load_x(0, 0)
+        nc.sync.dma_start(wgt_all[:, 0:HEAD], wgt[:, 0:HEAD])
+        nc.sync.dma_start(wgt_all[:, HEAD:J], wgt[:, HEAD:J])
+        place_scales(0, R)
+        for t in range(1, PACK):
+            load_x(0, t)
+        for t in range(PACK - 1):
+            load_x(1, t)
+        nc.sync.dma_start(wg_raw[0][:], wg_words[0].bitcast(I32))
+        load_x(1, PACK - 1)
+        nc.sync.dma_start(wg_raw[1][:], wg_words[1].bitcast(I32))
         load_wu(0)
+        place_scales(1, R)
         load_wu(1)
         nc.sync.dma_start(wd_raw[:], wd_words.rearrange("a p n i -> p a (n i)").bitcast(I32))
-        wd_sc_raw = keep.tile([P, N], U8, name="wd_sc_raw", align_bytes=64)
-        nc.vector.memset(wd_sc_raw[:].bitcast(I32), 0)
-        for q in range(4):
-            nc.sync.dma_start(
-                wd_sc_raw[32 * q + 8 : 32 * q + 16, :].bitcast(I32),
-                wd_scales[:, 4 * q : 4 * q + 4, :].bitcast(I32),
-            )
-
+        place_scales(2, N)
         bias = keep.tile([P, PACK], F32, name="bias")
         nc.sync.dma_start(bias[:], b.rearrange("(p t) -> p t", t=PACK))
 
-        picked0 = keep.tile([P, PACK, J], F32, name="picked0")
-        picked1 = keep.tile([P, 2, J - 2 * P], F32, name="picked1")
+        wg_w = [keep.tile([P, 2, PACK, 2 * P], U8, name="wg_%d" % a, align_bytes=64) for a in range(PASSES)]
+        wu_w = [keep.tile([P, PASSES, PACK, P], I32, name="wu_%d" % hf, align_bytes=64) for hf in range(2)]
+        wd_w = keep.tile([P, PASSES, PACK, P], I32, name="wd_w", align_bytes=64)
+
+        def plane(k, width, a, c0):
+            home, row = sc_home[k]
+            return home[row:P, width * a + c0 : width * a + c0 + P]
+
+        def deal_words(dst, src):
+            nc.vector.tensor_copy(
+                dst.rearrange("p a t (c i) -> p a c t i", i=4), src.rearrange("p a (c i t) -> p a c t i", i=4, t=PACK)
+            )
+
+        def deal_wg(a):
+            deal_narrow(wg_w[a][:].bitcast(U16), wg_raw[a][:].bitcast(U16))
+
+        picked0 = keep.tile([P, PACK, J], F32, name="picked0", tag="picked0")
+        picked1 = keep.tile([P, 2, J], F32, name="picked1")
         woven0 = [keep.tile([P, PAIR, PACK], BF16, name="woven0_%d" % c, align_bytes=64) for c in range(4)]
-        woven1 = [keep.tile([P, P, PACK], BF16, name="woven1_%d" % jt, tag="woven1_%d" % jt, align_bytes=64) for jt in range(J // P)]
-        xq = [keep.tile([P, J], I32, name="xq_%d" % a, align_bytes=64) for a in range(PASSES)]
+        woven1 = [
+            keep.tile([P, PAIR, PACK], BF16, name="woven1_%d" % c, tag="woven1_%d" % c, align_bytes=64) for c in range(4)
+        ]
+        xq_half = {}
+
+        def xq_tile(a, jh, tag):
+            xq_half[a, jh] = keep.tile([P, HALF], I32, name="xq_%d_%d" % (a, jh), tag=tag, align_bytes=64)
+
+        def xq(a, c0, c1):
+            return xq_half[a, c0 // HALF][:, c0 % HALF : c0 % HALF + c1 - c0].bitcast(FP8X4)
+
+        for a, jh in [(0, 0), (0, 1), (1, 0)]:
+            xq_tile(a, jh, "xq_%d_%d" % (a, jh))
         xs = [keep.tile([P, J], U8, name="xs_%d" % a, align_bytes=64) for a in range(PASSES)]
 
         def gather(dst, a, t, c0, c1):
@@ -117,168 +146,120 @@ def tile_list_relu_biasP_kernel(
             src = src.rearrange("p t (c i) -> p c t i", i=4)
             nc.scalar.activation(dst, src, ACT.Copy)
 
-        def quant_x(a, src, c0, c1):
+        def quant_x(a, src, c):
+            cols = slice(PAIR * c, PAIR * (c + 1))
             nc.vector.quantize_mx(
-                out=xq[a][:, c0:c1].bitcast(FP8X4), scales=xs[a][:, c0:c1], in_=src.rearrange("p j t -> p (j t)")
+                out=xq(a, cols.start, cols.stop), scales=xs[a][:, cols], in_=src.rearrange("p j t -> p (j t)")
             )
 
-        rest = {}
-
-        def first_rest_plane(jt):
-            return 0 if jt >= J // P - 2 else 2
-
-        def pick_rest(jt, t, tag=None):
-            first = first_rest_plane(jt)
-            if jt not in rest:
-                rest[jt] = keep.tile([P, PACK - first, P], F32, name="rest_%d" % jt, tag=tag, align_bytes=64)
-            gather(rest[jt][:, t - first, :], 1, t, P * jt, P * (jt + 1))
-
-        def finish(jt):
-            weave(woven1[jt][:, :, first_rest_plane(jt) : PACK], rest[jt][:])
-            quant_x(1, woven1[jt][:], P * jt, P * (jt + 1))
-
-        h_rows = {}
+        def bank(name):
+            return psum.tile([P, HALF], F32, name=name, tag="bank")
 
         gate_sums = {}
 
-        def gate_pass(jt, hf, a):
-            cols = slice(P * jt, P * (jt + 1))
-            if a == 0 and (jt, hf) in [(2, 1), (3, 1)]:
-                gate_sums[jt, hf] = psum.tile([P, HALF], F32, name="ga", tag="misc")
-            elif a == 0:
-                gate_sums[jt, hf] = psum_mm.tile([P, HALF], F32, name="ga", tag="sum")
+        def gate_pass(hf, t, jh, a):
+            cols = slice(HALF * jh, HALF * (jh + 1))
+            if a == 0:
+                gate_sums[hf, t, jh] = bank("ga")
             nc.tensor.matmul_mx(
-                out=gate_sums[jt, hf][:],
-                lhsT=xq[a][:, cols].bitcast(FP8X4),
-                lhsT_scale=xs[a][:, cols],
-                rhs=wg_w[a][:, 2 * HALF * hf : 2 * HALF * (hf + 1)].bitcast(FP4X4),
-                rhs_scale=wg_sc[:, a, HALF * hf : HALF * (hf + 1)],
+                out=gate_sums[hf, t, jh][:],
+                lhsT=wg_w[a][:, hf, t, :].bitcast(FP4X4),
+                lhsT_scale=plane(0, R, a, HALF * hf + P * t),
+                rhs=xq(a, cols.start, cols.stop),
+                rhs_scale=xs[a][:, cols],
                 start=(a == 0),
                 stop=(a == PASSES - 1),
             )
 
         gate_rows = {}
 
-        def gate_finish(jt, hf):
-            if (jt, hf) not in gate_sums:
-                gate_pass(jt, hf, 0)
-            gate_pass(jt, hf, 1)
-            gate = gates.tile([P, 2, P, 2], F32, name="gate")
-            nc.scalar.activation(gate[:], gate_sums[jt, hf][:].rearrange("p (m u e) -> p u m e", u=2, e=2), ACT.Relu)
-            gate_rows[jt, hf] = gate
-
-        up_sums = {}
-
-        def up_pass(jt, hf, a):
-            cols = slice(P * jt, P * (jt + 1))
-            if a == 0:
-                up_sums[jt, hf] = psum_mm.tile([P, HALF], F32, name="ub", tag="sum")
-            nc.tensor.matmul_mx(
-                out=up_sums[jt, hf][:],
-                lhsT=xq[a][:, cols].bitcast(FP8X4),
-                lhsT_scale=xs[a][:, cols],
-                rhs=wu_w[hf][:, a, :].bitcast(FP8X4),
-                rhs_scale=wu_sc[4 + 4 * a : P, HALF * hf : HALF * (hf + 1)],
-                start=(a == 0),
-                stop=(a == PASSES - 1),
-            )
-
-        def unit(jt, hf):
-            if (jt, hf) not in gate_rows:
-                gate_finish(jt, hf)
-            gate = gate_rows[jt, hf]
-            if (jt, hf) not in up_sums:
-                up_pass(jt, hf, 0)
-            up_pass(jt, hf, 1)
-            ub = up_sums[jt, hf]
-            h = keep.tile([P, 2, P, 2], BF16, name="h_%d_%d" % (jt, hf), tag="h_%d_%d" % (jt, hf), align_bytes=64)
-            sums = ub[:].rearrange("p (m u e) -> p u m e", u=2, e=2)
-            if (jt, hf) == (7, 1):
-                for u in range(2):
-                    nc.vector.tensor_tensor(h[:, u, :, :], sums[:, u, :, :], gate[:, u, :, :], MULT)
-            else:
-                nc.vector.tensor_tensor(h[:], sums, gate[:], MULT)
-            h_rows[jt, hf] = h
+        def gate_finish(hf, jh):
+            gate_rows[hf, jh] = keep.tile([P, PACK, HALF], F32, name="gate", tag="gate_%d_%d" % (hf, jh), align_bytes=64)
+            for t in range(PACK):
+                if (hf, t, jh) not in gate_sums:
+                    gate_pass(hf, t, jh, 0)
+                gate_pass(hf, t, jh, 1)
+                nc.scalar.activation(gate_rows[hf, jh][:, t, :], gate_sums[hf, t, jh][:], ACT.Relu)
 
         hq = [keep.tile([P, J], I32, name="hq_%d" % a, align_bytes=64) for a in range(PASSES)]
         hs = [keep.tile([P, J], U8, name="hs_%d" % a, align_bytes=64) for a in range(PASSES)]
+        h_woven = {}
 
-        def turn(jt0, tiles, a):
-            width = P * tiles
-            turned = psum.tile([P, 2, width], F32, name="turned", tag="misc")
-            for k in reversed(range(tiles)):
-                words = h_rows[jt0 + k, a][:].rearrange("p u m e -> p (u m e)").bitcast(F32)
-                for u in range(2):
-                    nc.tensor.transpose(turned[:, u, P * k : P * (k + 1)], words[:, P * u : P * (u + 1)], ident[:])
-            woven = ring.tile([P, width, PACK], BF16, name="hw", align_bytes=64)
-            flat = woven[:].rearrange("p j t -> p (j t)")
-            nc.scalar.copy(flat.bitcast(F32).rearrange("p (j u) -> p j u", u=2), turned[:].rearrange("p u j -> p j u"))
-            cols = slice(P * jt0, P * jt0 + width)
-            nc.vector.quantize_mx(out=hq[a][:, cols].bitcast(FP8X4), scales=hs[a][:, cols], in_=flat)
+        def unit(hf, jt, tiles):
+            cols = slice(P * jt, P * (jt + 1))
+            ub = bank("ub")
+            for t in range(PACK):
+                for a in range(PASSES):
+                    nc.tensor.matmul_mx(
+                        out=ub[:, P * t : P * (t + 1)],
+                        lhsT=wu_w[hf][:, a, t, :].bitcast(FP8X4),
+                        lhsT_scale=plane(1, R, a, HALF * hf + P * t),
+                        rhs=xq(a, cols.start, cols.stop),
+                        rhs_scale=xs[a][:, cols],
+                        start=(a == 0),
+                        stop=(a == PASSES - 1),
+                    )
+            first = jt - jt % tiles
+            if jt == first:
+                h_woven[hf, first] = ring.tile([P, P * tiles, PACK], BF16, name="hw", align_bytes=64)
+            woven = h_woven[hf, first]
+            c0 = P * (jt % 4)
+            nc.vector.tensor_tensor(
+                woven[:, P * (jt - first) : P * (jt - first + 1), :].rearrange("p (c i) t -> p c t i", i=2),
+                ub[:].rearrange("p (t c i) -> p c t i", t=PACK, i=2),
+                gate_rows[hf, jt // 4][:, :, c0 : c0 + P].rearrange("p t (c i) -> p c t i", i=2),
+                MULT,
+            )
 
-        wd_w = keep.tile([P, PASSES, PACK, P], I32, name="wd_w", align_bytes=64)
-        wd_sc = keep.tile([P, PACK, P], U8, name="wd_sc", align_bytes=64)
-
-        def deal_wd():
-            nc.gpsimd.tensor_copy(wd_sc[:], wd_sc_raw[:].rearrange("p (m t) -> p t m", t=PACK))
-            for a in range(PASSES):
-                nc.gpsimd.tensor_copy(wd_w[:, a, :, :], wd_raw[:, a, :].rearrange("p (m t) -> p t m", t=PACK))
+        def quant_h(hf, first, tiles):
+            cols = slice(P * first, P * (first + tiles))
+            nc.vector.quantize_mx(
+                out=hq[hf][:, cols].bitcast(FP8X4),
+                scales=hs[hf][:, cols],
+                in_=h_woven[hf, first][:].rearrange("p j t -> p (j t)"),
+            )
 
         out_rows = out_0.rearrange("(p t) j -> p t j", t=PACK)
         out_words = out_1[0].rearrange("p j i -> p (j i)").bitcast(I32)
         y_sc = keep.tile([P, J], U8, name="y_sc", align_bytes=64)
+        y_all = keep.tile([P, PACK * J], F32, name="y_all", tag="picked0")
 
-        def down_pass(out, t, a, cols):
-            nc.tensor.matmul_mx(
-                out=out,
-                lhsT=wd_w[:, a, t, :].bitcast(FP8X4),
-                lhsT_scale=wd_sc[8 + 4 * a : P, t, :],
-                rhs=hq[a][:, cols].bitcast(FP8X4),
-                rhs_scale=hs[a][:, cols],
-                start=(a == 0),
-                stop=(a == PASSES - 1),
-            )
-
-        def hand_out(y, cols, width):
-            nc.sync.dma_start(out_rows[:, :, cols], y[:])
+        def down(jt0, tiles):
+            width = P * tiles
+            per_bank = HALF // width
+            cols = slice(P * jt0, P * jt0 + width)
+            y = y_all[:, PACK * P * jt0 : PACK * (P * jt0 + width)].rearrange("p (t j) -> p t j", t=PACK)
+            for t0 in range(0, PACK, per_bank):
+                acc = bank("acc")
+                for e in range(per_bank):
+                    for a in range(PASSES):
+                        nc.tensor.matmul_mx(
+                            out=acc[:, width * e : width * (e + 1)],
+                            lhsT=wd_w[:, a, t0 + e, :].bitcast(FP8X4),
+                            lhsT_scale=plane(2, N, a, P * (t0 + e)),
+                            rhs=hq[a][:, cols].bitcast(FP8X4),
+                            rhs_scale=hs[a][:, cols],
+                            start=(a == 0),
+                            stop=(a == PASSES - 1),
+                        )
+                for e in range(per_bank):
+                    t = t0 + e
+                    nc.scalar.activation(
+                        y[:, t, :], acc[:, width * e : width * (e + 1)], ACT.Identity, bias=bias[:, t : t + 1]
+                    )
+            nc.sync.dma_start(out_rows[:, :, cols], y)
             woven = ring.tile([P, width, PACK], BF16, name="yw", align_bytes=64)
-            nc.vector.tensor_copy(
-                woven[:].rearrange("p (c i) t -> p c t i", i=4), y[:].rearrange("p t (c i) -> p c t i", i=4)
-            )
+            if tiles > 1:
+                weave(woven[:], y)
+            else:
+                nc.vector.tensor_copy(
+                    woven[:].rearrange("p (c i) t -> p c t i", i=4), y.rearrange("p t (c i) -> p c t i", i=4)
+                )
             yq = ring.tile([P, width], I32, name="yq", align_bytes=64)
             nc.vector.quantize_mx(
                 out=yq[:].bitcast(FP8X4), scales=y_sc[:, cols], in_=woven[:].rearrange("p j t -> p (j t)")
             )
             nc.sync.dma_start(out_words[:, cols], yq[:])
-
-        def down(jt0, tiles, pool=psum, tag="misc"):
-            width = P * tiles
-            per_bank = HALF // width
-            cols = slice(P * jt0, P * jt0 + width)
-            y = ring.tile([P, PACK, width], F32, name="y")
-            for t0 in range(0, PACK, per_bank):
-                acc = pool.tile([P, per_bank, width], F32, name="acc", tag=tag)
-                for e in range(per_bank):
-                    for a in range(PASSES):
-                        down_pass(acc[:, e, :], t0 + e, a, cols)
-                for e in range(per_bank):
-                    t = t0 + e
-                    nc.scalar.activation(y[:, t, :], acc[:, e, :], ACT.Identity, bias=bias[:, t : t + 1])
-            hand_out(y, cols, width)
-
-        def down_last(jt):
-            cols = slice(P * jt, P * (jt + 1))
-            y = ring.tile([P, PACK, P], F32, name="y")
-            accs = [psum_mm.tile([P, P], F32, name="acc_%d" % t, tag="sum") for t in range(PACK)]
-            for a in range(PASSES):
-                for t in range(PACK):
-                    down_pass(accs[t][:], t, a, cols)
-            for t in range(PACK):
-                if t % 2 == 0:
-                    nc.vector.tensor_scalar_add(y[:, t, :], accs[t][:], bias[:, t : t + 1])
-                else:
-                    nc.scalar.activation(y[:, t, :], accs[t][:], ACT.Identity, bias=bias[:, t : t + 1])
-            hand_out(y, cols, P)
 
         gather(picked0[:, 0, 0:HEAD], 0, 0, 0, HEAD)
         gather(picked0[:, 0, HEAD:J], 0, 0, HEAD, J)
@@ -286,67 +267,64 @@ def tile_list_relu_biasP_kernel(
             gather(picked0[:, t, :], 0, t, 0, J)
         for c in range(4):
             weave(woven0[c][:], picked0[:, :, PAIR * c : PAIR * (c + 1)])
-        gather(picked1[:, 0, :], 1, 0, 0, J - 2 * P)
+        gather(picked1[:, 0, :], 1, 0, 0, J)
         for c in range(4):
-            quant_x(0, woven0[c][:], PAIR * c, PAIR * (c + 1))
-        for jt0, jt1 in [(0, 4), (4, 6)]:
-            gather(picked1[:, 1, P * jt0 : P * jt1], 1, 1, P * jt0, P * jt1)
-            for jt in range(jt0, jt1):
-                weave(woven1[jt][:, :, 0:2], picked1[:, :, P * jt : P * (jt + 1)])
-        for jt in range(4):
-            pick_rest(jt, 2, "rest_%d" % jt)
-        for jt, hf in [(0, 0), (0, 1), (1, 0), (1, 1), (2, 0), (3, 0), (2, 1), (3, 1)]:
-            gate_pass(jt, hf, 0)
+            quant_x(0, woven0[c][:], c)
+        gather(picked1[:, 1, :], 1, 1, 0, J)
+        for c in range(4):
+            weave(woven1[c][:, :, 0:2], picked1[:, :, PAIR * c : PAIR * (c + 1)])
+        late0 = keep.tile([P, 2, HALF], F32, name="late0")
+        gather(late0[:, 0, :], 1, 2, 0, HALF)
+        deal_wg(0)
+        for hf in range(2):
+            for t in range(PACK):
+                gate_pass(hf, t, 0, 0)
 
         for jt in range(4):
-            pick_rest(jt, 3)
-        for jt in range(4):
-            finish(jt)
-        for jt, hf in [(0, 0), (0, 1), (1, 0), (1, 1), (2, 0), (3, 0), (2, 1), (3, 1)]:
-            gate_finish(jt, hf)
+            gather(late0[:, 1, P * jt : P * (jt + 1)], 1, 3, P * jt, P * (jt + 1))
+            weave(woven1[jt // 2][:, P * (jt % 2) : P * (jt % 2 + 1), 2:4], late0[:, :, P * jt : P * (jt + 1)])
+        deal_wg(1)
+        for c in range(2):
+            quant_x(1, woven1[c][:], c)
+        for hf in range(2):
+            gate_finish(hf, 0)
+        deal_words(wu_w[0][:], wu_raw[0][:])
+        late1 = keep.tile([P, 2, HALF], F32, name="late1", tag="wu_raw_0")
+        for t in (2, 3):
+            gather(late1[:, t - 2, :], 1, t, HALF, J)
+        deal_words(wu_w[1][:], wu_raw[1][:])
+        for c in (2, 3):
+            weave(woven1[c][:, :, 2:4], late1[:, :, PAIR * (c - 2) : PAIR * (c - 1)])
+        for hf in range(2):
+            for jt in range(4):
+                unit(hf, jt, 2)
+                if jt == 3 and hf == 0:
+                    xq_tile(1, 1, "gate_0_0")
+                    for c in (2, 3):
+                        quant_x(1, woven1[c][:], c)
+                if jt == 2:
+                    quant_h(hf, 0, 2)
+            quant_h(hf, 2, 2)
+        deal_words(wd_w[:], wd_raw[:])
+        for hf in range(2):
+            gate_finish(hf, 1)
+        down(0, 4)
         for jt in (4, 5):
-            for t in (2, 3):
-                pick_rest(jt, t, "woven1_%d" % (jt - 2))
-        unit(0, 0)
-        unit(1, 0)
-        unit(0, 1)
-        unit(1, 1)
-        finish(4)
-        unit(2, 0)
-        finish(5)
-        unit(3, 0)
-        deal_wd()
-        turn(0, 2, 1)
-        turn(0, 2, 0)
-        unit(2, 1)
-        unit(3, 1)
-        down(0, 2)
-        for t in range(PACK):
-            pick_rest(6, t, "h_0_0")
-        unit(4, 0)
-        finish(6)
-        unit(5, 0)
-        turn(2, 2, 1)
-        turn(2, 2, 0)
-        unit(4, 1)
-        for t in range(PACK):
-            pick_rest(7, t, "h_2_0")
-        unit(5, 1)
-        finish(7)
-        down(2, 2)
-        unit(6, 0)
-        unit(6, 1)
-        turn(4, 2, 1)
-        turn(4, 2, 0)
-        unit(7, 0)
-        unit(7, 1)
-        turn(6, 1, 1)
-        turn(6, 1, 0)
-        down(4, 2, psum_mm, "sum")
-        turn(7, 1, 0)
-        turn(7, 1, 1)
-        down(6, 1, psum_mm, "sum")
-        down_last(7)
+            for hf in range(2):
+                unit(hf, jt, 2)
+        unit(0, 6, 1)
+        quant_h(0, 4, 2)
+        unit(1, 6, 1)
+        quant_h(1, 4, 2)
+        down(4, 2)
+        unit(0, 7, 1)
+        quant_h(0, 6, 1)
+        unit(1, 7, 1)
+        quant_h(1, 6, 1)
+        quant_h(0, 7, 1)
+        quant_h(1, 7, 1)
+        down(6, 1)
+        down(7, 1)
         for q in range(4):
             eng = nc.sync if q % 2 == 0 else nc.scalar
             eng.dma_start(out_2[0, 4 * q : 4 * q + 4, :].bitcast(I32), y_sc[32 * q : 32 * q + 4, :].bitcast(I32))

@@ -1,6 +1,7 @@
 from contextlib import ExitStack
 
 import concourse.mybir as mybir
+from concourse.masks import make_identity
 
 K, R, N, T, J = 1024, 1024, 512, 2048, 1024
 FLOPS = 2 * J * (2 * K * R + R * N)
@@ -36,6 +37,14 @@ def tile_list_relu_biasP_kernel(
         offsets = keep.tile([P, J // 16], U16, name="offsets")
         nc.sync.dma_start(offsets[:], offs)
 
+        wgt_rows = keep.tile([P, P], F32, name="wgt_rows")
+        nc.sync.dma_start(
+            wgt_rows[0:64, :], wgt.rearrange("(g r) (jt s) -> r g jt s", r=16, s=P)[0]
+        )
+        nc.vector.memset(wgt_rows[64:P, :], 0.0)
+        ident = keep.tile([P, P], F32, name="ident")
+        make_identity(nc, ident[:])
+
         x_rows = xT.rearrange("(a p t) n -> a t p n", a=PASSES, t=PACK)
         x_plane = {}
         for a in range(PASSES):
@@ -57,7 +66,7 @@ def tile_list_relu_biasP_kernel(
         nc.vector.memset(usc[:].bitcast(I32), 0)
         nc.vector.memset(dsc[:].bitcast(I32), 0)
         for k, (scales, width) in enumerate([(wg_scales, R), (wu_scales, R), (wd_scales, N)]):
-            nc.sync.dma_start(
+            nc.scalar.dma_start(
                 sc_raw[32 * k : 32 * (k + 1), 0:width].bitcast(I32), scales.rearrange("a q r -> q a r").bitcast(I32)
             )
 
@@ -84,8 +93,6 @@ def tile_list_relu_biasP_kernel(
             )
 
         load_x(0, 0)
-        nc.sync.dma_start(wgt_all[:, 0:HEAD], wgt[:, 0:HEAD])
-        nc.sync.dma_start(wgt_all[:, HEAD:J], wgt[:, HEAD:J])
         place_scales(0, R)
         for t in range(1, PACK):
             load_x(0, t)
@@ -132,7 +139,7 @@ def tile_list_relu_biasP_kernel(
         def xq(a, c0, c1):
             return xq_half[a, c0 // HALF][:, c0 % HALF : c0 % HALF + c1 - c0].bitcast(FP8X4)
 
-        for a, jh in [(0, 0), (0, 1), (1, 0)]:
+        for a, jh in [(0, 0), (0, 1), (1, 0), (1, 1)]:
             xq_tile(a, jh, "xq_%d_%d" % (a, jh))
         xs = [keep.tile([P, J], U8, name="xs_%d" % a, align_bytes=64) for a in range(PASSES)]
 
@@ -173,13 +180,16 @@ def tile_list_relu_biasP_kernel(
 
         gate_rows = {}
 
-        def gate_finish(hf, jh):
-            gate_rows[hf, jh] = keep.tile([P, PACK, HALF], F32, name="gate", tag="gate_%d_%d" % (hf, jh), align_bytes=64)
+        def gate_relu(hf, jh):
+            gate_rows[hf, jh] = keep.tile([P, PACK, HALF], F32, name="gate_%d_%d" % (hf, jh))
             for t in range(PACK):
-                if (hf, t, jh) not in gate_sums:
-                    gate_pass(hf, t, jh, 0)
-                gate_pass(hf, t, jh, 1)
                 nc.scalar.activation(gate_rows[hf, jh][:, t, :], gate_sums[hf, t, jh][:], ACT.Relu)
+
+        def gate_whole(hf, jh):
+            for t in range(PACK):
+                for a in range(PASSES):
+                    gate_pass(hf, t, jh, a)
+            gate_relu(hf, jh)
 
         hq = [keep.tile([P, J], I32, name="hq_%d" % a, align_bytes=64) for a in range(PASSES)]
         hs = [keep.tile([P, J], U8, name="hs_%d" % a, align_bytes=64) for a in range(PASSES)]
@@ -261,6 +271,16 @@ def tile_list_relu_biasP_kernel(
             )
             nc.sync.dma_start(out_words[:, cols], yq[:])
 
+        by_token = bank("by_token")
+        nc.tensor.transpose(by_token[:, 0:P], wgt_rows[:], ident[:])
+        per_tile = by_token[:, 0:64].rearrange("p (g jt) -> p jt g", g=8)
+        for c in range(4):
+            wide = ring.tile([P, 2, 8, 16], F32, name="wide")
+            nc.scalar.copy(wide[:], per_tile[:, 2 * c : 2 * c + 2, :].unsqueeze(3).to_broadcast([P, 2, 8, 16]))
+            spread = bank("spread")
+            for e in range(2):
+                nc.tensor.transpose(spread[:, P * e : P * (e + 1)], wide[:, e].rearrange("p g r -> p (g r)"), ident[:])
+            nc.scalar.copy(wgt_all[:, PAIR * c : PAIR * (c + 1)], spread[:, 0:PAIR])
         gather(picked0[:, 0, 0:HEAD], 0, 0, 0, HEAD)
         gather(picked0[:, 0, HEAD:J], 0, 0, HEAD, J)
         for t in range(1, PACK):
@@ -287,7 +307,9 @@ def tile_list_relu_biasP_kernel(
         for c in range(2):
             quant_x(1, woven1[c][:], c)
         for hf in range(2):
-            gate_finish(hf, 0)
+            for t in range(PACK):
+                gate_pass(hf, t, 0, 1)
+        gate_relu(0, 0)
         deal_words(wu_w[0][:], wu_raw[0][:])
         late1 = keep.tile([P, 2, HALF], F32, name="late1", tag="wu_raw_0")
         for t in (2, 3):
@@ -295,19 +317,17 @@ def tile_list_relu_biasP_kernel(
         deal_words(wu_w[1][:], wu_raw[1][:])
         for c in (2, 3):
             weave(woven1[c][:, :, 2:4], late1[:, :, PAIR * (c - 2) : PAIR * (c - 1)])
+        gate_relu(1, 0)
+        for c in (2, 3):
+            quant_x(1, woven1[c][:], c)
         for hf in range(2):
             for jt in range(4):
                 unit(hf, jt, 2)
-                if jt == 3 and hf == 0:
-                    xq_tile(1, 1, "gate_0_0")
-                    for c in (2, 3):
-                        quant_x(1, woven1[c][:], c)
                 if jt == 2:
                     quant_h(hf, 0, 2)
             quant_h(hf, 2, 2)
+            gate_whole(hf, 1)
         deal_words(wd_w[:], wd_raw[:])
-        for hf in range(2):
-            gate_finish(hf, 1)
         down(0, 4)
         for jt in (4, 5):
             for hf in range(2):

@@ -52,23 +52,37 @@ def tile_list_relu_biasP_kernel(
                 x_plane[a, t] = keep.tile([P, T], F32, name="x_%d_%d" % (a, t))
         wgt_all = keep.tile([P, J], F32, name="wgt_all")
         wg_raw = [keep.tile([P, R // 2], I32, name="wg_raw_%d" % a) for a in range(PASSES)]
-        wu_raw = [keep.tile([P, PASSES, HALF], I32, name="wu_raw_%d" % hf, tag="wu_raw_%d" % hf) for hf in range(2)]
+        wu_raw = [keep.tile([P, PASSES, HALF], I32, name="wu_raw_%d" % hf, tag="wu_raw_%d" % hf, align_bytes=64) for hf in range(2)]
         wd_raw = keep.tile([P, PASSES, N], I32, name="wd_raw")
         sc_raw = keep.tile([P, R], U8, name="sc_raw")
         sc_dealt = keep.tile([P, R], U8, name="sc_dealt")
         gsc = keep.tile([P, PASSES * R], U8, name="gsc", align_bytes=64)
         usc = keep.tile([P, PASSES * R], U8, name="usc", align_bytes=64)
-        dsc = keep.tile([P, PASSES * N], U8, name="dsc", align_bytes=64)
-        sc_home = [(gsc, 0), (usc, 4), (dsc, 8)]
-        nc.vector.memset(sc_raw[64:96, N:R].bitcast(I32), 0)
-        nc.vector.memset(sc_raw[96:P, :].bitcast(I32), 0)
+        dsc = keep.tile([P, N], U8, name="dsc", align_bytes=64)
+        dsc_raw = keep.tile([P, N], U8, name="dsc_raw")
+        sc_home = [(gsc, 0), (usc, 4)]
+        nc.vector.memset(sc_raw[64:P, :].bitcast(I32), 0)
         nc.vector.memset(gsc[:].bitcast(I32), 0)
         nc.vector.memset(usc[:].bitcast(I32), 0)
-        nc.vector.memset(dsc[:].bitcast(I32), 0)
-        for k, (scales, width) in enumerate([(wg_scales, R), (wu_scales, R), (wd_scales, N)]):
+        nc.vector.memset(dsc_raw[:].bitcast(I32), 0)
+        for k, scales in enumerate([wg_scales, wu_scales]):
             nc.scalar.dma_start(
-                sc_raw[32 * k : 32 * (k + 1), 0:width].bitcast(I32), scales.rearrange("a q r -> q a r").bitcast(I32)
+                sc_raw[32 * k : 32 * (k + 1), :].bitcast(I32), scales.rearrange("a q r -> q a r").bitcast(I32)
             )
+
+        def bank(name):
+            return psum.tile([P, HALF], F32, name=name, tag="bank")
+
+        by_token = bank("by_token")
+        nc.tensor.transpose(by_token[:, 0:P], wgt_rows[:], ident[:])
+        per_tile = by_token[:, 0:64].rearrange("p (g jt) -> p jt g", g=8)
+        for c in range(4):
+            wide = ring.tile([P, 2, 8, 16], F32, name="wide", bufs=4)
+            nc.vector.tensor_copy(wide[:], per_tile[:, 2 * c : 2 * c + 2, :].unsqueeze(3).to_broadcast([P, 2, 8, 16]))
+            spread = bank("spread")
+            for e in range(2):
+                nc.tensor.transpose(spread[:, P * e : P * (e + 1)], wide[:, e].rearrange("p g r -> p (g r)"), ident[:])
+            nc.scalar.copy(wgt_all[:, PAIR * c : PAIR * (c + 1)], spread[:, 0:PAIR])
 
         def deal_narrow(dst, src):
             nc.vector.tensor_copy(dst, src.rearrange("p (g m t) -> p g t m", t=PACK, m=P))
@@ -105,7 +119,10 @@ def tile_list_relu_biasP_kernel(
         place_scales(1, R)
         load_wu(1)
         nc.sync.dma_start(wd_raw[:], wd_words.rearrange("a p n i -> p a (n i)").bitcast(I32))
-        place_scales(2, N)
+        for q in range(4):
+            nc.sync.dma_start(
+                dsc_raw[32 * q + 8 : 32 * q + 16, :].bitcast(I32), wd_scales[:, 4 * q : 4 * q + 4, :].bitcast(I32)
+            )
         bias = keep.tile([P, PACK], F32, name="bias")
         nc.sync.dma_start(bias[:], b.rearrange("(p t) -> p t", t=PACK))
 
@@ -126,7 +143,8 @@ def tile_list_relu_biasP_kernel(
             deal_narrow(wg_w[a][:].bitcast(U16), wg_raw[a][:].bitcast(U16))
 
         picked0 = keep.tile([P, PACK, J], F32, name="picked0", tag="picked0")
-        picked1 = keep.tile([P, 2, J], F32, name="picked1")
+        picked1 = keep.tile([P, 2, HALF], F32, name="picked1")
+        early1 = keep.tile([P, 1, HALF], F32, name="early1")
         woven0 = [keep.tile([P, PAIR, PACK], BF16, name="woven0_%d" % c, align_bytes=64) for c in range(4)]
         woven1 = [
             keep.tile([P, PAIR, PACK], BF16, name="woven1_%d" % c, tag="woven1_%d" % c, align_bytes=64) for c in range(4)
@@ -139,7 +157,7 @@ def tile_list_relu_biasP_kernel(
         def xq(a, c0, c1):
             return xq_half[a, c0 // HALF][:, c0 % HALF : c0 % HALF + c1 - c0].bitcast(FP8X4)
 
-        for a, jh in [(0, 0), (0, 1), (1, 0), (1, 1)]:
+        for a, jh in [(0, 0), (1, 0), (1, 1)]:
             xq_tile(a, jh, "xq_%d_%d" % (a, jh))
         xs = [keep.tile([P, J], U8, name="xs_%d" % a, align_bytes=64) for a in range(PASSES)]
 
@@ -158,9 +176,6 @@ def tile_list_relu_biasP_kernel(
             nc.vector.quantize_mx(
                 out=xq(a, cols.start, cols.stop), scales=xs[a][:, cols], in_=src.rearrange("p j t -> p (j t)")
             )
-
-        def bank(name):
-            return psum.tile([P, HALF], F32, name=name, tag="bank")
 
         gate_sums = {}
 
@@ -195,7 +210,7 @@ def tile_list_relu_biasP_kernel(
         hs = [keep.tile([P, J], U8, name="hs_%d" % a, align_bytes=64) for a in range(PASSES)]
         h_woven = {}
 
-        def unit(hf, jt, tiles):
+        def unit(hf, jt, tiles, tag=None):
             cols = slice(P * jt, P * (jt + 1))
             ub = bank("ub")
             for t in range(PACK):
@@ -210,8 +225,10 @@ def tile_list_relu_biasP_kernel(
                         stop=(a == PASSES - 1),
                     )
             first = jt - jt % tiles
-            if jt == first:
-                h_woven[hf, first] = ring.tile([P, P * tiles, PACK], BF16, name="hw", align_bytes=64)
+            if tag is not None:
+                h_woven[hf, first] = keep.tile([P, P * tiles, PACK], BF16, name="hw", tag=tag, align_bytes=64)
+            elif jt == first:
+                h_woven[hf, first] = ring.tile([P, P * tiles, PACK], BF16, name="hw", bufs=4, align_bytes=64)
             woven = h_woven[hf, first]
             c0 = P * (jt % 4)
             nc.vector.tensor_tensor(
@@ -246,7 +263,7 @@ def tile_list_relu_biasP_kernel(
                         nc.tensor.matmul_mx(
                             out=acc[:, width * e : width * (e + 1)],
                             lhsT=wd_w[:, a, t0 + e, :].bitcast(FP8X4),
-                            lhsT_scale=plane(2, N, a, P * (t0 + e)),
+                            lhsT_scale=dsc[8 + 4 * a : P, P * (t0 + e) : P * (t0 + e + 1)],
                             rhs=hq[a][:, cols].bitcast(FP8X4),
                             rhs_scale=hs[a][:, cols],
                             start=(a == 0),
@@ -259,40 +276,64 @@ def tile_list_relu_biasP_kernel(
                     )
             nc.sync.dma_start(out_rows[:, :, cols], y)
             woven = ring.tile([P, width, PACK], BF16, name="yw", align_bytes=64)
-            if tiles > 1:
-                weave(woven[:], y)
-            else:
-                nc.vector.tensor_copy(
-                    woven[:].rearrange("p (c i) t -> p c t i", i=4), y.rearrange("p t (c i) -> p c t i", i=4)
-                )
+            weave(woven[:], y)
+            hand_out_planes(woven, cols)
+
+        def down_tile(jt):
+            cols = slice(P * jt, P * (jt + 1))
+            y = y_all[:, PACK * P * jt : PACK * P * (jt + 1)].rearrange("p (t j) -> p t j", t=PACK)
+            acc = bank("acc")
+            for a in range(PASSES):
+                for t in range(PACK):
+                    nc.tensor.matmul_mx(
+                        out=acc[:, P * t : P * (t + 1)],
+                        lhsT=wd_w[:, a, t, :].bitcast(FP8X4),
+                        lhsT_scale=dsc[8 + 4 * a : P, P * t : P * (t + 1)],
+                        rhs=hq[a][:, cols].bitcast(FP8X4),
+                        rhs_scale=hs[a][:, cols],
+                        start=(a == 0 and t == 0),
+                        stop=(a == PASSES - 1 and t == PACK - 1),
+                    )
+            woven = ring.tile([P, P, PACK], BF16, name="yw", align_bytes=64)
+            nc.vector.tensor_tensor(
+                woven[:].rearrange("p j t -> p j t"),
+                acc[:].rearrange("p (t j) -> p j t", t=PACK),
+                bias[:].unsqueeze(1).to_broadcast([P, P, PACK]),
+                ADD,
+            )
+            hand_out_planes(woven, cols)
+            for t in range(PACK):
+                nc.scalar.activation(y[:, t, :], acc[:, P * t : P * (t + 1)], ACT.Identity, bias=bias[:, t : t + 1])
+            nc.sync.dma_start(out_rows[:, :, cols], y)
+
+        def hand_out_planes(woven, cols):
+            width = cols.stop - cols.start
             yq = ring.tile([P, width], I32, name="yq", align_bytes=64)
             nc.vector.quantize_mx(
                 out=yq[:].bitcast(FP8X4), scales=y_sc[:, cols], in_=woven[:].rearrange("p j t -> p (j t)")
             )
             nc.sync.dma_start(out_words[:, cols], yq[:])
 
-        by_token = bank("by_token")
-        nc.tensor.transpose(by_token[:, 0:P], wgt_rows[:], ident[:])
-        per_tile = by_token[:, 0:64].rearrange("p (g jt) -> p jt g", g=8)
-        for c in range(4):
-            wide = ring.tile([P, 2, 8, 16], F32, name="wide")
-            nc.scalar.copy(wide[:], per_tile[:, 2 * c : 2 * c + 2, :].unsqueeze(3).to_broadcast([P, 2, 8, 16]))
-            spread = bank("spread")
-            for e in range(2):
-                nc.tensor.transpose(spread[:, P * e : P * (e + 1)], wide[:, e].rearrange("p g r -> p (g r)"), ident[:])
-            nc.scalar.copy(wgt_all[:, PAIR * c : PAIR * (c + 1)], spread[:, 0:PAIR])
         gather(picked0[:, 0, 0:HEAD], 0, 0, 0, HEAD)
-        gather(picked0[:, 0, HEAD:J], 0, 0, HEAD, J)
-        for t in range(1, PACK):
+        gather(picked0[:, 0, HEAD:HALF], 0, 0, HEAD, HALF)
+        gather(picked0[:, 0, HALF:J], 0, 0, HALF, J)
+        for t in range(1, PACK - 1):
             gather(picked0[:, t, :], 0, t, 0, J)
         for c in range(4):
-            weave(woven0[c][:], picked0[:, :, PAIR * c : PAIR * (c + 1)])
-        gather(picked1[:, 0, :], 1, 0, 0, J)
+            weave(woven0[c][:, :, 0:3], picked0[:, 0:3, PAIR * c : PAIR * (c + 1)])
+        for jh in range(2):
+            gather(picked0[:, 3, HALF * jh : HALF * (jh + 1)], 0, 3, HALF * jh, HALF * (jh + 1))
         for c in range(4):
+            weave(woven0[c][:, :, 3:4], picked0[:, 3:4, PAIR * c : PAIR * (c + 1)])
+        gather(picked1[:, 0, :], 1, 0, 0, HALF)
+        for c in range(2):
             quant_x(0, woven0[c][:], c)
-        gather(picked1[:, 1, :], 1, 1, 0, J)
-        for c in range(4):
+        gather(early1[:, 0, :], 1, 0, HALF, J)
+        gather(picked1[:, 1, :], 1, 1, 0, HALF)
+        for c in range(2):
             weave(woven1[c][:, :, 0:2], picked1[:, :, PAIR * c : PAIR * (c + 1)])
+        for c in (2, 3):
+            weave(woven1[c][:, :, 0:1], early1[:, :, PAIR * (c - 2) : PAIR * (c - 1)])
         late0 = keep.tile([P, 2, HALF], F32, name="late0")
         gather(late0[:, 0, :], 1, 2, 0, HALF)
         deal_wg(0)
@@ -309,29 +350,38 @@ def tile_list_relu_biasP_kernel(
         for hf in range(2):
             for t in range(PACK):
                 gate_pass(hf, t, 0, 1)
-        gate_relu(0, 0)
+            gate_relu(hf, 0)
         deal_words(wu_w[0][:], wu_raw[0][:])
-        late1 = keep.tile([P, 2, HALF], F32, name="late1", tag="wu_raw_0")
-        for t in (2, 3):
-            gather(late1[:, t - 2, :], 1, t, HALF, J)
+        late1 = keep.tile([P, 3, HALF], F32, name="late1", tag="wu_raw_0", align_bytes=64)
+        for t in (1, 2, 3):
+            gather(late1[:, t - 1, :], 1, t, HALF, J)
         deal_words(wu_w[1][:], wu_raw[1][:])
+        xq_tile(0, 1, "wu_raw_1")
         for c in (2, 3):
-            weave(woven1[c][:, :, 2:4], late1[:, :, PAIR * (c - 2) : PAIR * (c - 1)])
-        gate_relu(1, 0)
+            quant_x(0, woven0[c][:], c)
         for c in (2, 3):
-            quant_x(1, woven1[c][:], c)
+            weave(woven1[c][:, :, 1:4], late1[:, :, PAIR * (c - 2) : PAIR * (c - 1)])
         for hf in range(2):
             for jt in range(4):
-                unit(hf, jt, 2)
+                unit(hf, jt, 2, "woven1_%d" % (3 - hf) if jt == 2 else None)
+                if jt == 1 and hf == 0:
+                    for c in (2, 3):
+                        quant_x(1, woven1[c][:], c)
                 if jt == 2:
                     quant_h(hf, 0, 2)
             quant_h(hf, 2, 2)
+        nc.gpsimd.tensor_copy(
+            dsc[:].rearrange("p (t m) -> p t m", t=PACK), dsc_raw[:].rearrange("p (m t) -> p t m", t=PACK)
+        )
+        for a in range(PASSES):
+            nc.gpsimd.tensor_copy(wd_w[:, a, :, :], wd_raw[:, a, :].rearrange("p (m t) -> p t m", t=PACK))
+        for hf in range(2):
             gate_whole(hf, 1)
-        deal_words(wd_w[:], wd_raw[:])
+        for hf in range(2):
+            unit(hf, 4, 2)
         down(0, 4)
-        for jt in (4, 5):
-            for hf in range(2):
-                unit(hf, jt, 2)
+        for hf in range(2):
+            unit(hf, 5, 2)
         unit(0, 6, 1)
         quant_h(0, 4, 2)
         unit(1, 6, 1)
@@ -343,8 +393,8 @@ def tile_list_relu_biasP_kernel(
         quant_h(1, 6, 1)
         quant_h(0, 7, 1)
         quant_h(1, 7, 1)
-        down(6, 1)
-        down(7, 1)
+        down_tile(6)
+        down_tile(7)
         for q in range(4):
             eng = nc.sync if q % 2 == 0 else nc.scalar
             eng.dma_start(out_2[0, 4 * q : 4 * q + 4, :].bitcast(I32), y_sc[32 * q : 32 * q + 4, :].bitcast(I32))

@@ -52,7 +52,9 @@ def tile_list_relu_biasP_kernel(
                 x_plane[a, t] = keep.tile([P, T], F32, name="x_%d_%d" % (a, t))
         wgt_all = keep.tile([P, J], F32, name="wgt_all")
         wg_raw = [keep.tile([P, R // 2], I32, name="wg_raw_%d" % a) for a in range(PASSES)]
-        wu_raw = [keep.tile([P, PASSES, HALF], I32, name="wu_raw_%d" % hf, tag="wu_raw_%d" % hf, align_bytes=64) for hf in range(2)]
+        wu_raw_1 = keep.tile([P, PASSES, HALF], I32, name="wu_raw_1", tag="wu_raw_1", align_bytes=64)
+        wu_raw_0 = keep.tile([P, PASSES, HALF], I32, name="wu_raw_0")
+        wu_raw = [wu_raw_0[:], wu_raw_1[:]]
         wd_raw = keep.tile([P, PASSES, N], I32, name="wd_raw")
         sc_raw = keep.tile([P, R], U8, name="sc_raw")
         sc_dealt = keep.tile([P, R], U8, name="sc_dealt")
@@ -87,7 +89,10 @@ def tile_list_relu_biasP_kernel(
         def deal_narrow(dst, src):
             nc.vector.tensor_copy(dst, src.rearrange("p (g m t) -> p g t m", t=PACK, m=P))
 
-        deal_narrow(sc_dealt[:].rearrange("p (g t m) -> p g t m", t=PACK, m=P), sc_raw[:])
+        nc.gpsimd.tensor_copy(
+            sc_dealt[:].rearrange("p (g t m) -> p g t m", t=PACK, m=P),
+            sc_raw[:].rearrange("p (g m t) -> p g t m", t=PACK, m=P),
+        )
 
         def place_scales(k, width):
             home, row = sc_home[k]
@@ -102,7 +107,7 @@ def tile_list_relu_biasP_kernel(
 
         def load_wu(hf):
             nc.sync.dma_start(
-                wu_raw[hf][:],
+                wu_raw[hf],
                 wu_words[:, :, HALF * hf : HALF * (hf + 1), :].rearrange("a p r i -> p a (r i)").bitcast(I32),
             )
 
@@ -143,8 +148,7 @@ def tile_list_relu_biasP_kernel(
             deal_narrow(wg_w[a][:].bitcast(U16), wg_raw[a][:].bitcast(U16))
 
         picked0 = keep.tile([P, PACK, J], F32, name="picked0", tag="picked0")
-        picked1 = keep.tile([P, 2, HALF], F32, name="picked1")
-        early1 = keep.tile([P, 1, HALF], F32, name="early1")
+        picked1 = keep.tile([P, PACK + 1, HALF], F32, name="picked1")
         woven0 = [keep.tile([P, PAIR, PACK], BF16, name="woven0_%d" % c, align_bytes=64) for c in range(4)]
         woven1 = [
             keep.tile([P, PAIR, PACK], BF16, name="woven1_%d" % c, tag="woven1_%d" % c, align_bytes=64) for c in range(4)
@@ -210,9 +214,12 @@ def tile_list_relu_biasP_kernel(
         hs = [keep.tile([P, J], U8, name="hs_%d" % a, align_bytes=64) for a in range(PASSES)]
         h_woven = {}
 
-        def unit(hf, jt, tiles, tag=None):
+        up_sums = {}
+
+        def up_sum(hf, jt):
             cols = slice(P * jt, P * (jt + 1))
             ub = bank("ub")
+            up_sums[hf, jt] = ub
             for t in range(PACK):
                 for a in range(PASSES):
                     nc.tensor.matmul_mx(
@@ -224,6 +231,11 @@ def tile_list_relu_biasP_kernel(
                         start=(a == 0),
                         stop=(a == PASSES - 1),
                     )
+
+        def unit(hf, jt, tiles, tag=None):
+            if (hf, jt) not in up_sums:
+                up_sum(hf, jt)
+            ub = up_sums[hf, jt]
             first = jt - jt % tiles
             if tag is not None:
                 h_woven[hf, first] = keep.tile([P, P * tiles, PACK], BF16, name="hw", tag=tag, align_bytes=64)
@@ -279,31 +291,32 @@ def tile_list_relu_biasP_kernel(
             weave(woven[:], y)
             hand_out_planes(woven, cols)
 
-        def down_tile(jt):
+        def down_tile(jt, copies):
             cols = slice(P * jt, P * (jt + 1))
             y = y_all[:, PACK * P * jt : PACK * P * (jt + 1)].rearrange("p (t j) -> p t j", t=PACK)
-            acc = bank("acc")
+            accs = [bank("acc") for copy in range(copies)]
             for a in range(PASSES):
-                for t in range(PACK):
-                    nc.tensor.matmul_mx(
-                        out=acc[:, P * t : P * (t + 1)],
-                        lhsT=wd_w[:, a, t, :].bitcast(FP8X4),
-                        lhsT_scale=dsc[8 + 4 * a : P, P * t : P * (t + 1)],
-                        rhs=hq[a][:, cols].bitcast(FP8X4),
-                        rhs_scale=hs[a][:, cols],
-                        start=(a == 0 and t == 0),
-                        stop=(a == PASSES - 1 and t == PACK - 1),
-                    )
+                for acc in accs:
+                    for t in range(PACK):
+                        nc.tensor.matmul_mx(
+                            out=acc[:, P * t : P * (t + 1)],
+                            lhsT=wd_w[:, a, t, :].bitcast(FP8X4),
+                            lhsT_scale=dsc[8 + 4 * a : P, P * t : P * (t + 1)],
+                            rhs=hq[a][:, cols].bitcast(FP8X4),
+                            rhs_scale=hs[a][:, cols],
+                            start=(a == 0 and t == 0),
+                            stop=(a == PASSES - 1 and t == PACK - 1),
+                        )
             woven = ring.tile([P, P, PACK], BF16, name="yw", align_bytes=64)
             nc.vector.tensor_tensor(
-                woven[:].rearrange("p j t -> p j t"),
-                acc[:].rearrange("p (t j) -> p j t", t=PACK),
-                bias[:].unsqueeze(1).to_broadcast([P, P, PACK]),
+                woven[:].rearrange("p (c i) t -> p c t i", i=2),
+                accs[-1][:].rearrange("p (t c i) -> p c t i", t=PACK, i=2),
+                bias[:].unsqueeze(1).unsqueeze(3).to_broadcast([P, P // 2, PACK, 2]),
                 ADD,
             )
             hand_out_planes(woven, cols)
             for t in range(PACK):
-                nc.scalar.activation(y[:, t, :], acc[:, P * t : P * (t + 1)], ACT.Identity, bias=bias[:, t : t + 1])
+                nc.scalar.activation(y[:, t, :], accs[0][:, P * t : P * (t + 1)], ACT.Identity, bias=bias[:, t : t + 1])
             nc.sync.dma_start(out_rows[:, :, cols], y)
 
         def hand_out_planes(woven, cols):
@@ -319,31 +332,24 @@ def tile_list_relu_biasP_kernel(
         gather(picked0[:, 0, HALF:J], 0, 0, HALF, J)
         for t in range(1, PACK - 1):
             gather(picked0[:, t, :], 0, t, 0, J)
-        for c in range(4):
-            weave(woven0[c][:, :, 0:3], picked0[:, 0:3, PAIR * c : PAIR * (c + 1)])
         for jh in range(2):
             gather(picked0[:, 3, HALF * jh : HALF * (jh + 1)], 0, 3, HALF * jh, HALF * (jh + 1))
         for c in range(4):
-            weave(woven0[c][:, :, 3:4], picked0[:, 3:4, PAIR * c : PAIR * (c + 1)])
+            weave(woven0[c][:], picked0[:, :, PAIR * c : PAIR * (c + 1)])
         gather(picked1[:, 0, :], 1, 0, 0, HALF)
+        gather(picked1[:, PACK, :], 1, 0, HALF, J)
         for c in range(2):
             quant_x(0, woven0[c][:], c)
-        gather(early1[:, 0, :], 1, 0, HALF, J)
-        gather(picked1[:, 1, :], 1, 1, 0, HALF)
-        for c in range(2):
-            weave(woven1[c][:, :, 0:2], picked1[:, :, PAIR * c : PAIR * (c + 1)])
-        for c in (2, 3):
-            weave(woven1[c][:, :, 0:1], early1[:, :, PAIR * (c - 2) : PAIR * (c - 1)])
-        late0 = keep.tile([P, 2, HALF], F32, name="late0")
-        gather(late0[:, 0, :], 1, 2, 0, HALF)
+        for t in (1, 2):
+            gather(picked1[:, t, :], 1, t, 0, HALF)
         deal_wg(0)
         for hf in range(2):
             for t in range(PACK):
                 gate_pass(hf, t, 0, 0)
 
         for jt in range(4):
-            gather(late0[:, 1, P * jt : P * (jt + 1)], 1, 3, P * jt, P * (jt + 1))
-            weave(woven1[jt // 2][:, P * (jt % 2) : P * (jt % 2 + 1), 2:4], late0[:, :, P * jt : P * (jt + 1)])
+            gather(picked1[:, 3, P * jt : P * (jt + 1)], 1, 3, P * jt, P * (jt + 1))
+            weave(woven1[jt // 2][:, P * (jt % 2) : P * (jt % 2 + 1), :], picked1[:, 0:PACK, P * jt : P * (jt + 1)])
         deal_wg(1)
         for c in range(2):
             quant_x(1, woven1[c][:], c)
@@ -351,16 +357,15 @@ def tile_list_relu_biasP_kernel(
             for t in range(PACK):
                 gate_pass(hf, t, 0, 1)
             gate_relu(hf, 0)
-        deal_words(wu_w[0][:], wu_raw[0][:])
-        late1 = keep.tile([P, 3, HALF], F32, name="late1", tag="wu_raw_0", align_bytes=64)
+        deal_words(wu_w[0][:], wu_raw[0])
         for t in (1, 2, 3):
-            gather(late1[:, t - 1, :], 1, t, HALF, J)
-        deal_words(wu_w[1][:], wu_raw[1][:])
+            gather(picked1[:, PACK - t, :], 1, t, HALF, J)
+        deal_words(wu_w[1][:], wu_raw[1])
         xq_tile(0, 1, "wu_raw_1")
         for c in (2, 3):
             quant_x(0, woven0[c][:], c)
         for c in (2, 3):
-            weave(woven1[c][:, :, 1:4], late1[:, :, PAIR * (c - 2) : PAIR * (c - 1)])
+            weave(woven1[c][:], picked1[:, PACK:0:-1, PAIR * (c - 2) : PAIR * (c - 1)])
         for hf in range(2):
             for jt in range(4):
                 unit(hf, jt, 2, "woven1_%d" % (3 - hf) if jt == 2 else None)
@@ -393,8 +398,8 @@ def tile_list_relu_biasP_kernel(
         quant_h(1, 6, 1)
         quant_h(0, 7, 1)
         quant_h(1, 7, 1)
-        down_tile(6)
-        down_tile(7)
+        down_tile(6, 1)
+        down_tile(7, 2)
         for q in range(4):
             eng = nc.sync if q % 2 == 0 else nc.scalar
             eng.dma_start(out_2[0, 4 * q : 4 * q + 4, :].bitcast(I32), y_sc[32 * q : 32 * q + 4, :].bitcast(I32))

@@ -60,7 +60,6 @@ def tile_list_relu_biasP_kernel(
         sc_dealt = keep.tile([P, R], U8, name="sc_dealt")
         gsc = keep.tile([P, PASSES * R], U8, name="gsc", align_bytes=64)
         usc = keep.tile([P, PASSES * R], U8, name="usc", align_bytes=64)
-        dsc = keep.tile([P, N], U8, name="dsc", align_bytes=64)
         dsc_raw = keep.tile([P, N], U8, name="dsc_raw")
         sc_home = [(gsc, 0), (usc, 4)]
         nc.vector.memset(sc_raw[64:P, :].bitcast(I32), 0)
@@ -89,10 +88,7 @@ def tile_list_relu_biasP_kernel(
         def deal_narrow(dst, src):
             nc.vector.tensor_copy(dst, src.rearrange("p (g m t) -> p g t m", t=PACK, m=P))
 
-        nc.gpsimd.tensor_copy(
-            sc_dealt[:].rearrange("p (g t m) -> p g t m", t=PACK, m=P),
-            sc_raw[:].rearrange("p (g m t) -> p g t m", t=PACK, m=P),
-        )
+        deal_narrow(sc_dealt[:].rearrange("p (g t m) -> p g t m", t=PACK, m=P), sc_raw[:])
 
         def place_scales(k, width):
             home, row = sc_home[k]
@@ -133,7 +129,6 @@ def tile_list_relu_biasP_kernel(
 
         wg_w = [keep.tile([P, 2, PACK, 2 * P], U8, name="wg_%d" % a, align_bytes=64) for a in range(PASSES)]
         wu_w = [keep.tile([P, PASSES, PACK, P], I32, name="wu_%d" % hf, align_bytes=64) for hf in range(2)]
-        wd_w = keep.tile([P, PASSES, PACK, P], I32, name="wd_w", align_bytes=64)
 
         def plane(k, width, a, c0):
             home, row = sc_home[k]
@@ -200,7 +195,7 @@ def tile_list_relu_biasP_kernel(
         gate_rows = {}
 
         def gate_relu(hf, jh):
-            gate_rows[hf, jh] = keep.tile([P, PACK, HALF], F32, name="gate_%d_%d" % (hf, jh))
+            gate_rows[hf, jh] = keep.tile([P, PACK, HALF], F32, name="gate", tag="gate_%d_%d" % (hf, jh), align_bytes=64)
             for t in range(PACK):
                 nc.scalar.activation(gate_rows[hf, jh][:, t, :], gate_sums[hf, t, jh][:], ACT.Relu)
 
@@ -375,11 +370,12 @@ def tile_list_relu_biasP_kernel(
                 if jt == 2:
                     quant_h(hf, 0, 2)
             quant_h(hf, 2, 2)
-        nc.gpsimd.tensor_copy(
+        wd_w = keep.tile([P, PASSES, PACK, P], I32, name="wd_w", tag="gate_0_0", align_bytes=64)
+        deal_words(wd_w[:], wd_raw[:])
+        dsc = keep.tile([P, N], U8, name="dsc", tag="gate_1_0", align_bytes=64)
+        nc.vector.tensor_copy(
             dsc[:].rearrange("p (t m) -> p t m", t=PACK), dsc_raw[:].rearrange("p (m t) -> p t m", t=PACK)
         )
-        for a in range(PASSES):
-            nc.gpsimd.tensor_copy(wd_w[:, a, :, :], wd_raw[:, a, :].rearrange("p (m t) -> p t m", t=PACK))
         for hf in range(2):
             gate_whole(hf, 1)
         for hf in range(2):

@@ -77,12 +77,15 @@ def tile_list_relu_biasP_kernel(
         by_token = bank("by_token")
         nc.tensor.transpose(by_token[:, 0:P], wgt_rows[:], ident[:])
         per_tile = by_token[:, 0:64].rearrange("p (g jt) -> p jt g", g=8)
+        wide = keep.tile([P, 8, 8, 16], F32, name="wide")
+        nc.scalar.copy(wide[:, 0:2], per_tile[:, 0:2, :].unsqueeze(3).to_broadcast([P, 2, 8, 16]))
+        nc.vector.tensor_copy(wide[:, 2:8], per_tile[:, 2:8, :].unsqueeze(3).to_broadcast([P, 6, 8, 16]))
         for c in range(4):
-            wide = ring.tile([P, 2, 8, 16], F32, name="wide", bufs=4)
-            nc.vector.tensor_copy(wide[:], per_tile[:, 2 * c : 2 * c + 2, :].unsqueeze(3).to_broadcast([P, 2, 8, 16]))
             spread = bank("spread")
             for e in range(2):
-                nc.tensor.transpose(spread[:, P * e : P * (e + 1)], wide[:, e].rearrange("p g r -> p (g r)"), ident[:])
+                nc.tensor.transpose(
+                    spread[:, P * e : P * (e + 1)], wide[:, 2 * c + e].rearrange("p g r -> p (g r)"), ident[:]
+                )
             nc.scalar.copy(wgt_all[:, PAIR * c : PAIR * (c + 1)], spread[:, 0:PAIR])
 
         def deal_narrow(dst, src):
@@ -165,10 +168,13 @@ def tile_list_relu_biasP_kernel(
                 dst, x_plane[a, t][:].indirect(offsets[:, c0 // 16 : c1 // 16]), wgt_all[:, c0:c1], MULT
             )
 
-        def weave(dst, src):
+        def weave(dst, src, on_vector=False):
             dst = dst.rearrange("p (c i) t -> p c t i", i=4)
             src = src.rearrange("p t (c i) -> p c t i", i=4)
-            nc.scalar.activation(dst, src, ACT.Copy)
+            if on_vector:
+                nc.vector.tensor_copy(dst, src)
+            else:
+                nc.scalar.activation(dst, src, ACT.Copy)
 
         def quant_x(a, src, c):
             cols = slice(PAIR * c, PAIR * (c + 1))
@@ -258,7 +264,7 @@ def tile_list_relu_biasP_kernel(
         y_sc = keep.tile([P, J], U8, name="y_sc", align_bytes=64)
         y_all = keep.tile([P, PACK * J], F32, name="y_all", tag="picked0")
 
-        def down(jt0, tiles):
+        def down(jt0, tiles, on_vector):
             width = P * tiles
             per_bank = HALF // width
             cols = slice(P * jt0, P * jt0 + width)
@@ -283,7 +289,7 @@ def tile_list_relu_biasP_kernel(
                     )
             nc.sync.dma_start(out_rows[:, :, cols], y)
             woven = ring.tile([P, width, PACK], BF16, name="yw", align_bytes=64)
-            weave(woven[:], y)
+            weave(woven[:], y, on_vector)
             hand_out_planes(woven, cols)
 
         def down_tile(jt, copies):
@@ -359,8 +365,8 @@ def tile_list_relu_biasP_kernel(
         xq_tile(0, 1, "wu_raw_1")
         for c in (2, 3):
             quant_x(0, woven0[c][:], c)
-        for c in (2, 3):
-            weave(woven1[c][:], picked1[:, PACK:0:-1, PAIR * (c - 2) : PAIR * (c - 1)])
+        weave(woven1[2][:], picked1[:, PACK:0:-1, 0:PAIR])
+        weave(woven1[3][:], picked1[:, PACK:0:-1, PAIR:HALF])
         for hf in range(2):
             for jt in range(4):
                 unit(hf, jt, 2, "woven1_%d" % (3 - hf) if jt == 2 else None)
@@ -376,18 +382,20 @@ def tile_list_relu_biasP_kernel(
         nc.vector.tensor_copy(
             dsc[:].rearrange("p (t m) -> p t m", t=PACK), dsc_raw[:].rearrange("p (m t) -> p t m", t=PACK)
         )
+        for jt in (4, 5):
+            up_sum(0, jt)
         for hf in range(2):
             gate_whole(hf, 1)
         for hf in range(2):
-            unit(hf, 4, 2)
-        down(0, 4)
+            for jt in (4, 5):
+                unit(hf, jt, 2)
         for hf in range(2):
-            unit(hf, 5, 2)
+            quant_h(hf, 4, 2)
+        down(0, 2, True)
+        down(2, 2, False)
         unit(0, 6, 1)
-        quant_h(0, 4, 2)
         unit(1, 6, 1)
-        quant_h(1, 4, 2)
-        down(4, 2)
+        down(4, 2, False)
         unit(0, 7, 1)
         quant_h(0, 6, 1)
         unit(1, 7, 1)

@@ -147,7 +147,7 @@ def tile_list_relu_biasP_kernel(
 
         picked0 = keep.tile([P, PACK, J], F32, name="picked0", tag="picked0")
         picked1 = keep.tile([P, PACK + 1, HALF], F32, name="picked1")
-        woven0 = [keep.tile([P, PAIR, PACK], BF16, name="woven0_%d" % c, align_bytes=64) for c in range(4)]
+        woven0 = [keep.tile([P, HALF, PACK], BF16, name="woven0_%d" % jh, align_bytes=64) for jh in range(2)]
         woven1 = [
             keep.tile([P, PAIR, PACK], BF16, name="woven1_%d" % c, tag="woven1_%d" % c, align_bytes=64) for c in range(4)
         ]
@@ -176,8 +176,8 @@ def tile_list_relu_biasP_kernel(
             else:
                 nc.scalar.activation(dst, src, ACT.Copy)
 
-        def quant_x(a, src, c):
-            cols = slice(PAIR * c, PAIR * (c + 1))
+        def quant_x(a, src, c, pairs=1):
+            cols = slice(PAIR * c, PAIR * (c + pairs))
             nc.vector.quantize_mx(
                 out=xq(a, cols.start, cols.stop), scales=xs[a][:, cols], in_=src.rearrange("p j t -> p (j t)")
             )
@@ -261,7 +261,7 @@ def tile_list_relu_biasP_kernel(
 
         out_rows = out_0.rearrange("(p t) j -> p t j", t=PACK)
         out_words = out_1[0].rearrange("p j i -> p (j i)").bitcast(I32)
-        y_sc = keep.tile([P, J], U8, name="y_sc", align_bytes=64)
+        y_sc = keep.tile([P, PAIR], U8, name="y_sc", align_bytes=64)
         y_all = keep.tile([P, PACK * J], F32, name="y_all", tag="picked0")
 
         def down(jt0, tiles, on_vector):
@@ -297,7 +297,7 @@ def tile_list_relu_biasP_kernel(
             y = y_all[:, PACK * P * jt : PACK * P * (jt + 1)].rearrange("p (t j) -> p t j", t=PACK)
             accs = [bank("acc") for copy in range(copies)]
             for a in range(PASSES):
-                for acc in accs:
+                for acc in reversed(accs):
                     for t in range(PACK):
                         nc.tensor.matmul_mx(
                             out=acc[:, P * t : P * (t + 1)],
@@ -324,7 +324,9 @@ def tile_list_relu_biasP_kernel(
             width = cols.stop - cols.start
             yq = ring.tile([P, width], I32, name="yq", align_bytes=64)
             nc.vector.quantize_mx(
-                out=yq[:].bitcast(FP8X4), scales=y_sc[:, cols], in_=woven[:].rearrange("p j t -> p (j t)")
+                out=yq[:].bitcast(FP8X4),
+                scales=y_sc[4 * (cols.start // PAIR) : P, cols.start % PAIR : cols.start % PAIR + width],
+                in_=woven[:].rearrange("p j t -> p (j t)"),
             )
             nc.sync.dma_start(out_words[:, cols], yq[:])
 
@@ -335,12 +337,11 @@ def tile_list_relu_biasP_kernel(
             gather(picked0[:, t, :], 0, t, 0, J)
         for jh in range(2):
             gather(picked0[:, 3, HALF * jh : HALF * (jh + 1)], 0, 3, HALF * jh, HALF * (jh + 1))
-        for c in range(4):
-            weave(woven0[c][:], picked0[:, :, PAIR * c : PAIR * (c + 1)])
+        for jh in range(2):
+            weave(woven0[jh][:], picked0[:, :, HALF * jh : HALF * (jh + 1)])
         gather(picked1[:, 0, :], 1, 0, 0, HALF)
         gather(picked1[:, PACK, :], 1, 0, HALF, J)
-        for c in range(2):
-            quant_x(0, woven0[c][:], c)
+        quant_x(0, woven0[0][:], 0, 2)
         for t in (1, 2):
             gather(picked1[:, t, :], 1, t, 0, HALF)
         deal_wg(0)
@@ -350,10 +351,15 @@ def tile_list_relu_biasP_kernel(
 
         for jt in range(4):
             gather(picked1[:, 3, P * jt : P * (jt + 1)], 1, 3, P * jt, P * (jt + 1))
-            weave(woven1[jt // 2][:, P * (jt % 2) : P * (jt % 2 + 1), :], picked1[:, 0:PACK, P * jt : P * (jt + 1)])
-        deal_wg(1)
+            weave(
+                woven1[jt // 2][:, P * (jt % 2) : P * (jt % 2 + 1), :],
+                picked1[:, 0:PACK, P * jt : P * (jt + 1)],
+                on_vector=jt == 3,
+            )
+        deal_narrow(wg_w[1][:, 0:1].bitcast(U16), wg_raw[1][:, 0:PAIR].bitcast(U16))
         for c in range(2):
             quant_x(1, woven1[c][:], c)
+        deal_narrow(wg_w[1][:, 1:2].bitcast(U16), wg_raw[1][:, PAIR:HALF].bitcast(U16))
         for hf in range(2):
             for t in range(PACK):
                 gate_pass(hf, t, 0, 1)
@@ -363,8 +369,7 @@ def tile_list_relu_biasP_kernel(
             gather(picked1[:, PACK - t, :], 1, t, HALF, J)
         deal_words(wu_w[1][:], wu_raw[1])
         xq_tile(0, 1, "wu_raw_1")
-        for c in (2, 3):
-            quant_x(0, woven0[c][:], c)
+        quant_x(0, woven0[1][:], 2, 2)
         weave(woven1[2][:], picked1[:, PACK:0:-1, 0:PAIR])
         weave(woven1[3][:], picked1[:, PACK:0:-1, PAIR:HALF])
         for hf in range(2):
@@ -402,8 +407,11 @@ def tile_list_relu_biasP_kernel(
         quant_h(1, 6, 1)
         quant_h(0, 7, 1)
         quant_h(1, 7, 1)
-        down_tile(6, 1)
+        down(6, 1, True)
         down_tile(7, 2)
         for q in range(4):
             eng = nc.sync if q % 2 == 0 else nc.scalar
-            eng.dma_start(out_2[0, 4 * q : 4 * q + 4, :].bitcast(I32), y_sc[32 * q : 32 * q + 4, :].bitcast(I32))
+            eng.dma_start(
+                out_2[0, 4 * q : 4 * q + 4, :].rearrange("r (c j) -> c r j", j=PAIR).bitcast(I32),
+                y_sc[32 * q : 32 * q + 16, :].bitcast(I32),
+            )

@@ -139,7 +139,7 @@ def tile_list_relu_biasP_kernel(
 
         def deal_words(dst, src):
             nc.vector.tensor_copy(
-                dst.rearrange("p a t (c i) -> p a c t i", i=4), src.rearrange("p a (c i t) -> p a c t i", i=4, t=PACK)
+                dst.rearrange("p a t (c i) -> p a c t i", i=2), src.rearrange("p a (c i t) -> p a c t i", i=2, t=PACK)
             )
 
         def deal_wg(a):
@@ -245,9 +245,9 @@ def tile_list_relu_biasP_kernel(
             woven = h_woven[hf, first]
             c0 = P * (jt % 4)
             nc.vector.tensor_tensor(
-                woven[:, P * (jt - first) : P * (jt - first + 1), :].rearrange("p (c i) t -> p c t i", i=2),
-                ub[:].rearrange("p (t c i) -> p c t i", t=PACK, i=2),
-                gate_rows[hf, jt // 4][:, :, c0 : c0 + P].rearrange("p t (c i) -> p c t i", i=2),
+                woven[:, P * (jt - first) : P * (jt - first + 1), :].rearrange("p (c i) t -> p c t i", i=4),
+                ub[:].rearrange("p (t c i) -> p c t i", t=PACK, i=4),
+                gate_rows[hf, jt // 4][:, :, c0 : c0 + P].rearrange("p t (c i) -> p c t i", i=4),
                 MULT,
             )
 
@@ -310,9 +310,9 @@ def tile_list_relu_biasP_kernel(
                         )
             woven = ring.tile([P, P, PACK], BF16, name="yw", align_bytes=64)
             nc.vector.tensor_tensor(
-                woven[:].rearrange("p (c i) t -> p c t i", i=2),
-                accs[-1][:].rearrange("p (t c i) -> p c t i", t=PACK, i=2),
-                bias[:].unsqueeze(1).unsqueeze(3).to_broadcast([P, P // 2, PACK, 2]),
+                woven[:].rearrange("p (c i) t -> p c t i", i=4),
+                accs[-1][:].rearrange("p (t c i) -> p c t i", t=PACK, i=4),
+                bias[:].unsqueeze(1).unsqueeze(3).to_broadcast([P, P // 4, PACK, 4]),
                 ADD,
             )
             hand_out_planes(woven, cols)

@@ -342,8 +342,10 @@ def tile_list_relu_biasP_kernel(
         gather(picked1[:, 0, :], 1, 0, 0, HALF)
         gather(picked1[:, PACK, :], 1, 0, HALF, J)
         quant_x(0, woven0[0][:], 0, 2)
+        xq_tile(0, 1, "xq_0_1")
         for t in (1, 2):
             gather(picked1[:, t, :], 1, t, 0, HALF)
+        quant_x(0, woven0[1][:], 2, 2)
         deal_wg(0)
         for hf in range(2):
             for t in range(PACK):
@@ -368,8 +370,6 @@ def tile_list_relu_biasP_kernel(
         for t in (1, 2, 3):
             gather(picked1[:, PACK - t, :], 1, t, HALF, J)
         deal_words(wu_w[1][:], wu_raw[1])
-        xq_tile(0, 1, "wu_raw_1")
-        quant_x(0, woven0[1][:], 2, 2)
         weave(woven1[2][:], picked1[:, PACK:0:-1, 0:PAIR])
         weave(woven1[3][:], picked1[:, PACK:0:-1, PAIR:HALF])
         for hf in range(2):
@@ -410,8 +410,7 @@ def tile_list_relu_biasP_kernel(
         down(6, 1, True)
         down_tile(7, 2)
         for q in range(4):
-            eng = nc.sync if q % 2 == 0 else nc.scalar
-            eng.dma_start(
+            nc.sync.dma_start(
                 out_2[0, 4 * q : 4 * q + 4, :].rearrange("r (c j) -> c r j", j=PAIR).bitcast(I32),
                 y_sc[32 * q : 32 * q + 16, :].bitcast(I32),
             )

@@ -31,16 +31,18 @@ def tile_list_relu_biasP_kernel(
     nc = tc.nc
     with ExitStack() as ctx:
         keep = ctx.enter_context(tc.tile_pool(name="keep", bufs=1))
+        shared = ctx.enter_context(tc.tile_pool(name="shared", bufs=1))
         ring = ctx.enter_context(tc.tile_pool(name="ring", bufs=3))
-        psum = ctx.enter_context(tc.psum_pool(name="psum", bufs=8))
+        psum = ctx.enter_context(tc.psum_pool(name="psum", bufs=1))
 
         offsets = keep.tile([P, J // 16], U16, name="offsets")
-        nc.sync.dma_start(offsets[:], offs)
-
         wgt_rows = keep.tile([P, P], F32, name="wgt_rows")
+        wg_raw = [keep.tile([P, R // 2], I32, name="wg_raw_%d" % a) for a in range(PASSES)]
         nc.sync.dma_start(
             wgt_rows[0:64, :], wgt.rearrange("(g r) (jt s) -> r g jt s", r=16, s=P)[0]
         )
+        nc.sync.dma_start(wg_raw[0][:], wg_words[0].bitcast(I32))
+        nc.sync.dma_start(offsets[:], offs)
         nc.vector.memset(wgt_rows[64:P, :], 0.0)
         ident = keep.tile([P, P], F32, name="ident")
         make_identity(nc, ident[:])
@@ -51,10 +53,7 @@ def tile_list_relu_biasP_kernel(
             for t in range(PACK):
                 x_plane[a, t] = keep.tile([P, T], F32, name="x_%d_%d" % (a, t))
         wgt_all = keep.tile([P, J], F32, name="wgt_all")
-        wg_raw = [keep.tile([P, R // 2], I32, name="wg_raw_%d" % a) for a in range(PASSES)]
-        wu_raw_1 = keep.tile([P, PASSES, HALF], I32, name="wu_raw_1", tag="wu_raw_1", align_bytes=64)
-        wu_raw_0 = keep.tile([P, PASSES, HALF], I32, name="wu_raw_0")
-        wu_raw = [wu_raw_0[:], wu_raw_1[:]]
+        wu_raw = [keep.tile([P, PASSES, HALF], I32, name="wu_raw_%d" % hf) for hf in range(2)]
         wd_raw = keep.tile([P, PASSES, N], I32, name="wd_raw")
         sc_raw = keep.tile([P, R], U8, name="sc_raw")
         sc_dealt = keep.tile([P, R], U8, name="sc_dealt")
@@ -71,17 +70,18 @@ def tile_list_relu_biasP_kernel(
                 sc_raw[32 * k : 32 * (k + 1), :].bitcast(I32), scales.rearrange("a q r -> q a r").bitcast(I32)
             )
 
-        def bank(name):
-            return psum.tile([P, HALF], F32, name=name, tag="bank")
+        def bank(name, number):
+            return psum.tile([P, HALF], F32, name=name, tag="bank_%d" % number)
 
-        by_token = bank("by_token")
+        by_token = bank("by_token", 0)
         nc.tensor.transpose(by_token[:, 0:P], wgt_rows[:], ident[:])
         per_tile = by_token[:, 0:64].rearrange("p (g jt) -> p jt g", g=8)
         wide = keep.tile([P, 8, 8, 16], F32, name="wide")
-        nc.scalar.copy(wide[:, 0:2], per_tile[:, 0:2, :].unsqueeze(3).to_broadcast([P, 2, 8, 16]))
-        nc.vector.tensor_copy(wide[:, 2:8], per_tile[:, 2:8, :].unsqueeze(3).to_broadcast([P, 6, 8, 16]))
         for c in range(4):
-            spread = bank("spread")
+            nc.scalar.copy(
+                wide[:, 2 * c : 2 * c + 2], per_tile[:, 2 * c : 2 * c + 2, :].unsqueeze(3).to_broadcast([P, 2, 8, 16])
+            )
+            spread = bank("spread", 1 + c)
             for e in range(2):
                 nc.tensor.transpose(
                     spread[:, P * e : P * (e + 1)], wide[:, 2 * c + e].rearrange("p g r -> p (g r)"), ident[:]
@@ -106,22 +106,22 @@ def tile_list_relu_biasP_kernel(
 
         def load_wu(hf):
             nc.sync.dma_start(
-                wu_raw[hf],
+                wu_raw[hf][:],
                 wu_words[:, :, HALF * hf : HALF * (hf + 1), :].rearrange("a p r i -> p a (r i)").bitcast(I32),
             )
 
         load_x(0, 0)
-        place_scales(0, R)
         for t in range(1, PACK):
             load_x(0, t)
-        for t in range(PACK - 1):
-            load_x(1, t)
-        nc.sync.dma_start(wg_raw[0][:], wg_words[0].bitcast(I32))
-        load_x(1, PACK - 1)
+        load_x(1, 0)
+        load_x(1, 1)
+        load_x(1, 2)
+        place_scales(0, R)
+        load_x(1, 3)
         nc.sync.dma_start(wg_raw[1][:], wg_words[1].bitcast(I32))
         load_wu(0)
-        place_scales(1, R)
         load_wu(1)
+        place_scales(1, R)
         nc.sync.dma_start(wd_raw[:], wd_words.rearrange("a p n i -> p a (n i)").bitcast(I32))
         for q in range(4):
             nc.sync.dma_start(
@@ -142,15 +142,10 @@ def tile_list_relu_biasP_kernel(
                 dst.rearrange("p a t (c i) -> p a c t i", i=2), src.rearrange("p a (c i t) -> p a c t i", i=2, t=PACK)
             )
 
-        def deal_wg(a):
-            deal_narrow(wg_w[a][:].bitcast(U16), wg_raw[a][:].bitcast(U16))
-
         picked0 = keep.tile([P, PACK, J], F32, name="picked0", tag="picked0")
-        picked1 = keep.tile([P, PACK + 1, HALF], F32, name="picked1")
+        picked1 = shared.tile([P, PACK, HALF], F32, name="picked1", offset=0, align_bytes=64)
         woven0 = [keep.tile([P, HALF, PACK], BF16, name="woven0_%d" % jh, align_bytes=64) for jh in range(2)]
-        woven1 = [
-            keep.tile([P, PAIR, PACK], BF16, name="woven1_%d" % c, tag="woven1_%d" % c, align_bytes=64) for c in range(4)
-        ]
+        woven1 = keep.tile([P, J, PACK], BF16, name="woven1", align_bytes=64)
         xq_half = {}
 
         def xq_tile(a, jh, tag):
@@ -168,6 +163,9 @@ def tile_list_relu_biasP_kernel(
                 dst, x_plane[a, t][:].indirect(offsets[:, c0 // 16 : c1 // 16]), wgt_all[:, c0:c1], MULT
             )
 
+        def gather1(t, c0, c1):
+            gather(picked1[:, t, c0 % HALF : c0 % HALF + c1 - c0], 1, t, c0, c1)
+
         def weave(dst, src, on_vector=False):
             dst = dst.rearrange("p (c i) t -> p c t i", i=4)
             src = src.rearrange("p t (c i) -> p c t i", i=4)
@@ -176,160 +174,172 @@ def tile_list_relu_biasP_kernel(
             else:
                 nc.scalar.activation(dst, src, ACT.Copy)
 
-        def quant_x(a, src, c, pairs=1):
-            cols = slice(PAIR * c, PAIR * (c + pairs))
-            nc.vector.quantize_mx(
-                out=xq(a, cols.start, cols.stop), scales=xs[a][:, cols], in_=src.rearrange("p j t -> p (j t)")
-            )
+        def weave1(c0, c1):
+            weave(woven1[:, c0:c1, :], picked1[:, :, c0 % HALF : c0 % HALF + c1 - c0])
 
-        gate_sums = {}
+        def quant_x(a, src, c0, c1):
+            nc.vector.quantize_mx(out=xq(a, c0, c1), scales=xs[a][:, c0:c1], in_=src.rearrange("p j t -> p (j t)"))
 
-        def gate_pass(hf, t, jh, a):
-            cols = slice(HALF * jh, HALF * (jh + 1))
-            if a == 0:
-                gate_sums[hf, t, jh] = bank("ga")
+        def quant1(c0, c1):
+            quant_x(1, woven1[:, c0:c1, :], c0, c1)
+
+        def gate_pass(out, hf, t, a, c0, c1, start, stop):
             nc.tensor.matmul_mx(
-                out=gate_sums[hf, t, jh][:],
+                out=out,
                 lhsT=wg_w[a][:, hf, t, :].bitcast(FP4X4),
                 lhsT_scale=plane(0, R, a, HALF * hf + P * t),
-                rhs=xq(a, cols.start, cols.stop),
-                rhs_scale=xs[a][:, cols],
-                start=(a == 0),
-                stop=(a == PASSES - 1),
+                rhs=xq(a, c0, c1),
+                rhs_scale=xs[a][:, c0:c1],
+                start=start,
+                stop=stop,
             )
 
+        gate_banks = {}
         gate_rows = {}
 
-        def gate_relu(hf, jh):
-            gate_rows[hf, jh] = keep.tile([P, PACK, HALF], F32, name="gate", tag="gate_%d_%d" % (hf, jh), align_bytes=64)
+        def gate_tile(hf, jt, a):
+            if a == 0:
+                gate_banks[hf, jt] = bank("ga", 2 * jt + hf)
             for t in range(PACK):
-                nc.scalar.activation(gate_rows[hf, jh][:, t, :], gate_sums[hf, t, jh][:], ACT.Relu)
+                gate_pass(
+                    gate_banks[hf, jt][:, P * t : P * (t + 1)], hf, t, a, P * jt, P * (jt + 1),
+                    a == 0 and t == 0, a == PASSES - 1 and t == PACK - 1,
+                )
 
-        def gate_whole(hf, jh):
+        def relu_tile(hf, jt):
+            rows = keep.tile([P, PACK, P], F32, name="gate_%d_%d" % (hf, jt))
+            nc.scalar.activation(rows[:].rearrange("p t j -> p (t j)"), gate_banks[hf, jt][:], ACT.Relu)
+            gate_rows[hf, jt] = rows[:]
+
+        def gate_half(hf):
+            rows = keep.tile([P, PACK, HALF], F32, name="gate_late_%d" % hf)
             for t in range(PACK):
-                for a in range(PASSES):
-                    gate_pass(hf, t, jh, a)
-            gate_relu(hf, jh)
+                sums = bank("ga", 1 + (PACK * hf + t) % 3)
+                for a in reversed(range(PASSES)):
+                    gate_pass(sums[:], hf, t, a, HALF, J, a == PASSES - 1, a == 0)
+                nc.scalar.activation(rows[:, t, :], sums[:], ACT.Relu)
+            for jt in range(4, 8):
+                gate_rows[hf, jt] = rows[:, :, P * (jt - 4) : P * (jt - 3)]
 
-        hq = [keep.tile([P, J], I32, name="hq_%d" % a, align_bytes=64) for a in range(PASSES)]
+        hq = {}
         hs = [keep.tile([P, J], U8, name="hs_%d" % a, align_bytes=64) for a in range(PASSES)]
         h_woven = {}
-
         up_sums = {}
 
-        def up_sum(hf, jt):
+        def up_sum(hf, jt, number):
             cols = slice(P * jt, P * (jt + 1))
-            ub = bank("ub")
+            ub = bank("ub", number)
             up_sums[hf, jt] = ub
             for t in range(PACK):
-                for a in range(PASSES):
+                for a in reversed(range(PASSES)):
                     nc.tensor.matmul_mx(
                         out=ub[:, P * t : P * (t + 1)],
                         lhsT=wu_w[hf][:, a, t, :].bitcast(FP8X4),
                         lhsT_scale=plane(1, R, a, HALF * hf + P * t),
                         rhs=xq(a, cols.start, cols.stop),
                         rhs_scale=xs[a][:, cols],
-                        start=(a == 0),
-                        stop=(a == PASSES - 1),
+                        start=(a == PASSES - 1),
+                        stop=(a == 0),
                     )
 
-        def unit(hf, jt, tiles, tag=None):
-            if (hf, jt) not in up_sums:
-                up_sum(hf, jt)
-            ub = up_sums[hf, jt]
+        def late_tile(shape, dtype, name, offset):
+            if offset is None:
+                return keep.tile(shape, dtype, name=name, align_bytes=64)
+            return shared.tile(shape, dtype, name=name, offset=offset, align_bytes=64)
+
+        def product(hf, jt, tiles, offset=None):
             first = jt - jt % tiles
-            if tag is not None:
-                h_woven[hf, first] = keep.tile([P, P * tiles, PACK], BF16, name="hw", tag=tag, align_bytes=64)
-            elif jt == first:
-                h_woven[hf, first] = ring.tile([P, P * tiles, PACK], BF16, name="hw", bufs=4, align_bytes=64)
-            woven = h_woven[hf, first]
-            c0 = P * (jt % 4)
+            if (hf, first) not in h_woven:
+                h_woven[hf, first] = late_tile([P, P * tiles, PACK], BF16, "hw_%d_%d" % (hf, jt), offset)[:]
             nc.vector.tensor_tensor(
-                woven[:, P * (jt - first) : P * (jt - first + 1), :].rearrange("p (c i) t -> p c t i", i=4),
-                ub[:].rearrange("p (t c i) -> p c t i", t=PACK, i=4),
-                gate_rows[hf, jt // 4][:, :, c0 : c0 + P].rearrange("p t (c i) -> p c t i", i=4),
+                h_woven[hf, first][:, P * (jt - first) : P * (jt - first + 1), :].rearrange("p (c i) t -> p c t i", i=4),
+                up_sums[hf, jt][:].rearrange("p (t c i) -> p c t i", t=PACK, i=4),
+                gate_rows[hf, jt].rearrange("p t (c i) -> p c t i", i=4),
                 MULT,
             )
 
-        def quant_h(hf, first, tiles):
+        def quant_h(hf, first, tiles, offset=None):
             cols = slice(P * first, P * (first + tiles))
+            hq[hf, first] = late_tile([P, P * tiles], I32, "hq_%d_%d" % (hf, first), offset)
             nc.vector.quantize_mx(
-                out=hq[hf][:, cols].bitcast(FP8X4),
+                out=hq[hf, first][:].bitcast(FP8X4),
                 scales=hs[hf][:, cols],
-                in_=h_woven[hf, first][:].rearrange("p j t -> p (j t)"),
+                in_=h_woven[hf, first].rearrange("p j t -> p (j t)"),
             )
 
         out_rows = out_0.rearrange("(p t) j -> p t j", t=PACK)
         out_words = out_1[0].rearrange("p j i -> p (j i)").bitcast(I32)
         y_sc = keep.tile([P, PAIR], U8, name="y_sc", align_bytes=64)
         y_all = keep.tile([P, PACK * J], F32, name="y_all", tag="picked0")
+        y_woven = {}
 
-        def down(jt0, tiles, on_vector):
+        def y_rows(jt0, tiles):
+            return y_all[:, PACK * P * jt0 : PACK * P * (jt0 + tiles)].rearrange("p (t j) -> p t j", t=PACK)
+
+        def down_pass(out, a, t, jt0, tiles, start, stop):
+            nc.tensor.matmul_mx(
+                out=out,
+                lhsT=wd_w[:, a, t, :].bitcast(FP8X4),
+                lhsT_scale=dsc[8 + 4 * a : P, P * t : P * (t + 1)],
+                rhs=hq[a, jt0][:].bitcast(FP8X4),
+                rhs_scale=hs[a][:, P * jt0 : P * (jt0 + tiles)],
+                start=start,
+                stop=stop,
+            )
+
+        def down(jt0, tiles, number):
             width = P * tiles
             per_bank = HALF // width
-            cols = slice(P * jt0, P * jt0 + width)
-            y = y_all[:, PACK * P * jt0 : PACK * (P * jt0 + width)].rearrange("p (t j) -> p t j", t=PACK)
+            y = y_rows(jt0, tiles)
             for t0 in range(0, PACK, per_bank):
-                acc = bank("acc")
+                acc = bank("acc", number + t0 // per_bank)
                 for e in range(per_bank):
                     for a in range(PASSES):
-                        nc.tensor.matmul_mx(
-                            out=acc[:, width * e : width * (e + 1)],
-                            lhsT=wd_w[:, a, t0 + e, :].bitcast(FP8X4),
-                            lhsT_scale=dsc[8 + 4 * a : P, P * (t0 + e) : P * (t0 + e + 1)],
-                            rhs=hq[a][:, cols].bitcast(FP8X4),
-                            rhs_scale=hs[a][:, cols],
-                            start=(a == 0),
-                            stop=(a == PASSES - 1),
-                        )
+                        down_pass(acc[:, width * e : width * (e + 1)], a, t0 + e, jt0, tiles, a == 0, a == PASSES - 1)
                 for e in range(per_bank):
                     t = t0 + e
                     nc.scalar.activation(
                         y[:, t, :], acc[:, width * e : width * (e + 1)], ACT.Identity, bias=bias[:, t : t + 1]
                     )
-            nc.sync.dma_start(out_rows[:, :, cols], y)
-            woven = ring.tile([P, width, PACK], BF16, name="yw", align_bytes=64)
-            weave(woven[:], y, on_vector)
-            hand_out_planes(woven, cols)
+            nc.sync.dma_start(out_rows[:, :, P * jt0 : P * jt0 + width], y)
 
-        def down_tile(jt, copies):
-            cols = slice(P * jt, P * (jt + 1))
-            y = y_all[:, PACK * P * jt : PACK * P * (jt + 1)].rearrange("p (t j) -> p t j", t=PACK)
-            accs = [bank("acc") for copy in range(copies)]
-            for a in range(PASSES):
-                for acc in reversed(accs):
-                    for t in range(PACK):
-                        nc.tensor.matmul_mx(
-                            out=acc[:, P * t : P * (t + 1)],
-                            lhsT=wd_w[:, a, t, :].bitcast(FP8X4),
-                            lhsT_scale=dsc[8 + 4 * a : P, P * t : P * (t + 1)],
-                            rhs=hq[a][:, cols].bitcast(FP8X4),
-                            rhs_scale=hs[a][:, cols],
-                            start=(a == 0 and t == 0),
-                            stop=(a == PASSES - 1 and t == PACK - 1),
-                        )
-            woven = ring.tile([P, P, PACK], BF16, name="yw", align_bytes=64)
-            nc.vector.tensor_tensor(
-                woven[:].rearrange("p (c i) t -> p c t i", i=4),
-                accs[-1][:].rearrange("p (t c i) -> p c t i", t=PACK, i=4),
-                bias[:].unsqueeze(1).unsqueeze(3).to_broadcast([P, P // 4, PACK, 4]),
-                ADD,
-            )
-            hand_out_planes(woven, cols)
-            for t in range(PACK):
-                nc.scalar.activation(y[:, t, :], accs[0][:, P * t : P * (t + 1)], ACT.Identity, bias=bias[:, t : t + 1])
-            nc.sync.dma_start(out_rows[:, :, cols], y)
+        def weave_y(jt0, tiles, on_vector):
+            y_woven[jt0] = ring.tile([P, P * tiles, PACK], BF16, name="yw", align_bytes=64)
+            weave(y_woven[jt0][:], y_rows(jt0, tiles), on_vector)
 
-        def hand_out_planes(woven, cols):
-            width = cols.stop - cols.start
+        def hand_out_planes(jt0, tiles):
+            c0, width = P * jt0, P * tiles
             yq = ring.tile([P, width], I32, name="yq", align_bytes=64)
             nc.vector.quantize_mx(
                 out=yq[:].bitcast(FP8X4),
-                scales=y_sc[4 * (cols.start // PAIR) : P, cols.start % PAIR : cols.start % PAIR + width],
-                in_=woven[:].rearrange("p j t -> p (j t)"),
+                scales=y_sc[4 * (c0 // PAIR) : P, c0 % PAIR : c0 % PAIR + width],
+                in_=y_woven[jt0][:].rearrange("p j t -> p (j t)"),
             )
-            nc.sync.dma_start(out_words[:, cols], yq[:])
+            nc.sync.dma_start(out_words[:, c0 : c0 + width], yq[:])
 
+        def down_last(jt, numbers):
+            y = y_rows(jt, 1)
+            accs = [bank("acc", number) for number in numbers]
+            for a in range(PASSES):
+                for acc in accs:
+                    for t in range(PACK):
+                        down_pass(
+                            acc[:, P * t : P * (t + 1)], a, t, jt, 1,
+                            a == 0 and t == 0, a == PASSES - 1 and t == PACK - 1,
+                        )
+            y_woven[jt] = ring.tile([P, P, PACK], BF16, name="yw", align_bytes=64)
+            nc.vector.tensor_tensor(
+                y_woven[jt][:].rearrange("p (c i) t -> p c t i", i=4),
+                accs[0][:].rearrange("p (t c i) -> p c t i", t=PACK, i=4),
+                bias[:].unsqueeze(1).unsqueeze(3).to_broadcast([P, P // 4, PACK, 4]),
+                ADD,
+            )
+            hand_out_planes(jt, 1)
+            for t in range(PACK):
+                nc.scalar.activation(y[:, t, :], accs[1][:, P * t : P * (t + 1)], ACT.Identity, bias=bias[:, t : t + 1])
+            nc.sync.dma_start(out_rows[:, :, P * jt : P * (jt + 1)], y)
+
+        deal_narrow(wg_w[0][:].bitcast(U16), wg_raw[0][:].bitcast(U16))
         gather(picked0[:, 0, 0:HEAD], 0, 0, 0, HEAD)
         gather(picked0[:, 0, HEAD:HALF], 0, 0, HEAD, HALF)
         gather(picked0[:, 0, HALF:J], 0, 0, HALF, J)
@@ -339,76 +349,99 @@ def tile_list_relu_biasP_kernel(
             gather(picked0[:, 3, HALF * jh : HALF * (jh + 1)], 0, 3, HALF * jh, HALF * (jh + 1))
         for jh in range(2):
             weave(woven0[jh][:], picked0[:, :, HALF * jh : HALF * (jh + 1)])
-        gather(picked1[:, 0, :], 1, 0, 0, HALF)
-        gather(picked1[:, PACK, :], 1, 0, HALF, J)
-        quant_x(0, woven0[0][:], 0, 2)
+        gather1(0, 0, HALF)
+        quant_x(0, woven0[0][:], 0, HALF)
+        gather1(1, 0, HALF)
         xq_tile(0, 1, "xq_0_1")
-        for t in (1, 2):
-            gather(picked1[:, t, :], 1, t, 0, HALF)
-        quant_x(0, woven0[1][:], 2, 2)
-        deal_wg(0)
-        for hf in range(2):
-            for t in range(PACK):
-                gate_pass(hf, t, 0, 0)
+        quant_x(0, woven0[1][:], HALF, J)
+        gather1(2, 0, HALF)
+        for jt in range(4):
+            for hf in range(2):
+                gate_tile(hf, jt, 0)
 
         for jt in range(4):
-            gather(picked1[:, 3, P * jt : P * (jt + 1)], 1, 3, P * jt, P * (jt + 1))
-            weave(
-                woven1[jt // 2][:, P * (jt % 2) : P * (jt % 2 + 1), :],
-                picked1[:, 0:PACK, P * jt : P * (jt + 1)],
-                on_vector=jt == 3,
-            )
-        deal_narrow(wg_w[1][:, 0:1].bitcast(U16), wg_raw[1][:, 0:PAIR].bitcast(U16))
-        for c in range(2):
-            quant_x(1, woven1[c][:], c)
-        deal_narrow(wg_w[1][:, 1:2].bitcast(U16), wg_raw[1][:, PAIR:HALF].bitcast(U16))
+            gather1(3, P * jt, P * (jt + 1))
+            weave1(P * jt, P * (jt + 1))
         for hf in range(2):
-            for t in range(PACK):
-                gate_pass(hf, t, 0, 1)
-            gate_relu(hf, 0)
-        deal_words(wu_w[0][:], wu_raw[0])
-        for t in (1, 2, 3):
-            gather(picked1[:, PACK - t, :], 1, t, HALF, J)
-        deal_words(wu_w[1][:], wu_raw[1])
-        weave(woven1[2][:], picked1[:, PACK:0:-1, 0:PAIR])
-        weave(woven1[3][:], picked1[:, PACK:0:-1, PAIR:HALF])
+            deal_narrow(wg_w[1][:, hf : hf + 1].bitcast(U16), wg_raw[1][:, PAIR * hf : PAIR * (hf + 1)].bitcast(U16))
+            quant1(P * hf, P * (hf + 1))
+        quant1(2 * P, 3 * P)
+        deal_words(wu_w[0][:], wu_raw[0][:])
+        quant1(3 * P, 4 * P)
+        for jt in range(4):
+            for hf in range(2):
+                gate_tile(hf, jt, 1)
+                relu_tile(hf, jt)
+
+        gather1(0, HALF, J)
+        deal_words(wu_w[1][:], wu_raw[1][:])
+        gather1(1, HALF, J)
+        for t in (2, 3):
+            gather1(t, HALF, HALF + PAIR)
+        weave1(HALF, HALF + PAIR)
+        gather1(2, HALF + PAIR, J)
+        for jt in (6, 7):
+            gather1(3, P * jt, P * (jt + 1))
+            weave1(P * jt, P * (jt + 1))
+        for jt0 in (0, 2):
+            for hf in range(2):
+                for jt in (jt0, jt0 + 1):
+                    up_sum(hf, jt, jt0 + jt + 2 * hf)
+        product(0, 0, 2)
+        product(0, 1, 2)
+        quant1(HALF, HALF + PAIR)
+        up_sum(0, 4, 0)
+        quant1(HALF + PAIR, J)
         for hf in range(2):
-            for jt in range(4):
-                unit(hf, jt, 2, "woven1_%d" % (3 - hf) if jt == 2 else None)
-                if jt == 1 and hf == 0:
-                    for c in (2, 3):
-                        quant_x(1, woven1[c][:], c)
-                if jt == 2:
-                    quant_h(hf, 0, 2)
-            quant_h(hf, 2, 2)
-        wd_w = keep.tile([P, PASSES, PACK, P], I32, name="wd_w", tag="gate_0_0", align_bytes=64)
+            gate_half(hf)
+        product(1, 0, 2, 0)
+        product(1, 1, 2)
+        dsc = late_tile([P, N], U8, "dsc", 7168)
+        wd_w = late_tile([P, PASSES, PACK, P], I32, "wd_w", 7680)
         deal_words(wd_w[:], wd_raw[:])
-        dsc = keep.tile([P, N], U8, name="dsc", tag="gate_1_0", align_bytes=64)
         nc.vector.tensor_copy(
             dsc[:].rearrange("p (t m) -> p t m", t=PACK), dsc_raw[:].rearrange("p (m t) -> p t m", t=PACK)
         )
-        for jt in (4, 5):
-            up_sum(0, jt)
+        quant_h(0, 0, 2, 6144)
+        quant_h(1, 0, 2)
+        product(0, 2, 2, 2048)
+        product(0, 3, 2)
+        product(1, 2, 2, 4096)
+        product(1, 3, 2)
         for hf in range(2):
-            gate_whole(hf, 1)
+            quant_h(hf, 2, 2)
+        up_sum(1, 4, 6)
         for hf in range(2):
-            for jt in (4, 5):
-                unit(hf, jt, 2)
+            product(hf, 4, 2)
+        down(0, 2, 4)
+        weave_y(0, 2, False)
+        for hf in range(2):
+            up_sum(hf, 5, (7, 3)[hf])
+            product(hf, 5, 2)
+        hand_out_planes(0, 2)
         for hf in range(2):
             quant_h(hf, 4, 2)
-        down(0, 2, True)
-        down(2, 2, False)
-        unit(0, 6, 1)
-        unit(1, 6, 1)
-        down(4, 2, False)
-        unit(0, 7, 1)
+        down(2, 2, 1)
+        weave_y(2, 2, False)
+        for hf in range(2):
+            up_sum(hf, 6, 6 * hf)
+            product(hf, 6, 1)
         quant_h(0, 6, 1)
-        unit(1, 7, 1)
+        hand_out_planes(2, 2)
         quant_h(1, 6, 1)
+        down(4, 2, 4)
+        up_sum(0, 7, 7)
+        product(0, 7, 1)
+        up_sum(1, 7, 3)
         quant_h(0, 7, 1)
+        product(1, 7, 1)
         quant_h(1, 7, 1)
-        down(6, 1, True)
-        down_tile(7, 2)
+        weave_y(4, 2, True)
+        hand_out_planes(4, 2)
+        down(6, 1, 1)
+        down_last(7, (2, 0))
+        weave_y(6, 1, True)
+        hand_out_planes(6, 1)
         for q in range(4):
             nc.sync.dma_start(
                 out_2[0, 4 * q : 4 * q + 4, :].rearrange("r (c j) -> c r j", j=PAIR).bitcast(I32),

@@ -143,7 +143,9 @@ def tile_list_relu_biasP_kernel(
             )
 
         picked0 = keep.tile([P, PACK, J], F32, name="picked0", tag="picked0")
-        picked1 = shared.tile([P, PACK, HALF], F32, name="picked1", offset=0, align_bytes=64)
+        picked1 = keep.tile([P, PACK + 1, HALF], F32, name="picked1")
+        woven_tile3 = shared.tile([P, P, PACK], BF16, name="woven_tile3", offset=0, align_bytes=64)
+        picked_last = shared.tile([P, PACK, HALF], F32, name="picked_last", offset=0, align_bytes=64)
         woven0 = [keep.tile([P, HALF, PACK], BF16, name="woven0_%d" % jh, align_bytes=64) for jh in range(2)]
         woven1 = keep.tile([P, J, PACK], BF16, name="woven1", align_bytes=64)
         xq_half = {}
@@ -163,8 +165,18 @@ def tile_list_relu_biasP_kernel(
                 dst, x_plane[a, t][:].indirect(offsets[:, c0 // 16 : c1 // 16]), wgt_all[:, c0:c1], MULT
             )
 
+        def picked_rows(c0, c1):
+            if c0 < HALF:
+                return picked1[:, 0:PACK, c0:c1]
+            if c0 < HALF + PAIR:
+                return picked1[:, PACK:0:-1, c0 - PAIR : c1 - PAIR]
+            return picked_last[:, :, c0 - HALF - PAIR : c1 - HALF - PAIR]
+
+        def woven_cols(c0, c1):
+            return woven_tile3[:] if c0 == 3 * P else woven1[:, c0:c1, :]
+
         def gather1(t, c0, c1):
-            gather(picked1[:, t, c0 % HALF : c0 % HALF + c1 - c0], 1, t, c0, c1)
+            gather(picked_rows(c0, c1)[:, t, :], 1, t, c0, c1)
 
         def weave(dst, src, on_vector=False):
             dst = dst.rearrange("p (c i) t -> p c t i", i=4)
@@ -175,13 +187,13 @@ def tile_list_relu_biasP_kernel(
                 nc.scalar.activation(dst, src, ACT.Copy)
 
         def weave1(c0, c1):
-            weave(woven1[:, c0:c1, :], picked1[:, :, c0 % HALF : c0 % HALF + c1 - c0])
+            weave(woven_cols(c0, c1), picked_rows(c0, c1))
 
         def quant_x(a, src, c0, c1):
             nc.vector.quantize_mx(out=xq(a, c0, c1), scales=xs[a][:, c0:c1], in_=src.rearrange("p j t -> p (j t)"))
 
         def quant1(c0, c1):
-            quant_x(1, woven1[:, c0:c1, :], c0, c1)
+            quant_x(1, woven_cols(c0, c1), c0, c1)
 
         def gate_pass(out, hf, t, a, c0, c1, start, stop):
             nc.tensor.matmul_mx(
@@ -214,7 +226,7 @@ def tile_list_relu_biasP_kernel(
         def gate_half(hf):
             rows = keep.tile([P, PACK, HALF], F32, name="gate_late_%d" % hf)
             for t in range(PACK):
-                sums = bank("ga", 1 + (PACK * hf + t) % 3)
+                sums = bank("ga", 1 + t)
                 for a in reversed(range(PASSES)):
                     gate_pass(sums[:], hf, t, a, HALF, J, a == PASSES - 1, a == 0)
                 nc.scalar.activation(rows[:, t, :], sums[:], ACT.Relu)
@@ -287,12 +299,12 @@ def tile_list_relu_biasP_kernel(
                 stop=stop,
             )
 
-        def down(jt0, tiles, number):
+        def down(jt0, tiles, numbers):
             width = P * tiles
             per_bank = HALF // width
             y = y_rows(jt0, tiles)
             for t0 in range(0, PACK, per_bank):
-                acc = bank("acc", number + t0 // per_bank)
+                acc = bank("acc", numbers[t0 // per_bank])
                 for e in range(per_bank):
                     for a in range(PASSES):
                         down_pass(acc[:, width * e : width * (e + 1)], a, t0 + e, jt0, tiles, a == 0, a == PASSES - 1)
@@ -305,7 +317,9 @@ def tile_list_relu_biasP_kernel(
 
         def weave_y(jt0, tiles, on_vector):
             y_woven[jt0] = ring.tile([P, P * tiles, PACK], BF16, name="yw", align_bytes=64)
-            weave(y_woven[jt0][:], y_rows(jt0, tiles), on_vector)
+            step = P if on_vector else P * tiles
+            for c0 in range(0, P * tiles, step):
+                weave(y_woven[jt0][:, c0 : c0 + step, :], y_rows(jt0, tiles)[:, :, c0 : c0 + step], on_vector)
 
         def hand_out_planes(jt0, tiles):
             c0, width = P * jt0, P * tiles
@@ -350,6 +364,7 @@ def tile_list_relu_biasP_kernel(
         for jh in range(2):
             weave(woven0[jh][:], picked0[:, :, HALF * jh : HALF * (jh + 1)])
         gather1(0, 0, HALF)
+        gather1(0, HALF, HALF + PAIR)
         quant_x(0, woven0[0][:], 0, HALF)
         gather1(1, 0, HALF)
         xq_tile(0, 1, "xq_0_1")
@@ -371,15 +386,19 @@ def tile_list_relu_biasP_kernel(
         for jt in range(4):
             for hf in range(2):
                 gate_tile(hf, jt, 1)
+        for jt in range(3):
+            for hf in range(2):
                 relu_tile(hf, jt)
 
-        gather1(0, HALF, J)
+        gather1(1, HALF, HALF + PAIR)
         deal_words(wu_w[1][:], wu_raw[1][:])
-        gather1(1, HALF, J)
         for t in (2, 3):
             gather1(t, HALF, HALF + PAIR)
         weave1(HALF, HALF + PAIR)
-        gather1(2, HALF + PAIR, J)
+        for hf in range(2):
+            relu_tile(hf, 3)
+        for t in range(PACK - 1):
+            gather1(t, HALF + PAIR, J)
         for jt in (6, 7):
             gather1(3, P * jt, P * (jt + 1))
             weave1(P * jt, P * (jt + 1))
@@ -387,15 +406,16 @@ def tile_list_relu_biasP_kernel(
             for hf in range(2):
                 for jt in (jt0, jt0 + 1):
                     up_sum(hf, jt, jt0 + jt + 2 * hf)
+        quant1(HALF, HALF + PAIR)
         product(0, 0, 2)
         product(0, 1, 2)
-        quant1(HALF, HALF + PAIR)
         up_sum(0, 4, 0)
         quant1(HALF + PAIR, J)
         for hf in range(2):
             gate_half(hf)
         product(1, 0, 2, 0)
         product(1, 1, 2)
+        product(0, 2, 2, 2048)
         dsc = late_tile([P, N], U8, "dsc", 7168)
         wd_w = late_tile([P, PASSES, PACK, P], I32, "wd_w", 7680)
         deal_words(wd_w[:], wd_raw[:])
@@ -404,43 +424,42 @@ def tile_list_relu_biasP_kernel(
         )
         quant_h(0, 0, 2, 6144)
         quant_h(1, 0, 2)
-        product(0, 2, 2, 2048)
         product(0, 3, 2)
         product(1, 2, 2, 4096)
         product(1, 3, 2)
         for hf in range(2):
             quant_h(hf, 2, 2)
-        up_sum(1, 4, 6)
+        down(0, 2, (5, 6))
+        weave_y(0, 2, False)
+        up_sum(1, 4, 7)
         for hf in range(2):
             product(hf, 4, 2)
-        down(0, 2, 4)
-        weave_y(0, 2, False)
         for hf in range(2):
-            up_sum(hf, 5, (7, 3)[hf])
+            up_sum(hf, 5, 1 + hf)
             product(hf, 5, 2)
         hand_out_planes(0, 2)
         for hf in range(2):
             quant_h(hf, 4, 2)
-        down(2, 2, 1)
+        down(2, 2, (3, 4))
         weave_y(2, 2, False)
         for hf in range(2):
-            up_sum(hf, 6, 6 * hf)
+            up_sum(hf, 6, 5 * hf)
             product(hf, 6, 1)
         quant_h(0, 6, 1)
         hand_out_planes(2, 2)
         quant_h(1, 6, 1)
-        down(4, 2, 4)
-        up_sum(0, 7, 7)
+        up_sum(0, 7, 6)
         product(0, 7, 1)
-        up_sum(1, 7, 3)
+        down(4, 2, (7, 1))
+        up_sum(1, 7, 2)
         quant_h(0, 7, 1)
         product(1, 7, 1)
         quant_h(1, 7, 1)
         weave_y(4, 2, True)
         hand_out_planes(4, 2)
-        down(6, 1, 1)
-        down_last(7, (2, 0))
-        weave_y(6, 1, True)
+        down(6, 1, (3,))
+        weave_y(6, 1, False)
+        down_last(7, (4, 0))
         hand_out_planes(6, 1)
         for q in range(4):
             nc.sync.dma_start(

@@ -111,12 +111,13 @@ def tile_list_relu_biasP_kernel(
             )
 
         load_x(0, 0)
-        for t in range(1, PACK):
+        load_x(0, 1)
+        place_scales(0, R)
+        for t in range(2, PACK):
             load_x(0, t)
         load_x(1, 0)
         load_x(1, 1)
         load_x(1, 2)
-        place_scales(0, R)
         load_x(1, 3)
         nc.sync.dma_start(wg_raw[1][:], wg_words[1].bitcast(I32))
         load_wu(0)
@@ -341,34 +342,33 @@ def tile_list_relu_biasP_kernel(
                             acc[:, P * t : P * (t + 1)], a, t, jt, 1,
                             a == 0 and t == 0, a == PASSES - 1 and t == PACK - 1,
                         )
-            y_woven[jt] = ring.tile([P, P, PACK], BF16, name="yw", align_bytes=64)
             nc.vector.tensor_tensor(
-                y_woven[jt][:].rearrange("p (c i) t -> p c t i", i=4),
+                y_woven[jt - 1][:, P:PAIR, :].rearrange("p (c i) t -> p c t i", i=4),
                 accs[0][:].rearrange("p (t c i) -> p c t i", t=PACK, i=4),
                 bias[:].unsqueeze(1).unsqueeze(3).to_broadcast([P, P // 4, PACK, 4]),
                 ADD,
             )
-            hand_out_planes(jt, 1)
+            hand_out_planes(jt - 1, 2)
             for t in range(PACK):
                 nc.scalar.activation(y[:, t, :], accs[1][:, P * t : P * (t + 1)], ACT.Identity, bias=bias[:, t : t + 1])
             nc.sync.dma_start(out_rows[:, :, P * jt : P * (jt + 1)], y)
 
         deal_narrow(wg_w[0][:].bitcast(U16), wg_raw[0][:].bitcast(U16))
-        gather(picked0[:, 0, 0:HEAD], 0, 0, 0, HEAD)
-        gather(picked0[:, 0, HEAD:HALF], 0, 0, HEAD, HALF)
-        gather(picked0[:, 0, HALF:J], 0, 0, HALF, J)
+        gather(picked0[:, 3, 0:HEAD], 0, 0, 0, HEAD)
+        gather(picked0[:, 3, HEAD:HALF], 0, 0, HEAD, HALF)
+        gather(picked0[:, 3, HALF:J], 0, 0, HALF, J)
         for t in range(1, PACK - 1):
-            gather(picked0[:, t, :], 0, t, 0, J)
-        for jh in range(2):
-            gather(picked0[:, 3, HALF * jh : HALF * (jh + 1)], 0, 3, HALF * jh, HALF * (jh + 1))
-        for jh in range(2):
-            weave(woven0[jh][:], picked0[:, :, HALF * jh : HALF * (jh + 1)])
+            gather(picked0[:, 3 - t, :], 0, t, 0, J)
+        for jh in (1, 0):
+            gather(picked0[:, 0, HALF * jh : HALF * (jh + 1)], 0, 3, HALF * jh, HALF * (jh + 1))
+        weave(woven0[1][:], picked0[:, ::-1, HALF:J])
+        weave(woven0[0][:], picked0[:, ::-1, 0:HALF])
         gather1(0, 0, HALF)
         gather1(0, HALF, HALF + PAIR)
-        quant_x(0, woven0[0][:], 0, HALF)
-        gather1(1, 0, HALF)
         xq_tile(0, 1, "xq_0_1")
         quant_x(0, woven0[1][:], HALF, J)
+        gather1(1, 0, HALF)
+        quant_x(0, woven0[0][:], 0, HALF)
         gather1(2, 0, HALF)
         for jt in range(4):
             for hf in range(2):
@@ -458,9 +458,9 @@ def tile_list_relu_biasP_kernel(
         weave_y(4, 2, True)
         hand_out_planes(4, 2)
         down(6, 1, (3,))
-        weave_y(6, 1, False)
+        y_woven[6] = ring.tile([P, PAIR, PACK], BF16, name="yw", align_bytes=64)
+        weave(y_woven[6][:, 0:P, :], y_rows(6, 1))
         down_last(7, (4, 0))
-        hand_out_planes(6, 1)
         for q in range(4):
             nc.sync.dma_start(
                 out_2[0, 4 * q : 4 * q + 4, :].rearrange("r (c j) -> c r j", j=PAIR).bitcast(I32),

@@ -37,11 +37,13 @@ def tile_list_relu_biasP_kernel(
 
         offsets = keep.tile([P, J // 16], U16, name="offsets")
         wgt_rows = keep.tile([P, P], F32, name="wgt_rows")
-        wg_raw = [keep.tile([P, R // 2], I32, name="wg_raw_%d" % a) for a in range(PASSES)]
+        wg_raw_0 = keep.tile([P, R // 2], I32, name="wg_raw_0")
+        wg_raw_1 = [keep.tile([P, PAIR], I32, name="wg_raw_1_%d" % hf) for hf in range(2)]
         nc.sync.dma_start(
             wgt_rows[0:64, :], wgt.rearrange("(g r) (jt s) -> r g jt s", r=16, s=P)[0]
         )
-        nc.sync.dma_start(wg_raw[0][:], wg_words[0].bitcast(I32))
+        nc.sync.dma_start(wg_raw_0[:], wg_words[0].bitcast(I32))
+        nc.sync.dma_start(wg_raw_1[0][:], wg_words[1].bitcast(I32)[:, 0:PAIR])
         nc.sync.dma_start(offsets[:], offs)
         nc.vector.memset(wgt_rows[64:P, :], 0.0)
         ident = keep.tile([P, P], F32, name="ident")
@@ -119,7 +121,7 @@ def tile_list_relu_biasP_kernel(
         load_x(1, 1)
         load_x(1, 2)
         load_x(1, 3)
-        nc.sync.dma_start(wg_raw[1][:], wg_words[1].bitcast(I32))
+        nc.sync.dma_start(wg_raw_1[1][:], wg_words[1].bitcast(I32)[:, PAIR:HALF])
         load_wu(0)
         load_wu(1)
         place_scales(1, R)
@@ -144,7 +146,7 @@ def tile_list_relu_biasP_kernel(
             )
 
         picked0 = keep.tile([P, PACK, J], F32, name="picked0", tag="picked0")
-        picked1 = keep.tile([P, PACK + 1, HALF], F32, name="picked1")
+        picked1 = shared.tile([P, PACK + 1, HALF], F32, name="picked1", offset=12288, align_bytes=64)
         woven_tile3 = shared.tile([P, P, PACK], BF16, name="woven_tile3", offset=0, align_bytes=64)
         picked_last = shared.tile([P, PACK, HALF], F32, name="picked_last", offset=0, align_bytes=64)
         woven0 = [keep.tile([P, HALF, PACK], BF16, name="woven0_%d" % jh, align_bytes=64) for jh in range(2)]
@@ -322,21 +324,24 @@ def tile_list_relu_biasP_kernel(
             for c0 in range(0, P * tiles, step):
                 weave(y_woven[jt0][:, c0 : c0 + step, :], y_rows(jt0, tiles)[:, :, c0 : c0 + step], on_vector)
 
+        def quant_y(codes, woven, c0, width):
+            nc.vector.quantize_mx(
+                out=codes.bitcast(FP8X4),
+                scales=y_sc[4 * (c0 // PAIR) : P, c0 % PAIR : c0 % PAIR + width],
+                in_=woven.rearrange("p j t -> p (j t)"),
+            )
+
         def hand_out_planes(jt0, tiles):
             c0, width = P * jt0, P * tiles
             yq = ring.tile([P, width], I32, name="yq", align_bytes=64)
-            nc.vector.quantize_mx(
-                out=yq[:].bitcast(FP8X4),
-                scales=y_sc[4 * (c0 // PAIR) : P, c0 % PAIR : c0 % PAIR + width],
-                in_=y_woven[jt0][:].rearrange("p j t -> p (j t)"),
-            )
+            quant_y(yq[:], y_woven[jt0][:], c0, width)
             nc.sync.dma_start(out_words[:, c0 : c0 + width], yq[:])
 
         def down_last(jt, numbers):
             y = y_rows(jt, 1)
             accs = [bank("acc", number) for number in numbers]
             for a in range(PASSES):
-                for acc in accs:
+                for acc in reversed(accs):
                     for t in range(PACK):
                         down_pass(
                             acc[:, P * t : P * (t + 1)], a, t, jt, 1,
@@ -348,12 +353,17 @@ def tile_list_relu_biasP_kernel(
                 bias[:].unsqueeze(1).unsqueeze(3).to_broadcast([P, P // 4, PACK, 4]),
                 ADD,
             )
-            hand_out_planes(jt - 1, 2)
+            codes = ring.tile([P, PAIR], I32, name="yq", align_bytes=64)
+            for e in range(2):
+                cols = slice(P * e, P * (e + 1))
+                quant_y(codes[:, cols], y_woven[jt - 1][:, cols, :], P * (jt - 1 + e), P)
+            nc.sync.dma_start(out_words[:, P * (jt - 1) : P * (jt + 1)], codes[:])
             for t in range(PACK):
                 nc.scalar.activation(y[:, t, :], accs[1][:, P * t : P * (t + 1)], ACT.Identity, bias=bias[:, t : t + 1])
             nc.sync.dma_start(out_rows[:, :, P * jt : P * (jt + 1)], y)
 
-        deal_narrow(wg_w[0][:].bitcast(U16), wg_raw[0][:].bitcast(U16))
+        deal_narrow(wg_w[0][:].bitcast(U16), wg_raw_0[:].bitcast(U16))
+        deal_narrow(wg_w[1][:, 0:1].bitcast(U16), wg_raw_1[0][:].bitcast(U16))
         gather(picked0[:, 3, 0:HEAD], 0, 0, 0, HEAD)
         gather(picked0[:, 3, HEAD:HALF], 0, 0, HEAD, HALF)
         gather(picked0[:, 3, HALF:J], 0, 0, HALF, J)
@@ -377,9 +387,9 @@ def tile_list_relu_biasP_kernel(
         for jt in range(4):
             gather1(3, P * jt, P * (jt + 1))
             weave1(P * jt, P * (jt + 1))
-        for hf in range(2):
-            deal_narrow(wg_w[1][:, hf : hf + 1].bitcast(U16), wg_raw[1][:, PAIR * hf : PAIR * (hf + 1)].bitcast(U16))
-            quant1(P * hf, P * (hf + 1))
+        quant1(0, P)
+        deal_narrow(wg_w[1][:, 1:2].bitcast(U16), wg_raw_1[1][:].bitcast(U16))
+        quant1(P, 2 * P)
         quant1(2 * P, 3 * P)
         deal_words(wu_w[0][:], wu_raw[0][:])
         quant1(3 * P, 4 * P)
@@ -407,7 +417,7 @@ def tile_list_relu_biasP_kernel(
                 for jt in (jt0, jt0 + 1):
                     up_sum(hf, jt, jt0 + jt + 2 * hf)
         quant1(HALF, HALF + PAIR)
-        product(0, 0, 2)
+        product(0, 0, 2, 12288)
         product(0, 1, 2)
         up_sum(0, 4, 0)
         quant1(HALF + PAIR, J)

@@ -11,6 +11,7 @@ BF16 = mybir.dt.bfloat16
 I32 = mybir.dt.int32
 U8 = mybir.dt.uint8
 U16 = mybir.dt.uint16
+U32 = mybir.dt.uint32
 FP8X4 = mybir.dt.float8_e4m3fn_x4
 FP4X4 = mybir.dt.float4_e2m1fn_x4
 MULT = mybir.AluOpType.mult
@@ -150,7 +151,8 @@ def tile_list_relu_biasP_kernel(
         woven_tile3 = shared.tile([P, P, PACK], BF16, name="woven_tile3", offset=0, align_bytes=64)
         picked_last = shared.tile([P, PACK, HALF], F32, name="picked_last", offset=0, align_bytes=64)
         woven0 = [keep.tile([P, HALF, PACK], BF16, name="woven0_%d" % jh, align_bytes=64) for jh in range(2)]
-        woven1 = keep.tile([P, J, PACK], BF16, name="woven1", align_bytes=64)
+        woven1 = keep.tile([P, HALF + PAIR, PACK], BF16, name="woven1", align_bytes=64)
+        late = shared.tile([P, 3 * P, PACK], BF16, name="late", offset=12288, align_bytes=64)
         xq_half = {}
 
         def xq_tile(a, jh, tag):
@@ -176,6 +178,8 @@ def tile_list_relu_biasP_kernel(
             return picked_last[:, :, c0 - HALF - PAIR : c1 - HALF - PAIR]
 
         def woven_cols(c0, c1):
+            if c0 >= HALF + PAIR:
+                return late[:, c0 - HALF - PAIR : c1 - HALF - PAIR, :]
             return woven_tile3[:] if c0 == 3 * P else woven1[:, c0:c1, :]
 
         def gather1(t, c0, c1):
@@ -407,18 +411,28 @@ def tile_list_relu_biasP_kernel(
         weave1(HALF, HALF + PAIR)
         for hf in range(2):
             relu_tile(hf, 3)
+        for jt in range(2):
+            up_sum(0, jt, jt)
+            parked = keep.tile([P, HALF], F32, name="parked_%d" % jt)
+            nc.scalar.activation(parked[:], up_sums[0, jt][:], ACT.Copy)
+            up_sums[0, jt] = parked
+        wd_w = late_tile([P, PASSES, PACK, P], I32, "wd_w", 16384)
+        nc.scalar.copy(
+            wd_w[:].bitcast(U32).rearrange("p a t (c i) -> p a c t i", i=4),
+            wd_raw[:].bitcast(U32).rearrange("p a (c i t) -> p a c t i", i=4, t=PACK),
+        )
         for t in range(PACK - 1):
             gather1(t, HALF + PAIR, J)
         for jt in (6, 7):
             gather1(3, P * jt, P * (jt + 1))
-            weave1(P * jt, P * (jt + 1))
         for jt0 in (0, 2):
             for hf in range(2):
                 for jt in (jt0, jt0 + 1):
-                    up_sum(hf, jt, jt0 + jt + 2 * hf)
+                    if (hf, jt0) != (0, 0):
+                        up_sum(hf, jt, jt0 + jt + 2 * hf)
         quant1(HALF, HALF + PAIR)
-        product(0, 0, 2, 12288)
-        product(0, 1, 2)
+        weave(woven_cols(6 * P, J), picked_rows(6 * P, J), True)
+        h_woven[0, 0] = late[:, 0:PAIR, :]
         up_sum(0, 4, 0)
         quant1(HALF + PAIR, J)
         for hf in range(2):
@@ -426,9 +440,9 @@ def tile_list_relu_biasP_kernel(
         product(1, 0, 2, 0)
         product(1, 1, 2)
         product(0, 2, 2, 2048)
+        product(0, 0, 2)
+        product(0, 1, 2)
         dsc = late_tile([P, N], U8, "dsc", 7168)
-        wd_w = late_tile([P, PASSES, PACK, P], I32, "wd_w", 7680)
-        deal_words(wd_w[:], wd_raw[:])
         nc.vector.tensor_copy(
             dsc[:].rearrange("p (t m) -> p t m", t=PACK), dsc_raw[:].rearrange("p (m t) -> p t m", t=PACK)
         )
@@ -439,38 +453,38 @@ def tile_list_relu_biasP_kernel(
         product(1, 3, 2)
         for hf in range(2):
             quant_h(hf, 2, 2)
-        down(0, 2, (5, 6))
+        down(0, 2, (1, 2))
         weave_y(0, 2, False)
-        up_sum(1, 4, 7)
+        up_sum(1, 4, 3)
         for hf in range(2):
             product(hf, 4, 2)
         for hf in range(2):
-            up_sum(hf, 5, 1 + hf)
+            up_sum(hf, 5, 4 + hf)
             product(hf, 5, 2)
         hand_out_planes(0, 2)
         for hf in range(2):
             quant_h(hf, 4, 2)
-        down(2, 2, (3, 4))
+        down(2, 2, (6, 7))
         weave_y(2, 2, False)
         for hf in range(2):
-            up_sum(hf, 6, 5 * hf)
+            up_sum(hf, 6, hf)
             product(hf, 6, 1)
         quant_h(0, 6, 1)
         hand_out_planes(2, 2)
         quant_h(1, 6, 1)
-        up_sum(0, 7, 6)
+        up_sum(0, 7, 2)
         product(0, 7, 1)
-        down(4, 2, (7, 1))
-        up_sum(1, 7, 2)
+        down(4, 2, (3, 4))
+        up_sum(1, 7, 5)
         quant_h(0, 7, 1)
         product(1, 7, 1)
         quant_h(1, 7, 1)
         weave_y(4, 2, True)
         hand_out_planes(4, 2)
-        down(6, 1, (3,))
+        down(6, 1, (6,))
         y_woven[6] = ring.tile([P, PAIR, PACK], BF16, name="yw", align_bytes=64)
         weave(y_woven[6][:, 0:P, :], y_rows(6, 1))
-        down_last(7, (4, 0))
+        down_last(7, (7, 0))
         for q in range(4):
             nc.sync.dma_start(
                 out_2[0, 4 * q : 4 * q + 4, :].rearrange("r (c j) -> c r j", j=PAIR).bitcast(I32),

@@ -134,7 +134,12 @@ def tile_list_relu_biasP_kernel(
         bias = keep.tile([P, PACK], F32, name="bias")
         nc.sync.dma_start(bias[:], b.rearrange("(p t) -> p t", t=PACK))
 
-        wg_w = [keep.tile([P, 2, PACK, 2 * P], U8, name="wg_%d" % a, align_bytes=64) for a in range(PASSES)]
+        wg_w = {
+            (a, hf): keep.tile([P, PACK, 2 * P], U8, name="wg_%d_%d" % (a, hf), align_bytes=64)
+            for a, hf in [(1, 0)]
+        }
+        wg_0 = keep.tile([P, 2, PACK, 2 * P], U8, name="wg_0", align_bytes=64)
+        wg_w.update({(0, hf): wg_0[:, hf] for hf in range(2)})
         wu_w = [keep.tile([P, PASSES, PACK, P], I32, name="wu_%d" % hf, align_bytes=64) for hf in range(2)]
 
         def plane(k, width, a, c0):
@@ -149,6 +154,7 @@ def tile_list_relu_biasP_kernel(
         picked0 = keep.tile([P, PACK, J], F32, name="picked0", tag="picked0")
         picked1 = shared.tile([P, PACK + 1, HALF], F32, name="picked1", offset=12288, align_bytes=64)
         woven_tile3 = shared.tile([P, P, PACK], BF16, name="woven_tile3", offset=0, align_bytes=64)
+        woven_tile0 = shared.tile([P, P, PACK], BF16, name="woven_tile0", offset=8192, align_bytes=64)
         picked_last = shared.tile([P, PACK, HALF], F32, name="picked_last", offset=0, align_bytes=64)
         woven0 = [keep.tile([P, HALF, PACK], BF16, name="woven0_%d" % jh, align_bytes=64) for jh in range(2)]
         woven1 = keep.tile([P, HALF + PAIR, PACK], BF16, name="woven1", align_bytes=64)
@@ -180,6 +186,8 @@ def tile_list_relu_biasP_kernel(
         def woven_cols(c0, c1):
             if c0 >= HALF + PAIR:
                 return late[:, c0 - HALF - PAIR : c1 - HALF - PAIR, :]
+            if c0 == 0:
+                return woven_tile0[:]
             return woven_tile3[:] if c0 == 3 * P else woven1[:, c0:c1, :]
 
         def gather1(t, c0, c1):
@@ -205,7 +213,7 @@ def tile_list_relu_biasP_kernel(
         def gate_pass(out, hf, t, a, c0, c1, start, stop):
             nc.tensor.matmul_mx(
                 out=out,
-                lhsT=wg_w[a][:, hf, t, :].bitcast(FP4X4),
+                lhsT=wg_w[a, hf][:, t, :].bitcast(FP4X4),
                 lhsT_scale=plane(0, R, a, HALF * hf + P * t),
                 rhs=xq(a, c0, c1),
                 rhs_scale=xs[a][:, c0:c1],
@@ -245,21 +253,24 @@ def tile_list_relu_biasP_kernel(
         h_woven = {}
         up_sums = {}
 
+        def up_slice(out, hf, t, cols):
+            for a in reversed(range(PASSES)):
+                nc.tensor.matmul_mx(
+                    out=out,
+                    lhsT=wu_w[hf][:, a, t, :].bitcast(FP8X4),
+                    lhsT_scale=plane(1, R, a, HALF * hf + P * t),
+                    rhs=xq(a, cols.start, cols.stop),
+                    rhs_scale=xs[a][:, cols],
+                    start=(a == PASSES - 1),
+                    stop=(a == 0),
+                )
+
         def up_sum(hf, jt, number):
             cols = slice(P * jt, P * (jt + 1))
             ub = bank("ub", number)
-            up_sums[hf, jt] = ub
+            up_sums[hf, jt] = ub[:].rearrange("p (t j) -> p t j", t=PACK)
             for t in range(PACK):
-                for a in reversed(range(PASSES)):
-                    nc.tensor.matmul_mx(
-                        out=ub[:, P * t : P * (t + 1)],
-                        lhsT=wu_w[hf][:, a, t, :].bitcast(FP8X4),
-                        lhsT_scale=plane(1, R, a, HALF * hf + P * t),
-                        rhs=xq(a, cols.start, cols.stop),
-                        rhs_scale=xs[a][:, cols],
-                        start=(a == PASSES - 1),
-                        stop=(a == 0),
-                    )
+                up_slice(ub[:, P * t : P * (t + 1)], hf, t, cols)
 
         def late_tile(shape, dtype, name, offset):
             if offset is None:
@@ -272,7 +283,7 @@ def tile_list_relu_biasP_kernel(
                 h_woven[hf, first] = late_tile([P, P * tiles, PACK], BF16, "hw_%d_%d" % (hf, jt), offset)[:]
             nc.vector.tensor_tensor(
                 h_woven[hf, first][:, P * (jt - first) : P * (jt - first + 1), :].rearrange("p (c i) t -> p c t i", i=4),
-                up_sums[hf, jt][:].rearrange("p (t c i) -> p c t i", t=PACK, i=4),
+                up_sums[hf, jt].rearrange("p t (c i) -> p c t i", i=4),
                 gate_rows[hf, jt].rearrange("p t (c i) -> p c t i", i=4),
                 MULT,
             )
@@ -366,8 +377,8 @@ def tile_list_relu_biasP_kernel(
                 nc.scalar.activation(y[:, t, :], accs[1][:, P * t : P * (t + 1)], ACT.Identity, bias=bias[:, t : t + 1])
             nc.sync.dma_start(out_rows[:, :, P * jt : P * (jt + 1)], y)
 
-        deal_narrow(wg_w[0][:].bitcast(U16), wg_raw_0[:].bitcast(U16))
-        deal_narrow(wg_w[1][:, 0:1].bitcast(U16), wg_raw_1[0][:].bitcast(U16))
+        deal_narrow(wg_0[:].bitcast(U16), wg_raw_0[:].bitcast(U16))
+        deal_narrow(wg_w[1, 0][:].bitcast(U16).unsqueeze(1), wg_raw_1[0][:].bitcast(U16))
         gather(picked0[:, 3, 0:HEAD], 0, 0, 0, HEAD)
         gather(picked0[:, 3, HEAD:HALF], 0, 0, HEAD, HALF)
         gather(picked0[:, 3, HALF:J], 0, 0, HALF, J)
@@ -376,13 +387,15 @@ def tile_list_relu_biasP_kernel(
         for jh in (1, 0):
             gather(picked0[:, 0, HALF * jh : HALF * (jh + 1)], 0, 3, HALF * jh, HALF * (jh + 1))
         weave(woven0[1][:], picked0[:, ::-1, HALF:J])
-        weave(woven0[0][:], picked0[:, ::-1, 0:HALF])
+        weave(woven0[0][:, 0:P, :], picked0[:, ::-1, 0:P])
+        weave(woven0[0][:, P:HALF, :], picked0[:, ::-1, P:HALF])
         gather1(0, 0, HALF)
         gather1(0, HALF, HALF + PAIR)
         xq_tile(0, 1, "xq_0_1")
         quant_x(0, woven0[1][:], HALF, J)
+        quant_x(0, woven0[0][:, 0:P, :], 0, P)
         gather1(1, 0, HALF)
-        quant_x(0, woven0[0][:], 0, HALF)
+        quant_x(0, woven0[0][:, P:HALF, :], P, HALF)
         gather1(2, 0, HALF)
         for jt in range(4):
             for hf in range(2):
@@ -392,7 +405,8 @@ def tile_list_relu_biasP_kernel(
             gather1(3, P * jt, P * (jt + 1))
             weave1(P * jt, P * (jt + 1))
         quant1(0, P)
-        deal_narrow(wg_w[1][:, 1:2].bitcast(U16), wg_raw_1[1][:].bitcast(U16))
+        wg_w[1, 1] = shared.tile([P, PACK, 2 * P], U8, name="wg_1_1", offset=8192, align_bytes=64)
+        deal_narrow(wg_w[1, 1][:].bitcast(U16).unsqueeze(1), wg_raw_1[1][:].bitcast(U16))
         quant1(P, 2 * P)
         quant1(2 * P, 3 * P)
         deal_words(wu_w[0][:], wu_raw[0][:])
@@ -411,11 +425,14 @@ def tile_list_relu_biasP_kernel(
         weave1(HALF, HALF + PAIR)
         for hf in range(2):
             relu_tile(hf, 3)
+        parked = keep.tile([P, PACK, PAIR], F32, name="parked")
+        for u in range(2):
+            ub = bank("ub", u)
+            for e in range(2):
+                up_slice(ub[:, PAIR * e : PAIR * (e + 1)], 0, 2 * u + e, slice(0, PAIR))
+            nc.scalar.activation(parked[:, 2 * u : 2 * u + 2, :].rearrange("p t j -> p (t j)"), ub[:], ACT.Copy)
         for jt in range(2):
-            up_sum(0, jt, jt)
-            parked = keep.tile([P, HALF], F32, name="parked_%d" % jt)
-            nc.scalar.activation(parked[:], up_sums[0, jt][:], ACT.Copy)
-            up_sums[0, jt] = parked
+            up_sums[0, jt] = parked[:, :, P * jt : P * (jt + 1)]
         wd_w = late_tile([P, PASSES, PACK, P], I32, "wd_w", 16384)
         nc.scalar.copy(
             wd_w[:].bitcast(U32).rearrange("p a t (c i) -> p a c t i", i=4),

@@ -151,14 +151,21 @@ def tile_list_relu_biasP_kernel(
                 dst.rearrange("p a t (c i) -> p a c t i", i=2), src.rearrange("p a (c i t) -> p a c t i", i=2, t=PACK)
             )
 
+        def deal_words_on_scalar(dst, src):
+            nc.scalar.copy(
+                dst.bitcast(U32).rearrange("p a t (c i) -> p a c t i", i=4),
+                src.bitcast(U32).rearrange("p a (c i t) -> p a c t i", i=4, t=PACK),
+            )
+
         picked0 = keep.tile([P, PACK, J], F32, name="picked0", tag="picked0")
-        picked1 = shared.tile([P, PACK + 1, HALF], F32, name="picked1", offset=12288, align_bytes=64)
+        first_low = keep.tile([P, 2, HALF], F32, name="first_low")
+        picked1 = shared.tile([P, (PACK + 1) * PAIR], F32, name="picked1", offset=12288, align_bytes=64)
         woven_tile3 = shared.tile([P, P, PACK], BF16, name="woven_tile3", offset=0, align_bytes=64)
         woven_tile0 = shared.tile([P, P, PACK], BF16, name="woven_tile0", offset=8192, align_bytes=64)
         picked_last = shared.tile([P, PACK, HALF], F32, name="picked_last", offset=0, align_bytes=64)
         woven0 = [keep.tile([P, HALF, PACK], BF16, name="woven0_%d" % jh, align_bytes=64) for jh in range(2)]
         woven1 = keep.tile([P, HALF + PAIR, PACK], BF16, name="woven1", align_bytes=64)
-        late = shared.tile([P, 3 * P, PACK], BF16, name="late", offset=12288, align_bytes=64)
+        late = shared.tile([P, PAIR, PACK], BF16, name="late", offset=12288, align_bytes=64)
         xq_half = {}
 
         def xq_tile(a, jh, tag):
@@ -176,12 +183,14 @@ def tile_list_relu_biasP_kernel(
                 dst, x_plane[a, t][:].indirect(offsets[:, c0 // 16 : c1 // 16]), wgt_all[:, c0:c1], MULT
             )
 
-        def picked_rows(c0, c1):
+        def picked_rows(c0, c1, t0=0, t1=PACK):
+            if c0 < HALF and t0 < 2:
+                return first_low[:, t0:t1, c0:c1]
             if c0 < HALF:
-                return picked1[:, 0:PACK, c0:c1]
+                return picked1[:, 0:J].rearrange("p (t j) -> p t j", t=2)[:, t0 - 2 : t1 - 2, c0:c1]
             if c0 < HALF + PAIR:
-                return picked1[:, PACK:0:-1, c0 - PAIR : c1 - PAIR]
-            return picked_last[:, :, c0 - HALF - PAIR : c1 - HALF - PAIR]
+                return picked1[:].rearrange("p (r j) -> p r j", j=PAIR)[:, PACK:0:-1, c0 - HALF : c1 - HALF][:, t0:t1]
+            return picked_last[:, t0:t1, c0 - HALF - PAIR : c1 - HALF - PAIR]
 
         def woven_cols(c0, c1):
             if c0 >= HALF + PAIR:
@@ -191,7 +200,7 @@ def tile_list_relu_biasP_kernel(
             return woven_tile3[:] if c0 == 3 * P else woven1[:, c0:c1, :]
 
         def gather1(t, c0, c1):
-            gather(picked_rows(c0, c1)[:, t, :], 1, t, c0, c1)
+            gather(picked_rows(c0, c1, t, t + 1)[:, 0, :], 1, t, c0, c1)
 
         def weave(dst, src, on_vector=False):
             dst = dst.rearrange("p (c i) t -> p c t i", i=4)
@@ -201,8 +210,8 @@ def tile_list_relu_biasP_kernel(
             else:
                 nc.scalar.activation(dst, src, ACT.Copy)
 
-        def weave1(c0, c1):
-            weave(woven_cols(c0, c1), picked_rows(c0, c1))
+        def weave1(c0, c1, t0=0, t1=PACK):
+            weave(woven_cols(c0, c1)[:, :, t0:t1], picked_rows(c0, c1, t0, t1))
 
         def quant_x(a, src, c0, c1):
             nc.vector.quantize_mx(out=xq(a, c0, c1), scales=xs[a][:, c0:c1], in_=src.rearrange("p j t -> p (j t)"))
@@ -234,7 +243,7 @@ def tile_list_relu_biasP_kernel(
                 )
 
         def relu_tile(hf, jt):
-            rows = keep.tile([P, PACK, P], F32, name="gate_%d_%d" % (hf, jt))
+            rows = late_tile([P, PACK, P], F32, "gate_%d_%d" % (hf, jt), 9216 if (hf, jt) == (0, 2) else None)
             nc.scalar.activation(rows[:].rearrange("p t j -> p (t j)"), gate_banks[hf, jt][:], ACT.Relu)
             gate_rows[hf, jt] = rows[:]
 
@@ -396,6 +405,8 @@ def tile_list_relu_biasP_kernel(
         quant_x(0, woven0[0][:, 0:P, :], 0, P)
         gather1(1, 0, HALF)
         quant_x(0, woven0[0][:, P:HALF, :], P, HALF)
+        for c0, c1 in [(0, P), (P, 3 * P), (3 * P, HALF)]:
+            weave1(c0, c1, 0, 2)
         gather1(2, 0, HALF)
         for jt in range(4):
             for hf in range(2):
@@ -403,7 +414,7 @@ def tile_list_relu_biasP_kernel(
 
         for jt in range(4):
             gather1(3, P * jt, P * (jt + 1))
-            weave1(P * jt, P * (jt + 1))
+            weave1(P * jt, P * (jt + 1), 2, PACK)
         quant1(0, P)
         wg_w[1, 1] = shared.tile([P, PACK, 2 * P], U8, name="wg_1_1", offset=8192, align_bytes=64)
         deal_narrow(wg_w[1, 1][:].bitcast(U16).unsqueeze(1), wg_raw_1[1][:].bitcast(U16))
@@ -414,12 +425,13 @@ def tile_list_relu_biasP_kernel(
         for jt in range(4):
             for hf in range(2):
                 gate_tile(hf, jt, 1)
+        deal_words_on_scalar(wu_w[1][:, 0:1], wu_raw[1][:, 0:1])
         for jt in range(3):
             for hf in range(2):
                 relu_tile(hf, jt)
 
         gather1(1, HALF, HALF + PAIR)
-        deal_words(wu_w[1][:], wu_raw[1][:])
+        deal_words(wu_w[1][:, 1:2], wu_raw[1][:, 1:2])
         for t in (2, 3):
             gather1(t, HALF, HALF + PAIR)
         weave1(HALF, HALF + PAIR)
@@ -434,14 +446,9 @@ def tile_list_relu_biasP_kernel(
         for jt in range(2):
             up_sums[0, jt] = parked[:, :, P * jt : P * (jt + 1)]
         wd_w = late_tile([P, PASSES, PACK, P], I32, "wd_w", 16384)
-        nc.scalar.copy(
-            wd_w[:].bitcast(U32).rearrange("p a t (c i) -> p a c t i", i=4),
-            wd_raw[:].bitcast(U32).rearrange("p a (c i t) -> p a c t i", i=4, t=PACK),
-        )
-        for t in range(PACK - 1):
+        deal_words_on_scalar(wd_w[:], wd_raw[:])
+        for t in range(PACK):
             gather1(t, HALF + PAIR, J)
-        for jt in (6, 7):
-            gather1(3, P * jt, P * (jt + 1))
         for jt0 in (0, 2):
             for hf in range(2):
                 for jt in (jt0, jt0 + 1):
@@ -449,7 +456,6 @@ def tile_list_relu_biasP_kernel(
                         up_sum(hf, jt, jt0 + jt + 2 * hf)
         quant1(HALF, HALF + PAIR)
         weave(woven_cols(6 * P, J), picked_rows(6 * P, J), True)
-        h_woven[0, 0] = late[:, 0:PAIR, :]
         up_sum(0, 4, 0)
         quant1(HALF + PAIR, J)
         for hf in range(2):
@@ -457,7 +463,7 @@ def tile_list_relu_biasP_kernel(
         product(1, 0, 2, 0)
         product(1, 1, 2)
         product(0, 2, 2, 2048)
-        product(0, 0, 2)
+        product(0, 0, 2, 9216)
         product(0, 1, 2)
         dsc = late_tile([P, N], U8, "dsc", 7168)
         nc.vector.tensor_copy(

from contextlib import ExitStack

import concourse.mybir as mybir
from concourse.masks import make_identity

K, R, N, T, J = 1024, 1024, 512, 2048, 1024
FLOPS = 2 * J * (2 * K * R + R * N)

F32 = mybir.dt.float32
BF16 = mybir.dt.bfloat16
I32 = mybir.dt.int32
U8 = mybir.dt.uint8
U16 = mybir.dt.uint16
U32 = mybir.dt.uint32
FP8X4 = mybir.dt.float8_e4m3fn_x4
FP4X4 = mybir.dt.float4_e2m1fn_x4
MULT = mybir.AluOpType.mult
ADD = mybir.AluOpType.add
ACT = mybir.ActivationFunctionType

P = 128
PACK = 4
PASSES = 2
HALF = 512
PAIR = 256
HEAD = 256


def tile_list_relu_biasP_kernel(
    tc, xT, wgt, wg_words, wg_scales, wu_words, wu_scales, wd_words, wd_scales, b, offs, out_0, out_1, out_2
):
    nc = tc.nc
    with ExitStack() as ctx:
        keep = ctx.enter_context(tc.tile_pool(name="keep", bufs=1))
        shared = ctx.enter_context(tc.tile_pool(name="shared", bufs=1))
        ring = ctx.enter_context(tc.tile_pool(name="ring", bufs=3))
        psum = ctx.enter_context(tc.psum_pool(name="psum", bufs=1))

        offsets = keep.tile([P, J // 16], U16, name="offsets")
        wgt_rows = keep.tile([P, P], F32, name="wgt_rows")
        wg_raw_0 = keep.tile([P, R // 2], I32, name="wg_raw_0")
        wg_raw_1 = [keep.tile([P, PAIR], I32, name="wg_raw_1_%d" % hf) for hf in range(2)]
        nc.sync.dma_start(
            wgt_rows[0:64, :], wgt.rearrange("(g r) (jt s) -> r g jt s", r=16, s=P)[0]
        )
        nc.sync.dma_start(wg_raw_0[:], wg_words[0].bitcast(I32))
        nc.sync.dma_start(wg_raw_1[0][:], wg_words[1].bitcast(I32)[:, 0:PAIR])
        nc.sync.dma_start(offsets[:], offs)
        nc.vector.memset(wgt_rows[64:P, :], 0.0)
        ident = keep.tile([P, P], F32, name="ident")
        make_identity(nc, ident[:])

        x_rows = xT.rearrange("(a p t) n -> a t p n", a=PASSES, t=PACK)
        x_plane = {}
        for a in range(PASSES):
            for t in range(PACK):
                x_plane[a, t] = keep.tile([P, T], F32, name="x_%d_%d" % (a, t))
        wgt_all = keep.tile([P, J], F32, name="wgt_all")
        wu_raw = [keep.tile([P, PASSES, HALF], I32, name="wu_raw_%d" % hf) for hf in range(2)]
        wd_raw = keep.tile([P, PASSES, N], I32, name="wd_raw")
        sc_raw = keep.tile([P, R], U8, name="sc_raw")
        sc_dealt = keep.tile([P, R], U8, name="sc_dealt")
        gsc = keep.tile([P, PASSES * R], U8, name="gsc", align_bytes=64)
        usc = keep.tile([P, PASSES * R], U8, name="usc", align_bytes=64)
        dsc_raw = keep.tile([P, N], U8, name="dsc_raw")
        sc_home = [(gsc, 0), (usc, 4)]
        nc.vector.memset(sc_raw[64:P, :].bitcast(I32), 0)
        nc.vector.memset(gsc[:].bitcast(I32), 0)
        nc.vector.memset(usc[:].bitcast(I32), 0)
        nc.vector.memset(dsc_raw[:].bitcast(I32), 0)
        for k, scales in enumerate([wg_scales, wu_scales]):
            nc.scalar.dma_start(
                sc_raw[32 * k : 32 * (k + 1), :].bitcast(I32), scales.rearrange("a q r -> q a r").bitcast(I32)
            )

        def bank(name, number):
            return psum.tile([P, HALF], F32, name=name, tag="bank_%d" % number)

        by_token = bank("by_token", 0)
        nc.tensor.transpose(by_token[:, 0:P], wgt_rows[:], ident[:])
        per_tile = by_token[:, 0:64].rearrange("p (g jt) -> p jt g", g=8)
        wide = keep.tile([P, 8, 8, 16], F32, name="wide")
        for c in range(4):
            nc.scalar.copy(
                wide[:, 2 * c : 2 * c + 2], per_tile[:, 2 * c : 2 * c + 2, :].unsqueeze(3).to_broadcast([P, 2, 8, 16])
            )
            spread = bank("spread", 1 + c)
            for e in range(2):
                nc.tensor.transpose(
                    spread[:, P * e : P * (e + 1)], wide[:, 2 * c + e].rearrange("p g r -> p (g r)"), ident[:]
                )
            nc.scalar.copy(wgt_all[:, PAIR * c : PAIR * (c + 1)], spread[:, 0:PAIR])

        def deal_narrow(dst, src):
            nc.vector.tensor_copy(dst, src.rearrange("p (g m t) -> p g t m", t=PACK, m=P))

        deal_narrow(sc_dealt[:].rearrange("p (g t m) -> p g t m", t=PACK, m=P), sc_raw[:])

        def place_scales(k, width):
            home, row = sc_home[k]
            for q in range(4):
                nc.sync.dma_start(
                    home[32 * q + row : 32 * q + row + 4, 0 : PASSES * width].bitcast(I32),
                    sc_dealt[32 * k + 8 * q : 32 * k + 8 * q + 8, 0:width].bitcast(I32),
                )

        def load_x(a, t):
            nc.sync.dma_start(x_plane[a, t][:], x_rows[a, t])

        def load_wu(hf):
            nc.sync.dma_start(
                wu_raw[hf][:],
                wu_words[:, :, HALF * hf : HALF * (hf + 1), :].rearrange("a p r i -> p a (r i)").bitcast(I32),
            )

        load_x(0, 0)
        load_x(0, 1)
        place_scales(0, R)
        for t in range(2, PACK):
            load_x(0, t)
        load_x(1, 0)
        load_x(1, 1)
        load_x(1, 2)
        load_x(1, 3)
        nc.sync.dma_start(wg_raw_1[1][:], wg_words[1].bitcast(I32)[:, PAIR:HALF])
        load_wu(0)
        load_wu(1)
        place_scales(1, R)
        nc.sync.dma_start(wd_raw[:], wd_words.rearrange("a p n i -> p a (n i)").bitcast(I32))
        for q in range(4):
            nc.sync.dma_start(
                dsc_raw[32 * q + 8 : 32 * q + 16, :].bitcast(I32), wd_scales[:, 4 * q : 4 * q + 4, :].bitcast(I32)
            )
        bias = keep.tile([P, PACK], F32, name="bias")
        nc.sync.dma_start(bias[:], b.rearrange("(p t) -> p t", t=PACK))

        wg_w = {
            (a, hf): keep.tile([P, PACK, 2 * P], U8, name="wg_%d_%d" % (a, hf), align_bytes=64)
            for a, hf in [(1, 0)]
        }
        wg_0 = keep.tile([P, 2, PACK, 2 * P], U8, name="wg_0", align_bytes=64)
        wg_w.update({(0, hf): wg_0[:, hf] for hf in range(2)})
        wu_w = [keep.tile([P, PASSES, PACK, P], I32, name="wu_%d" % hf, align_bytes=64) for hf in range(2)]

        def plane(k, width, a, c0):
            home, row = sc_home[k]
            return home[row:P, width * a + c0 : width * a + c0 + P]

        def deal_words(dst, src):
            nc.vector.tensor_copy(
                dst.rearrange("p a t (c i) -> p a c t i", i=2), src.rearrange("p a (c i t) -> p a c t i", i=2, t=PACK)
            )

        def deal_words_on_scalar(dst, src):
            nc.scalar.copy(
                dst.bitcast(U32).rearrange("p a t (c i) -> p a c t i", i=4),
                src.bitcast(U32).rearrange("p a (c i t) -> p a c t i", i=4, t=PACK),
            )

        picked0 = keep.tile([P, PACK, J], F32, name="picked0", tag="picked0")
        first_low = keep.tile([P, 2, HALF], F32, name="first_low")
        picked1 = shared.tile([P, (PACK + 1) * PAIR], F32, name="picked1", offset=12288, align_bytes=64)
        woven_tile3 = shared.tile([P, P, PACK], BF16, name="woven_tile3", offset=0, align_bytes=64)
        woven_tile0 = shared.tile([P, P, PACK], BF16, name="woven_tile0", offset=8192, align_bytes=64)
        picked_last = shared.tile([P, PACK, HALF], F32, name="picked_last", offset=0, align_bytes=64)
        woven0 = [keep.tile([P, HALF, PACK], BF16, name="woven0_%d" % jh, align_bytes=64) for jh in range(2)]
        woven1 = keep.tile([P, HALF + PAIR, PACK], BF16, name="woven1", align_bytes=64)
        late = shared.tile([P, PAIR, PACK], BF16, name="late", offset=12288, align_bytes=64)
        xq_half = {}

        def xq_tile(a, jh, tag):
            xq_half[a, jh] = keep.tile([P, HALF], I32, name="xq_%d_%d" % (a, jh), tag=tag, align_bytes=64)

        def xq(a, c0, c1):
            return xq_half[a, c0 // HALF][:, c0 % HALF : c0 % HALF + c1 - c0].bitcast(FP8X4)

        for a, jh in [(0, 0), (1, 0), (1, 1)]:
            xq_tile(a, jh, "xq_%d_%d" % (a, jh))
        xs = [keep.tile([P, J], U8, name="xs_%d" % a, align_bytes=64) for a in range(PASSES)]

        def gather(dst, a, t, c0, c1):
            nc.vector.tensor_tensor(
                dst, x_plane[a, t][:].indirect(offsets[:, c0 // 16 : c1 // 16]), wgt_all[:, c0:c1], MULT
            )

        def picked_rows(c0, c1, t0=0, t1=PACK):
            if c0 < HALF and t0 < 2:
                return first_low[:, t0:t1, c0:c1]
            if c0 < HALF:
                return picked1[:, 0:J].rearrange("p (t j) -> p t j", t=2)[:, t0 - 2 : t1 - 2, c0:c1]
            if c0 < HALF + PAIR:
                return picked1[:].rearrange("p (r j) -> p r j", j=PAIR)[:, PACK:0:-1, c0 - HALF : c1 - HALF][:, t0:t1]
            return picked_last[:, t0:t1, c0 - HALF - PAIR : c1 - HALF - PAIR]

        def woven_cols(c0, c1):
            if c0 >= HALF + PAIR:
                return late[:, c0 - HALF - PAIR : c1 - HALF - PAIR, :]
            if c0 == 0:
                return woven_tile0[:]
            return woven_tile3[:] if c0 == 3 * P else woven1[:, c0:c1, :]

        def gather1(t, c0, c1):
            gather(picked_rows(c0, c1, t, t + 1)[:, 0, :], 1, t, c0, c1)

        def weave(dst, src, on_vector=False):
            dst = dst.rearrange("p (c i) t -> p c t i", i=4)
            src = src.rearrange("p t (c i) -> p c t i", i=4)
            if on_vector:
                nc.vector.tensor_copy(dst, src)
            else:
                nc.scalar.activation(dst, src, ACT.Copy)

        def weave1(c0, c1, t0=0, t1=PACK):
            weave(woven_cols(c0, c1)[:, :, t0:t1], picked_rows(c0, c1, t0, t1))

        def quant_x(a, src, c0, c1):
            nc.vector.quantize_mx(out=xq(a, c0, c1), scales=xs[a][:, c0:c1], in_=src.rearrange("p j t -> p (j t)"))

        def quant1(c0, c1):
            quant_x(1, woven_cols(c0, c1), c0, c1)

        def gate_pass(out, hf, t, a, c0, c1, start, stop):
            nc.tensor.matmul_mx(
                out=out,
                lhsT=wg_w[a, hf][:, t, :].bitcast(FP4X4),
                lhsT_scale=plane(0, R, a, HALF * hf + P * t),
                rhs=xq(a, c0, c1),
                rhs_scale=xs[a][:, c0:c1],
                start=start,
                stop=stop,
            )

        gate_banks = {}
        gate_rows = {}

        def gate_tile(hf, jt, a):
            if a == 0:
                gate_banks[hf, jt] = bank("ga", 2 * jt + hf)
            for t in range(PACK):
                gate_pass(
                    gate_banks[hf, jt][:, P * t : P * (t + 1)], hf, t, a, P * jt, P * (jt + 1),
                    a == 0 and t == 0, a == PASSES - 1 and t == PACK - 1,
                )

        def relu_tile(hf, jt):
            rows = late_tile([P, PACK, P], F32, "gate_%d_%d" % (hf, jt), 9216 if (hf, jt) == (0, 2) else None)
            nc.scalar.activation(rows[:].rearrange("p t j -> p (t j)"), gate_banks[hf, jt][:], ACT.Relu)
            gate_rows[hf, jt] = rows[:]

        def gate_half(hf):
            rows = keep.tile([P, PACK, HALF], F32, name="gate_late_%d" % hf)
            for t in range(PACK):
                sums = bank("ga", 1 + t)
                for a in reversed(range(PASSES)):
                    gate_pass(sums[:], hf, t, a, HALF, J, a == PASSES - 1, a == 0)
                nc.scalar.activation(rows[:, t, :], sums[:], ACT.Relu)
            for jt in range(4, 8):
                gate_rows[hf, jt] = rows[:, :, P * (jt - 4) : P * (jt - 3)]

        hq = {}
        hs = [keep.tile([P, J], U8, name="hs_%d" % a, align_bytes=64) for a in range(PASSES)]
        h_woven = {}
        up_sums = {}

        def up_slice(out, hf, t, cols):
            for a in reversed(range(PASSES)):
                nc.tensor.matmul_mx(
                    out=out,
                    lhsT=wu_w[hf][:, a, t, :].bitcast(FP8X4),
                    lhsT_scale=plane(1, R, a, HALF * hf + P * t),
                    rhs=xq(a, cols.start, cols.stop),
                    rhs_scale=xs[a][:, cols],
                    start=(a == PASSES - 1),
                    stop=(a == 0),
                )

        def up_sum(hf, jt, number):
            cols = slice(P * jt, P * (jt + 1))
            ub = bank("ub", number)
            up_sums[hf, jt] = ub[:].rearrange("p (t j) -> p t j", t=PACK)
            for t in range(PACK):
                up_slice(ub[:, P * t : P * (t + 1)], hf, t, cols)

        def late_tile(shape, dtype, name, offset):
            if offset is None:
                return keep.tile(shape, dtype, name=name, align_bytes=64)
            return shared.tile(shape, dtype, name=name, offset=offset, align_bytes=64)

        def product(hf, jt, tiles, offset=None):
            first = jt - jt % tiles
            if (hf, first) not in h_woven:
                h_woven[hf, first] = late_tile([P, P * tiles, PACK], BF16, "hw_%d_%d" % (hf, jt), offset)[:]
            nc.vector.tensor_tensor(
                h_woven[hf, first][:, P * (jt - first) : P * (jt - first + 1), :].rearrange("p (c i) t -> p c t i", i=4),
                up_sums[hf, jt].rearrange("p t (c i) -> p c t i", i=4),
                gate_rows[hf, jt].rearrange("p t (c i) -> p c t i", i=4),
                MULT,
            )

        def quant_h(hf, first, tiles, offset=None):
            cols = slice(P * first, P * (first + tiles))
            hq[hf, first] = late_tile([P, P * tiles], I32, "hq_%d_%d" % (hf, first), offset)
            nc.vector.quantize_mx(
                out=hq[hf, first][:].bitcast(FP8X4),
                scales=hs[hf][:, cols],
                in_=h_woven[hf, first].rearrange("p j t -> p (j t)"),
            )

        out_rows = out_0.rearrange("(p t) j -> p t j", t=PACK)
        out_words = out_1[0].rearrange("p j i -> p (j i)").bitcast(I32)
        y_sc = keep.tile([P, PAIR], U8, name="y_sc", align_bytes=64)
        y_all = keep.tile([P, PACK * J], F32, name="y_all", tag="picked0")
        y_woven = {}

        def y_rows(jt0, tiles):
            return y_all[:, PACK * P * jt0 : PACK * P * (jt0 + tiles)].rearrange("p (t j) -> p t j", t=PACK)

        def down_pass(out, a, t, jt0, tiles, start, stop):
            nc.tensor.matmul_mx(
                out=out,
                lhsT=wd_w[:, a, t, :].bitcast(FP8X4),
                lhsT_scale=dsc[8 + 4 * a : P, P * t : P * (t + 1)],
                rhs=hq[a, jt0][:].bitcast(FP8X4),
                rhs_scale=hs[a][:, P * jt0 : P * (jt0 + tiles)],
                start=start,
                stop=stop,
            )

        def down(jt0, tiles, numbers):
            width = P * tiles
            per_bank = HALF // width
            y = y_rows(jt0, tiles)
            for t0 in range(0, PACK, per_bank):
                acc = bank("acc", numbers[t0 // per_bank])
                for e in range(per_bank):
                    for a in range(PASSES):
                        down_pass(acc[:, width * e : width * (e + 1)], a, t0 + e, jt0, tiles, a == 0, a == PASSES - 1)
                for e in range(per_bank):
                    t = t0 + e
                    nc.scalar.activation(
                        y[:, t, :], acc[:, width * e : width * (e + 1)], ACT.Identity, bias=bias[:, t : t + 1]
                    )
            nc.sync.dma_start(out_rows[:, :, P * jt0 : P * jt0 + width], y)

        def weave_y(jt0, tiles, on_vector):
            y_woven[jt0] = ring.tile([P, P * tiles, PACK], BF16, name="yw", align_bytes=64)
            step = P if on_vector else P * tiles
            for c0 in range(0, P * tiles, step):
                weave(y_woven[jt0][:, c0 : c0 + step, :], y_rows(jt0, tiles)[:, :, c0 : c0 + step], on_vector)

        def quant_y(codes, woven, c0, width):
            nc.vector.quantize_mx(
                out=codes.bitcast(FP8X4),
                scales=y_sc[4 * (c0 // PAIR) : P, c0 % PAIR : c0 % PAIR + width],
                in_=woven.rearrange("p j t -> p (j t)"),
            )

        def hand_out_planes(jt0, tiles):
            c0, width = P * jt0, P * tiles
            yq = ring.tile([P, width], I32, name="yq", align_bytes=64)
            quant_y(yq[:], y_woven[jt0][:], c0, width)
            nc.sync.dma_start(out_words[:, c0 : c0 + width], yq[:])

        def down_last(jt, numbers):
            y = y_rows(jt, 1)
            accs = [bank("acc", number) for number in numbers]
            for a in range(PASSES):
                for acc in reversed(accs):
                    for t in range(PACK):
                        down_pass(
                            acc[:, P * t : P * (t + 1)], a, t, jt, 1,
                            a == 0 and t == 0, a == PASSES - 1 and t == PACK - 1,
                        )
            nc.vector.tensor_tensor(
                y_woven[jt - 1][:, P:PAIR, :].rearrange("p (c i) t -> p c t i", i=4),
                accs[0][:].rearrange("p (t c i) -> p c t i", t=PACK, i=4),
                bias[:].unsqueeze(1).unsqueeze(3).to_broadcast([P, P // 4, PACK, 4]),
                ADD,
            )
            codes = ring.tile([P, PAIR], I32, name="yq", align_bytes=64)
            for e in range(2):
                cols = slice(P * e, P * (e + 1))
                quant_y(codes[:, cols], y_woven[jt - 1][:, cols, :], P * (jt - 1 + e), P)
            nc.sync.dma_start(out_words[:, P * (jt - 1) : P * (jt + 1)], codes[:])
            for t in range(PACK):
                nc.scalar.activation(y[:, t, :], accs[1][:, P * t : P * (t + 1)], ACT.Identity, bias=bias[:, t : t + 1])
            nc.sync.dma_start(out_rows[:, :, P * jt : P * (jt + 1)], y)

        deal_narrow(wg_0[:].bitcast(U16), wg_raw_0[:].bitcast(U16))
        deal_narrow(wg_w[1, 0][:].bitcast(U16).unsqueeze(1), wg_raw_1[0][:].bitcast(U16))
        gather(picked0[:, 3, 0:HEAD], 0, 0, 0, HEAD)
        gather(picked0[:, 3, HEAD:HALF], 0, 0, HEAD, HALF)
        gather(picked0[:, 3, HALF:J], 0, 0, HALF, J)
        for t in range(1, PACK - 1):
            gather(picked0[:, 3 - t, :], 0, t, 0, J)
        for jh in (1, 0):
            gather(picked0[:, 0, HALF * jh : HALF * (jh + 1)], 0, 3, HALF * jh, HALF * (jh + 1))
        weave(woven0[1][:], picked0[:, ::-1, HALF:J])
        weave(woven0[0][:, 0:P, :], picked0[:, ::-1, 0:P])
        weave(woven0[0][:, P:HALF, :], picked0[:, ::-1, P:HALF])
        gather1(0, 0, HALF)
        gather1(0, HALF, HALF + PAIR)
        xq_tile(0, 1, "xq_0_1")
        quant_x(0, woven0[1][:], HALF, J)
        quant_x(0, woven0[0][:, 0:P, :], 0, P)
        gather1(1, 0, HALF)
        quant_x(0, woven0[0][:, P:HALF, :], P, HALF)
        for c0, c1 in [(0, P), (P, 3 * P), (3 * P, HALF)]:
            weave1(c0, c1, 0, 2)
        gather1(2, 0, HALF)
        for jt in range(4):
            for hf in range(2):
                gate_tile(hf, jt, 0)

        for jt in range(4):
            gather1(3, P * jt, P * (jt + 1))
            weave1(P * jt, P * (jt + 1), 2, PACK)
        quant1(0, P)
        wg_w[1, 1] = shared.tile([P, PACK, 2 * P], U8, name="wg_1_1", offset=8192, align_bytes=64)
        deal_narrow(wg_w[1, 1][:].bitcast(U16).unsqueeze(1), wg_raw_1[1][:].bitcast(U16))
        quant1(P, 2 * P)
        quant1(2 * P, 3 * P)
        deal_words(wu_w[0][:], wu_raw[0][:])
        quant1(3 * P, 4 * P)
        for jt in range(4):
            for hf in range(2):
                gate_tile(hf, jt, 1)
        deal_words_on_scalar(wu_w[1][:, 0:1], wu_raw[1][:, 0:1])
        for jt in range(3):
            for hf in range(2):
                relu_tile(hf, jt)

        gather1(1, HALF, HALF + PAIR)
        deal_words(wu_w[1][:, 1:2], wu_raw[1][:, 1:2])
        for t in (2, 3):
            gather1(t, HALF, HALF + PAIR)
        weave1(HALF, HALF + PAIR)
        for hf in range(2):
            relu_tile(hf, 3)
        parked = keep.tile([P, PACK, PAIR], F32, name="parked")
        for u in range(2):
            ub = bank("ub", u)
            for e in range(2):
                up_slice(ub[:, PAIR * e : PAIR * (e + 1)], 0, 2 * u + e, slice(0, PAIR))
            nc.scalar.activation(parked[:, 2 * u : 2 * u + 2, :].rearrange("p t j -> p (t j)"), ub[:], ACT.Copy)
        for jt in range(2):
            up_sums[0, jt] = parked[:, :, P * jt : P * (jt + 1)]
        wd_w = late_tile([P, PASSES, PACK, P], I32, "wd_w", 16384)
        deal_words_on_scalar(wd_w[:], wd_raw[:])
        for t in range(PACK):
            gather1(t, HALF + PAIR, J)
        for jt0 in (0, 2):
            for hf in range(2):
                for jt in (jt0, jt0 + 1):
                    if (hf, jt0) != (0, 0):
                        up_sum(hf, jt, jt0 + jt + 2 * hf)
        quant1(HALF, HALF + PAIR)
        weave(woven_cols(6 * P, J), picked_rows(6 * P, J), True)
        up_sum(0, 4, 0)
        quant1(HALF + PAIR, J)
        for hf in range(2):
            gate_half(hf)
        product(1, 0, 2, 0)
        product(1, 1, 2)
        product(0, 2, 2, 2048)
        product(0, 0, 2, 9216)
        product(0, 1, 2)
        dsc = late_tile([P, N], U8, "dsc", 7168)
        nc.vector.tensor_copy(
            dsc[:].rearrange("p (t m) -> p t m", t=PACK), dsc_raw[:].rearrange("p (m t) -> p t m", t=PACK)
        )
        quant_h(0, 0, 2, 6144)
        quant_h(1, 0, 2)
        product(0, 3, 2)
        product(1, 2, 2, 4096)
        product(1, 3, 2)
        for hf in range(2):
            quant_h(hf, 2, 2)
        down(0, 2, (1, 2))
        weave_y(0, 2, False)
        up_sum(1, 4, 3)
        for hf in range(2):
            product(hf, 4, 2)
        for hf in range(2):
            up_sum(hf, 5, 4 + hf)
            product(hf, 5, 2)
        hand_out_planes(0, 2)
        for hf in range(2):
            quant_h(hf, 4, 2)
        down(2, 2, (6, 7))
        weave_y(2, 2, False)
        for hf in range(2):
            up_sum(hf, 6, hf)
            product(hf, 6, 1)
        quant_h(0, 6, 1)
        hand_out_planes(2, 2)
        quant_h(1, 6, 1)
        up_sum(0, 7, 2)
        product(0, 7, 1)
        down(4, 2, (3, 4))
        up_sum(1, 7, 5)
        quant_h(0, 7, 1)
        product(1, 7, 1)
        quant_h(1, 7, 1)
        weave_y(4, 2, True)
        hand_out_planes(4, 2)
        down(6, 1, (6,))
        y_woven[6] = ring.tile([P, PAIR, PACK], BF16, name="yw", align_bytes=64)
        weave(y_woven[6][:, 0:P, :], y_rows(6, 1))
        down_last(7, (7, 0))
        for q in range(4):
            nc.sync.dma_start(
                out_2[0, 4 * q : 4 * q + 4, :].rearrange("r (c j) -> c r j", j=PAIR).bitcast(I32),
                y_sc[32 * q : 32 * q + 16, :].bitcast(I32),
            )
